import numpy as np
import ml_dtypes


def mxq(x, axis, fmt="e4m3"):
    dtype, down = {"e4m3": (ml_dtypes.float8_e4m3fn, 7), "e5m2": (ml_dtypes.float8_e5m2, 14)}[fmt]
    v = np.moveaxis(np.asarray(x, np.float32).astype(ml_dtypes.bfloat16).astype(np.float64), axis, -1)
    blocks = v.reshape(v.shape[:-1] + (-1, 32))
    amax = np.abs(blocks).max(-1, keepdims=True)
    byte = np.maximum(np.where(amax > 0, np.frexp(amax)[1] - 1 + 127, 0) - down, 1)
    scale = np.exp2(byte - 127.0)
    codes = (blocks / scale).astype(np.float32).astype(dtype).astype(np.float64)
    return np.moveaxis((codes * scale).reshape(v.shape), -1, axis)


WIDE = False


def mx_kscale(k):
    if not WIDE:
        return np.ones(k)
    levels = np.array([10, -10, 5, -5, 0])
    if k % 512:
        return np.exp2(np.random.permutation(np.resize(levels, k // 32))).repeat(32)
    a = np.empty((k // 512, 16))
    for p in range(k // 512):
        a[p, :8] = np.random.permutation(np.resize(levels, 8))
        for g in range(8):
            far = levels[np.abs(levels - a[p, g]) >= 10]
            a[p, g + 8] = far[np.random.randint(len(far))]
    return np.exp2(a.ravel()).repeat(32)


def f64(x):
    return np.asarray(x).astype(np.float64)


def striped(idx):
    return np.tile(idx.reshape(-1, 16).T, (8, 1)).astype(np.uint16)


def unstriped(offs):
    return offs[:16].T.reshape(-1).astype(np.int64)


E2M1 = np.array([0.0, 0.5, 1.0, 1.5, 2.0, 3.0, 4.0, 6.0, -0.0, -0.5, -1.0, -1.5, -2.0, -3.0, -4.0, -6.0])


def pack_weight(w, fmt):
    k, n = w.shape
    w = f64(np.asarray(w, np.float32).astype(ml_dtypes.bfloat16)).reshape(k // 32, 32, n)
    amax = np.abs(w).max(1)
    if fmt == "e4m3":
        byte = np.frexp(amax)[1] - 1 + 127 - 7
    else:
        mant, ex = np.frexp(amax / 6.0)
        byte = np.where(mant > 0.5, ex, ex - 1) + 127
    byte = np.clip(np.where(amax > 0, byte, 1), 1, 254)
    scaled = (w * np.exp2(127.0 - byte)[:, None, :]).reshape(k, n).astype(np.float32)
    by_word = np.ascontiguousarray(scaled.reshape(k // 512, 128, 4, n).transpose(0, 1, 3, 2))
    if fmt == "e4m3":
        words = by_word.astype(ml_dtypes.float8_e4m3fn).view(np.uint8)
    else:
        c = by_word.astype(ml_dtypes.float4_e2m1fn).view(np.uint8) & 0xF
        words = (c[..., 0::2] | (c[..., 1::2] << 4)).reshape(k // 512, 128, 2 * n)
    return np.ascontiguousarray(words), np.ascontiguousarray(byte.astype(np.uint8).reshape(k // 512, 16, n))


def unpack_weight(words, scales, fmt):
    g, _, n = scales.shape
    words = np.ascontiguousarray(words).reshape(g, 128, n, -1)
    if fmt == "e4m3":
        vals = words.view(ml_dtypes.float8_e4m3fn).astype(np.float64)
    else:
        nib = np.empty((g, 128, n, 4), np.uint8)
        nib[..., 0::2] = words & 0xF
        nib[..., 1::2] = words >> 4
        vals = E2M1[nib]
    vals = vals * np.repeat(np.exp2(scales.astype(np.float64) - 127.0), 8, axis=1)[..., None]
    return vals.transpose(0, 1, 3, 2).reshape(g * 512, n)


def gelu(v):
    return 0.5 * v * (1.0 + np.tanh(np.sqrt(2.0 / np.pi) * (v + 0.044715 * v**3)))


def striped8(idx):
    return np.concatenate([v.reshape(-1, 16).T for v in idx]).astype(np.uint16)


def unstriped8(offs):
    return np.stack([offs[16 * g:16 * g + 16].T.reshape(-1) for g in range(8)]).astype(np.int64)


def heads(xT, wgt, idx8):
    k = np.arange(xT.shape[0])
    return wgt[k // 4 % 128] * xT[k[:, None], idx8[k % 512 // 64]]


KC, KS, H, N, T, S = 1024, 512, 1024, 256, 2048, 1024

def setup_inputs():
    n = np.random.standard_normal
    sc = mx_kscale(KC)[:, None]
    ss = mx_kscale(KS)[:, None]
    u = mx_kscale(H)[:, None]
    tab_words, tab_scales = pack_weight(n((KS, T)) * ss, "e4m3")
    ws_words, ws_scales = pack_weight(n((KS, H)) / np.sqrt(KS) / ss * u.T, "e2m1")
    return {
        "xT": (n((KC, T)) * sc).astype(np.float32),
        "wgt": np.repeat(np.random.uniform(0.5, 2.0, (8, S)), 16, axis=0).astype(np.float32),
        "offs2": striped8(np.stack([np.random.permutation(T)[:S] for _ in range(8)])),
        "tab_words": tab_words, "tab_scales": tab_scales,
        "offs": striped(np.random.permutation(T)[:S]),
        "wc": (n((KC, H)) / np.sqrt(KC) / sc * u.T).astype(np.float32),
        "ws_words": ws_words, "ws_scales": ws_scales,
        "wm": (n((H, N)) / np.sqrt(H) / u).astype(np.float32),
        "bm": (0.5 * n(N)).astype(np.float32),
    }

def reference(xT, wgt, offs2, tab_words, tab_scales, offs, wc, ws_words, ws_scales, wm, bm):
    xg = heads(f64(xT), f64(wgt), unstriped8(offs2))
    v = unpack_weight(tab_words, tab_scales, "e4m3")[:, unstriped(offs)]
    ws = unpack_weight(ws_words, ws_scales, "e2m1")
    a = mxq(f64(wc), 0, "e4m3").T @ mxq(xg, 0, "e4m3")
    b = ws.T @ v
    h = np.sqrt(np.square(a) + np.square(b))
    y = mxq(f64(wm), 0, "e4m3").T @ mxq(h, 0, "e4m3")
    return y + f64(bm)[:, None]

@@ -1,0 +1,536 @@
+from contextlib import ExitStack
+
+import concourse.mybir as mybir
+from concourse.masks import make_identity
+
+KC, KS, H, N, T, S = 1024, 512, 1024, 256, 2048, 1024
+FLOPS = 2 * S * H * (KC + KS + N)
+
+F32 = mybir.dt.float32
+BF16 = mybir.dt.bfloat16
+I32 = mybir.dt.int32
+U32 = mybir.dt.uint32
+U16 = mybir.dt.uint16
+U8 = mybir.dt.uint8
+FP8X4 = mybir.dt.float8_e4m3fn_x4
+FP4X4 = mybir.dt.float4_e2m1fn_x4
+ACT = mybir.ActivationFunctionType
+ALU = mybir.AluOpType
+
+P = 128
+GATHER_CHUNKS = [256,256,256,256]
+TABLE_CHUNKS = [512,512]
+Y_CHUNKS = [256,256,256,128,128]
+FORM = "BABBBABBABBAABAA"
+XG_ENG = "SSSSSSSV"
+WC_ENG = "SSSVVVVV"
+WM_ENG = "VV"
+Y_ENG = "VVVSS"
+LOADS = ["offs","tabs","wsw","tabw","wgt","wss","offs2","x0","x1","x2","x3","x4","wc00","x5","wc10","x6","x7","bm"]
+PERM16 = True
+WARM = True
+SLOT = {"tabw":"s0","pk10":"s0","pk00":"s1","pk11":"s1","pk01":"s2","wc00":"s3","wc01":"s3","wm":"s3","wc10":"s4","wc11":"s4","xg0_0":"u0","xg0_512":"u1","w16_00":"u2","w16_10":"u0","xg1_0":"u3","xg1_128":"u4","xg1_256":"u1","w16_01":"u2","w16_11":"u0","xg1_512":"u3","xg1_768":"u4","w16_m":"u2"}
+A_BUFS, B_BUFS, T_BUFS, Y_BUFS = 4, 2, 1, 2
+
+
+def spans(widths):
+    result = []
+    start = 0
+    for w in widths:
+        result.append((start, w))
+        start += w
+    return result
+
+
+def tile_list_quadrature_magnitude_mel_kernel(
+    tc, xT, wgt, offs2, tab_words, tab_scales, offs, wc, ws_words, ws_scales, wm, bm, out
+):
+    nc = tc.nc
+    with ExitStack() as ctx:
+        held = ctx.enter_context(tc.tile_pool(name="held", bufs=1))
+        ring = ctx.enter_context(tc.tile_pool(name="ring", bufs=2))
+        psum = ctx.enter_context(tc.psum_pool(name="psum", bufs=1))
+
+        def copy_on(eng, dst, src):
+            if eng == "V":
+                nc.vector.tensor_copy(out=dst, in_=src)
+            else:
+                nc.scalar.copy(out=dst, in_=src)
+
+        offs_t = held.tile([P, S // 16], U16, name="offs_t")
+        offs2_t = held.tile([P, S // 16], U16, name="offs2_t")
+        wgt_t = held.tile([P, S], F32, name="wgt_t")
+        tabw = ring.tile([P, T], I32, name="tabw", tag=SLOT["tabw"], bufs=1)
+        tabs = held.tile([P, T // 4], I32, name="tabs")
+        wsw = held.tile([P, H // 2], I32, name="wsw")
+        wss = held.tile([P, H // 4], I32, name="wss")
+        bias = held.tile([P, 2], F32, name="bias")
+        xp = [held.tile([P, T], F32, name="xp%d" % q) for q in range(8)]
+        raw = {}
+        ident = held.tile([P, P], F32, name="ident")
+
+        if WARM:
+            warm_in = held.tile([P, 1], F32, name="warm_in")
+            warm_out = held.tile([P, 1], F32, name="warm_out")
+            nc.vector.memset(warm_in[:], 1.0)
+            nc.scalar.activation(out=warm_out[:], in_=warm_in[:], func=ACT.Sqrt)
+        nc.gpsimd.memset(tabs[:], 0)
+        nc.vector.memset(wss[:], 0)
+        if "B" in FORM:
+            make_identity(nc, ident[:])
+
+        def load(name):
+            if name == "offs":
+                nc.sync.dma_start(offs_t[:], offs)
+            elif name == "offs2":
+                nc.sync.dma_start(offs2_t[:], offs2)
+            elif name == "wgt":
+                nc.sync.dma_start(out=wgt_t[:], in_=wgt)
+            elif name == "wgt0":
+                nc.sync.dma_start(out=wgt_t[:, : S // 2], in_=wgt[:, : S // 2])
+            elif name == "wgt1":
+                nc.sync.dma_start(out=wgt_t[:, S // 2 :], in_=wgt[:, S // 2 :])
+            elif name == "tabw":
+                nc.sync.dma_start(out=tabw[:], in_=tab_words[0].rearrange("p t i -> p (t i)").bitcast(I32))
+            elif name == "tabs":
+                for q in range(4):
+                    nc.sync.dma_start(out=tabs[32 * q : 32 * q + 4, :], in_=tab_scales[0, 4 * q : 4 * q + 4, :].bitcast(I32))
+            elif name == "wsw":
+                nc.sync.dma_start(out=wsw[:], in_=ws_words[0].bitcast(I32))
+            elif name == "wss":
+                for q in range(4):
+                    nc.sync.dma_start(out=wss[32 * q : 32 * q + 4, :], in_=ws_scales[0, 4 * q : 4 * q + 4, :].bitcast(I32))
+            elif name == "bm":
+                with nc.allow_non_contiguous_dma(reason="one bias value for each partition and band tile"):
+                    nc.sync.dma_start(out=bias[:], in_=bm.rearrange("(c p) -> p c", p=P))
+            elif name[0] == "x":
+                q = int(name[1])
+                a, i = divmod(q, 4)
+                nc.sync.dma_start(out=xp[q][:], in_=xT[512 * a : 512 * (a + 1), :].rearrange("(p i) t -> p i t", i=4)[:, i, :])
+            elif name[:2] == "wc":
+                a, hh = int(name[2]), int(name[3])
+                raw[name] = ring.tile([P, 4, 512], F32, name="raw", tag=SLOT[name], bufs=1)
+                nc.sync.dma_start(
+                    out=raw[name][:],
+                    in_=wc[512 * a : 512 * (a + 1), 512 * hh : 512 * (hh + 1)].rearrange("(p i) r -> p i r", i=4),
+                )
+            elif name == "wm":
+                raw[name] = ring.tile([P, 2, 4 * N], F32, name="raw", tag=SLOT[name], bufs=1)
+                nc.sync.dma_start(out=raw[name][:], in_=wm.rearrange("(a p i) n -> p a (i n)", a=2, i=4))
+
+        for name in LOADS:
+            load(name)
+
+        wsw_p = held.tile([P, 2 * H], U8, name="wsw_p", align_bytes=64)
+        wss_p = held.tile([P, H], U8, name="wss_p", align_bytes=64)
+
+        def perm_words():
+            nc.vector.tensor_copy(
+                out=wsw_p[:].bitcast(U16).rearrange("p (h t m) -> p h m t", h=2, t=4),
+                in_=wsw[:].bitcast(U16).rearrange("p (h m t) -> p h m t", h=2, t=4),
+            )
+
+        def perm_scales():
+            nc.vector.tensor_copy(
+                out=wss_p[:].rearrange("p (h t m) -> p h m t", h=2, t=4),
+                in_=wss[:].bitcast(U8).rearrange("p (h m t) -> p h m t", h=2, t=4),
+            )
+
+        v_words = held.tile([P, S], U32, name="v_words", align_bytes=64)
+        v_scales = held.tile([P, S], U8, name="v_scales", align_bytes=64)
+        bsq = [[held.tile([P, 512], F32, name="bsq%d_%d" % (hh, jt)) for jt in range(8)] for hh in range(2)]
+
+        def form(hh, jt):
+            return FORM[2 * jt + hh]
+
+        bbank = {}
+
+        def sine_mm(hh, jt, bk):
+            js = slice(P * jt, P * (jt + 1))
+            bank = psum.tile([P, 512], F32, name="bank_b", tag="bank%d" % bk, bufs=1)
+            bbank[(hh, jt)] = bank
+            if form(hh, jt) == "A":
+                for t in range(4):
+                    c0 = 512 * hh + P * t
+                    nc.tensor.matmul_mx(
+                        out=bank[:, P * t : P * (t + 1)],
+                        lhsT=wsw_p[:, 2 * c0 : 2 * c0 + 2 * P].bitcast(FP4X4),
+                        lhsT_scale=wss_p[:, c0 : c0 + P],
+                        rhs=v_words[:, js].bitcast(FP8X4),
+                        rhs_scale=v_scales[:, js],
+                        start=True,
+                        stop=True,
+                    )
+            else:
+                nc.tensor.matmul_mx(
+                    out=bank[:],
+                    lhsT=v_words[:, js].bitcast(FP8X4),
+                    lhsT_scale=v_scales[:, js],
+                    rhs=wsw_p[:, 1024 * hh : 1024 * (hh + 1)].bitcast(FP4X4),
+                    rhs_scale=wss_p[:, 512 * hh : 512 * (hh + 1)],
+                    start=True,
+                    stop=True,
+                )
+
+        def sine_sq(hh, jt):
+            bank = bbank[(hh, jt)]
+            if form(hh, jt) == "A":
+                nc.scalar.activation(
+                    out=bsq[hh][jt][:].rearrange("p (j t) -> p j t", t=4),
+                    in_=bank[:].rearrange("p (t j) -> p j t", t=4),
+                    func=ACT.Square,
+                )
+            else:
+                nc.scalar.activation(out=bsq[hh][jt][:], in_=bank[:], func=ACT.Square)
+
+        xg_codes = held.tile([P, 2, S], U32, name="xg_codes", align_bytes=64)
+        xg_scales = held.tile([P, 2, S], U8, name="xg_scales", align_bytes=64)
+        wc_codes = held.tile([P, 2, H], U32, name="wc_codes", align_bytes=64)
+        wc_scales = held.tile([P, 2, H], U8, name="wc_scales", align_bytes=64)
+        wm_codes = held.tile([P, 2, N], U32, name="wm_codes", align_bytes=64)
+        wm_scales = held.tile([P, 2, N], U8, name="wm_scales", align_bytes=64)
+        h_codes = held.tile([P, 2, S], U32, name="h_codes", align_bytes=64)
+        h_scales = held.tile([P, 2, S], U8, name="h_scales", align_bytes=64)
+
+        picked = {}
+        xg16 = {}
+        w16 = {}
+
+        def table_words(j0, w):
+            sel = offs_t[:, j0 // 16 : (j0 + w) // 16]
+            nc.vector.tensor_copy(out=v_words[:, j0 : j0 + w], in_=tabw[:].bitcast(U32).indirect(sel))
+
+        def table_scales(j0, w):
+            sel = offs_t[:, j0 // 16 : (j0 + w) // 16]
+            nc.vector.tensor_copy(out=v_scales[:, j0 : j0 + w], in_=tabs[:].bitcast(U8).indirect(sel))
+
+        def gather(q, j0, w):
+            a, i = divmod(q, 4)
+            half = j0 // 512
+            if (a, half) not in picked:
+                picked[(a, half)] = ring.tile([P, 4, 512], F32, name="picked", tag=SLOT["pk%d%d" % (a, half)], bufs=1)
+            sel = offs2_t[:, j0 // 16 : (j0 + w) // 16]
+            dst = picked[(a, half)][:, i, j0 % 512 : j0 % 512 + w]
+            nc.vector.tensor_tensor(dst, xp[q][:].indirect(sel), wgt_t[:, j0 : j0 + w], ALU.mult)
+
+        def group_xg(a, j0, w, eng):
+            xg16[(a, j0)] = ring.tile([P, w, 4], BF16, name="xg16", tag=SLOT["xg%d_%d" % (a, j0)], bufs=1, align_bytes=64)
+            src = picked[(a, j0 // 512)][:, :, j0 % 512 : j0 % 512 + w]
+            copy_on(
+                eng,
+                xg16[(a, j0)][:].rearrange("p (c e) i -> p c i e", e=4),
+                src.rearrange("p i (c e) -> p c i e", e=4),
+            )
+
+        def quant_xg(a, j0, w):
+            nc.vector.quantize_mx(
+                out=xg_codes[:, a, j0 : j0 + w].bitcast(FP8X4),
+                scales=xg_scales[:, a, j0 : j0 + w],
+                in_=xg16[(a, j0)][:].rearrange("p j i -> p (j i)"),
+            )
+
+        def group_wc(a, hh, eng, m0, m1):
+            if (a, hh) not in w16:
+                w16[(a, hh)] = ring.tile([P, 2048], BF16, name="w16", tag=SLOT["w16_%d%d" % (a, hh)], bufs=1, align_bytes=64)
+            src = raw["wc%d%d" % (a, hh)][:].rearrange("p i (m t) -> p m i t", t=4)
+            dst = w16[(a, hh)][:].rearrange("p (t m i) -> p m i t", t=4, i=4)
+            copy_on(eng, dst[:, m0:m1], src[:, m0:m1])
+
+        def quant_wc(a, hh):
+            cols = slice(512 * hh, 512 * (hh + 1))
+            nc.vector.quantize_mx(out=wc_codes[:, a, cols].bitcast(FP8X4), scales=wc_scales[:, a, cols], in_=w16[(a, hh)][:])
+
+        def group_wm(a, eng):
+            if "wm" not in w16:
+                w16["wm"] = ring.tile([P, 2048], BF16, name="w16", tag=SLOT["w16_m"], bufs=1, align_bytes=64)
+            copy_on(
+                eng,
+                w16["wm"][:, 1024 * a : 1024 * (a + 1)].rearrange("p (c e i) -> p c i e", e=4, i=4),
+                raw["wm"][:, a, :].rearrange("p (i c e) -> p c i e", i=4, e=4),
+            )
+
+        def quant_wm():
+            nc.vector.quantize_mx(
+                out=wm_codes[:].rearrange("p a n -> p (a n)").bitcast(FP8X4),
+                scales=wm_scales[:].rearrange("p a n -> p (a n)"),
+                in_=w16["wm"][:],
+            )
+
+        abank = {}
+        asq = {}
+        tbank = {}
+        ybank = {}
+
+        def a_mm(hh, jt, bk, passes):
+            js = slice(P * jt, P * (jt + 1))
+            if (hh, jt) not in abank:
+                abank[(hh, jt)] = psum.tile([P, 512], F32, name="bank_a", tag="bank%d" % bk, bufs=1)
+            bank = abank[(hh, jt)]
+            if form(hh, jt) == "A":
+                for t in range(4):
+                    cols = slice(512 * hh + P * t, 512 * hh + P * (t + 1))
+                    for a in (1, 0):
+                        nc.tensor.matmul_mx(
+                            out=bank[:, P * t : P * (t + 1)],
+                            lhsT=wc_codes[:, a, cols].bitcast(FP8X4),
+                            lhsT_scale=wc_scales[:, a, cols],
+                            rhs=xg_codes[:, a, js].bitcast(FP8X4),
+                            rhs_scale=xg_scales[:, a, js],
+                            start=(a == 1),
+                            stop=(a == 0),
+                        )
+            else:
+                cols = slice(512 * hh, 512 * (hh + 1))
+                first = 1 if passes == 2 else 0
+                for a in ((1, 0) if passes == 2 else (passes,)):
+                    nc.tensor.matmul_mx(
+                        out=bank[:],
+                        lhsT=xg_codes[:, a, js].bitcast(FP8X4),
+                        lhsT_scale=xg_scales[:, a, js],
+                        rhs=wc_codes[:, a, cols].bitcast(FP8X4),
+                        rhs_scale=wc_scales[:, a, cols],
+                        start=(a == first),
+                        stop=(a != first),
+                    )
+
+        def a_sq(hh, jt):
+            bank = abank[(hh, jt)]
+            asq[(hh, jt)] = ring.tile([P, 512], F32, name="asq", tag="asq", bufs=4)
+            if form(hh, jt) == "A":
+                nc.scalar.activation(
+                    out=asq[(hh, jt)][:].rearrange("p (j t) -> p j t", t=4),
+                    in_=bank[:].rearrange("p (t j) -> p j t", t=4),
+                    func=ACT.Square,
+                )
+            else:
+                nc.scalar.activation(out=asq[(hh, jt)][:], in_=bank[:], func=ACT.Square)
+
+        def add_sq(hh, jt, bk):
+            if form(hh, jt) == "A":
+                nc.vector.tensor_tensor(bsq[hh][jt][:], asq[(hh, jt)][:], bsq[hh][jt][:], ALU.add)
+            else:
+                total = psum.tile([P, 512], F32, name="bank_t", tag="bank%d" % bk, bufs=1)
+                tbank[(hh, jt)] = total
+                for t in range(4):
+                    ts = slice(P * t, P * (t + 1))
+                    nc.tensor.matmul(total[:, ts], lhsT=asq[(hh, jt)][:, ts], rhs=ident[:], start=True, stop=False, is_transpose=True)
+                    nc.tensor.matmul(total[:, ts], lhsT=bsq[hh][jt][:, ts], rhs=ident[:], start=False, stop=True, is_transpose=True)
+
+        h16 = [held.tile([P, 4 * S], BF16, name="h16_%d" % hh, align_bytes=64) for hh in range(2)]
+
+        def root(hh, jt):
+            dst = h16[hh][:, 512 * jt : 512 * (jt + 1)]
+            if form(hh, jt) == "A":
+                nc.scalar.activation(out=dst, in_=bsq[hh][jt][:], func=ACT.Sqrt)
+            else:
+                nc.scalar.activation(
+                    out=dst.rearrange("p (j t) -> p j t", t=4),
+                    in_=tbank[(hh, jt)][:].rearrange("p (t j) -> p j t", t=4),
+                    func=ACT.Sqrt,
+                )
+
+        def quant_h(hh, jt, n):
+            js = slice(P * jt, P * (jt + n))
+            nc.vector.quantize_mx(
+                out=h_codes[:, hh, js].bitcast(FP8X4),
+                scales=h_scales[:, hh, js],
+                in_=h16[hh][:, 512 * jt : 512 * (jt + n)],
+            )
+
+        def y_mm(j0, w, bk):
+            bank = psum.tile([P, 2, w], F32, name="bank_y", tag="bank%d" % bk, bufs=1)
+            ybank[j0] = bank
+            for c in range(2):
+                for hh in (1, 0):
+                    nc.tensor.matmul_mx(
+                        out=bank[:, c, :],
+                        lhsT=wm_codes[:, hh, P * c : P * (c + 1)].bitcast(FP8X4),
+                        lhsT_scale=wm_scales[:, hh, P * c : P * (c + 1)],
+                        rhs=h_codes[:, hh, j0 : j0 + w].bitcast(FP8X4),
+                        rhs_scale=h_scales[:, hh, j0 : j0 + w],
+                        start=(hh == 1),
+                        stop=(hh == 0),
+                    )
+
+        def y_out(j0, w, eng):
+            bank = ybank[j0]
+            res = ring.tile([P, 2, w], F32, name="res", tag="res", bufs=3)
+            if eng == "V":
+                nc.vector.tensor_tensor(res[:], bank[:], bias[:].unsqueeze(2).to_broadcast([P, 2, w]), ALU.add)
+            else:
+                for c in range(2):
+                    nc.scalar.activation(out=res[:, c, :], in_=bank[:, c, :], func=ACT.Identity, bias=bias[:, c : c + 1])
+            nc.sync.dma_start(out=out.rearrange("(c p) j -> p c j", p=P)[:, :, j0 : j0 + w], in_=res[:])
+
+        perm_words()
+        table_scales(0, 512)
+        table_words(0, 512)
+        perm_scales()
+        table_words(512, 512)
+        table_scales(512, 512)
+        gather(0, 0, 512)
+        sine_mm(0, 1, 1)
+        gather(0, 512, 512)
+        sine_mm(0, 2, 2)
+        sine_mm(0, 3, 3)
+        gather(1, 512, 512)
+        sine_mm(0, 0, 0)
+        sine_mm(0, 5, 5)
+        sine_sq(0, 1)
+        gather(1, 0, 512)
+        sine_sq(0, 2)
+        gather(2, 0, 512)
+        sine_sq(0, 3)
+        sine_sq(0, 0)
+        sine_mm(0, 4, 4)
+        sine_mm(1, 2, 2)
+        sine_mm(0, 7, 7)
+        sine_sq(0, 5)
+        sine_sq(1, 2)
+        sine_mm(1, 0, 0)
+        sine_mm(1, 1, 1)
+        gather(3, 0, 512)
+        gather(3, 512, 512)
+        sine_mm(1, 3, 3)
+        gather(4, 0, 512)
+        sine_sq(1, 3)
+        sine_mm(0, 6, 6)
+        sine_sq(1, 1)
+        sine_sq(0, 4)
+        sine_mm(1, 6, 2)
+        sine_sq(1, 0)
+        sine_sq(1, 6)
+        sine_mm(1, 5, 1)
+        group_xg(0, 0, 512, "S")
+        gather(2, 512, 512)
+        quant_xg(0, 0, 512)
+        sine_mm(1, 7, 3)
+        sine_mm(1, 4, 0)
+        gather(4, 512, 512)
+        group_wc(0, 0, "S", 0, 128)
+        quant_wc(0, 0)
+        gather(5, 512, 512)
+        group_xg(0, 512, 512, "S")
+        gather(5, 0, 512)
+        sine_sq(1, 7)
+        quant_xg(0, 512, 512)
+        gather(6, 512, 512)
+        sine_sq(1, 5)
+        gather(6, 0, 512)
+        group_wc(1, 0, "S", 0, 128)
+        sine_sq(1, 4)
+        a_mm(0, 3, 3, 0)
+        gather(7, 128, 128)
+        gather(7, 0, 128)
+        quant_wc(1, 0)
+        group_xg(1, 0, 128, "V")
+        sine_sq(0, 6)
+        a_mm(0, 2, 2, 0)
+        load("wc01")
+        a_mm(0, 1, 1, 0)
+        group_xg(1, 128, 128, "S")
+        quant_xg(1, 128, 128)
+        a_mm(0, 0, 0, 0)
+        gather(7, 256, 256)
+        quant_xg(1, 0, 128)
+        a_mm(0, 1, 1, 1)
+        a_mm(0, 0, 0, 1)
+        a_sq(0, 1)
+        gather(7, 512, 256)
+        add_sq(0, 1, 5)
+        a_sq(0, 0)
+        add_sq(0, 0, 4)
+        sine_sq(0, 7)
+        group_xg(1, 256, 256, "V")
+        group_xg(1, 512, 256, "V")
+        quant_xg(1, 256, 256)
+        a_mm(0, 2, 2, 1)
+        quant_xg(1, 512, 256)
+        load("wc11")
+        a_mm(0, 3, 3, 1)
+        a_mm(0, 4, 0, 2)
+        group_wc(1, 1, "V", 0, 128)
+        root(0, 1)
+        root(0, 0)
+        a_sq(0, 2)
+        a_mm(0, 5, 1, 2)
+        group_wc(0, 1, "V", 0, 128)
+        quant_wc(1, 1)
+        a_sq(0, 3)
+        add_sq(0, 2, 4)
+        a_sq(0, 4)
+        a_sq(0, 5)
+        root(0, 2)
+        quant_wc(0, 1)
+        add_sq(0, 3, 5)
+        add_sq(0, 4, 0)
+        root(0, 4)
+        root(0, 3)
+        load("wm")
+        gather(7, 768, 256)
+        group_xg(1, 768, 256, "V")
+        a_mm(1, 0, 2, 2)
+        quant_xg(1, 768, 256)
+        a_mm(1, 2, 0, 2)
+        a_mm(1, 1, 3, 2)
+        a_mm(1, 3, 1, 2)
+        a_sq(1, 0)
+        a_sq(1, 2)
+        add_sq(0, 5, 4)
+        add_sq(1, 0, 0)
+        a_sq(1, 1)
+        group_wm(1, "V")
+        a_mm(0, 6, 2, 2)
+        root(1, 0)
+        add_sq(1, 2, 0)
+        a_sq(1, 3)
+        a_mm(1, 5, 0, 2)
+        add_sq(1, 1, 5)
+        quant_h(0, 0, 4)
+        group_wm(0, "V")
+        root(0, 5)
+        root(1, 2)
+        a_sq(0, 6)
+        root(1, 1)
+        add_sq(0, 6, 0)
+        quant_h(1, 0, 2)
+        a_mm(1, 4, 3, 2)
+        quant_wm()
+        a_sq(1, 4)
+        a_sq(1, 5)
+        a_mm(1, 6, 1, 2)
+        add_sq(1, 3, 4)
+        root(1, 3)
+        add_sq(1, 5, 0)
+        a_mm(0, 7, 2, 2)
+        a_sq(0, 7)
+        quant_h(1, 2, 2)
+        add_sq(1, 4, 5)
+        y_mm(0, 256, 6)
+        root(1, 5)
+        quant_h(0, 4, 2)
+        a_sq(1, 6)
+        a_mm(1, 7, 3, 2)
+        add_sq(0, 7, 0)
+        root(1, 4)
+        y_out(0, 256, "V")
+        y_mm(256, 256, 7)
+        quant_h(1, 4, 2)
+        root(0, 6)
+        y_out(256, 256, "V")
+        a_sq(1, 7)
+        root(0, 7)
+        add_sq(1, 6, 4)
+        root(1, 6)
+        quant_h(0, 6, 1)
+        y_mm(512, 256, 6)
+        add_sq(1, 7, 0)
+        root(1, 7)
+        y_out(512, 256, "V")
+        quant_h(0, 7, 1)
+        quant_h(1, 6, 1)
+        quant_h(1, 7, 1)
+        y_mm(768, 128, 7)
+        y_out(768, 128, "V")
+        y_mm(896, 128, 4)
+        y_out(896, 128, "V")

@@ -21,15 +21,17 @@ P = 128
 GATHER_CHUNKS = [256,256,256,256]
 TABLE_CHUNKS = [512,512]
 Y_CHUNKS = [256,256,256,128,128]
-FORM = "BABBBABBABBAABAA"
+FORM = "BABBBABABBBABABA"
 XG_ENG = "SSSSSSSV"
 WC_ENG = "SSSVVVVV"
 WM_ENG = "VV"
 Y_ENG = "VVVSS"
-LOADS = ["offs","tabs","wsw","tabw","wgt","wss","offs2","x0","x1","x2","x3","x4","wc00","x5","wc10","x6","x7","bm"]
+LOADS = ["offs","tabs","wsw","tabw","wgt","wss","offs2","x0","x1","x2","x3","x4","wc00","x5","x6","x7","wc10a","wc10b","bm"]
 PERM16 = True
 WARM = True
-SLOT = {"tabw":"s0","pk10":"s0","pk00":"s1","pk11":"s1","pk01":"s2","wc00":"s3","wc01":"s3","wm":"s3","wc10":"s4","wc11":"s4","xg0_0":"u0","xg0_512":"u1","w16_00":"u2","w16_10":"u0","xg1_0":"u3","xg1_128":"u4","xg1_256":"u1","w16_01":"u2","w16_11":"u0","xg1_512":"u3","xg1_768":"u4","w16_m":"u2"}
+SLOT = {"tabw":"s0","pk10":"s0","pk00":"s1","pk11":"xp3","pk01":"s2","wc00":"s3","wc01":"xp0","wm":"xp2","wc10":"s4","wc11":"xp1","xg0_0":"u0","xg0_512":"u1","w16_00":"u2","w16_10":"u5","xg1_0":"u3","xg1_128":"u4","xg1_256":"u0","w16_01":"u2","w16_11":"u1","xg1_512":"u3","xg1_768":"u4","w16_m":"u2"}
+LATE = []
+CODE_SLOT = {"xg00":["xp4",0],"wc00":["xp6",0],"xg01":["u5",0]}
 A_BUFS, B_BUFS, T_BUFS, Y_BUFS = 4, 2, 1, 2
 
 
@@ -60,12 +62,12 @@ def tile_list_quadrature_magnitude_mel_kernel(
         offs_t = held.tile([P, S // 16], U16, name="offs_t")
         offs2_t = held.tile([P, S // 16], U16, name="offs2_t")
         wgt_t = held.tile([P, S], F32, name="wgt_t")
-        tabw = ring.tile([P, T], I32, name="tabw", tag=SLOT["tabw"], bufs=1)
+        tabw = ring.tile([P, T], I32, name="tabw", tag=SLOT["tabw"], bufs=1, align_bytes=64)
         tabs = held.tile([P, T // 4], I32, name="tabs")
         wsw = held.tile([P, H // 2], I32, name="wsw")
-        wss = held.tile([P, H // 4], I32, name="wss")
+        wss = ring.tile([P, H // 4], I32, name="wss", tag="wss", bufs=1, align_bytes=64)
         bias = held.tile([P, 2], F32, name="bias")
-        xp = [held.tile([P, T], F32, name="xp%d" % q) for q in range(8)]
+        xp = [ring.tile([P, T], F32, name="xp%d" % q, tag="xp%d" % q, bufs=1, align_bytes=64) for q in range(8)]
         raw = {}
         ident = held.tile([P, P], F32, name="ident")
 
@@ -76,7 +78,7 @@ def tile_list_quadrature_magnitude_mel_kernel(
             nc.scalar.activation(out=warm_out[:], in_=warm_in[:], func=ACT.Sqrt)
         nc.gpsimd.memset(tabs[:], 0)
         nc.vector.memset(wss[:], 0)
-        if "B" in FORM:
+        if "B" in FORM or "C" in FORM:
             make_identity(nc, ident[:])
 
         def load(name):
@@ -107,15 +109,24 @@ def tile_list_quadrature_magnitude_mel_kernel(
                 q = int(name[1])
                 a, i = divmod(q, 4)
                 nc.sync.dma_start(out=xp[q][:], in_=xT[512 * a : 512 * (a + 1), :].rearrange("(p i) t -> p i t", i=4)[:, i, :])
+            elif name[:2] == "wc" and len(name) == 5:
+                a, hh, part = int(name[2]), int(name[3]), "ab".index(name[4])
+                if name[:4] not in raw:
+                    raw[name[:4]] = ring.tile([P, 4, 512], F32, name="raw", tag=SLOT[name[:4]], bufs=1, align_bytes=64)
+                c0 = 512 * hh + 256 * part
+                nc.sync.dma_start(
+                    out=raw[name[:4]][:, :, 256 * part : 256 * (part + 1)],
+                    in_=wc[512 * a : 512 * (a + 1), c0 : c0 + 256].rearrange("(p i) r -> p i r", i=4),
+                )
             elif name[:2] == "wc":
                 a, hh = int(name[2]), int(name[3])
-                raw[name] = ring.tile([P, 4, 512], F32, name="raw", tag=SLOT[name], bufs=1)
+                raw[name] = ring.tile([P, 4, 512], F32, name="raw", tag=SLOT[name], bufs=1, align_bytes=64)
                 nc.sync.dma_start(
                     out=raw[name][:],
                     in_=wc[512 * a : 512 * (a + 1), 512 * hh : 512 * (hh + 1)].rearrange("(p i) r -> p i r", i=4),
                 )
             elif name == "wm":
-                raw[name] = ring.tile([P, 2, 4 * N], F32, name="raw", tag=SLOT[name], bufs=1)
+                raw[name] = ring.tile([P, 2, 4 * N], F32, name="raw", tag=SLOT[name], bufs=1, align_bytes=64)
                 nc.sync.dma_start(out=raw[name][:], in_=wm.rearrange("(a p i) n -> p a (i n)", a=2, i=4))
 
         for name in LOADS:
@@ -136,9 +147,10 @@ def tile_list_quadrature_magnitude_mel_kernel(
                 in_=wss[:].bitcast(U8).rearrange("p (h m t) -> p h m t", h=2, t=4),
             )
 
-        v_words = held.tile([P, S], U32, name="v_words", align_bytes=64)
+        v_half = {}
         v_scales = held.tile([P, S], U8, name="v_scales", align_bytes=64)
-        bsq = [[held.tile([P, 512], F32, name="bsq%d_%d" % (hh, jt)) for jt in range(8)] for hh in range(2)]
+        bsq = {}
+        late = {}
 
         def form(hh, jt):
             return FORM[2 * jt + hh]
@@ -149,14 +161,14 @@ def tile_list_quadrature_magnitude_mel_kernel(
             js = slice(P * jt, P * (jt + 1))
             bank = psum.tile([P, 512], F32, name="bank_b", tag="bank%d" % bk, bufs=1)
             bbank[(hh, jt)] = bank
-            if form(hh, jt) == "A":
+            if form(hh, jt) in "AD":
                 for t in range(4):
                     c0 = 512 * hh + P * t
                     nc.tensor.matmul_mx(
                         out=bank[:, P * t : P * (t + 1)],
                         lhsT=wsw_p[:, 2 * c0 : 2 * c0 + 2 * P].bitcast(FP4X4),
                         lhsT_scale=wss_p[:, c0 : c0 + P],
-                        rhs=v_words[:, js].bitcast(FP8X4),
+                        rhs=v_half[jt // 4][:, P * (jt % 4) : P * (jt % 4 + 1)].bitcast(FP8X4),
                         rhs_scale=v_scales[:, js],
                         start=True,
                         stop=True,
@@ -164,7 +176,7 @@ def tile_list_quadrature_magnitude_mel_kernel(
             else:
                 nc.tensor.matmul_mx(
                     out=bank[:],
-                    lhsT=v_words[:, js].bitcast(FP8X4),
+                    lhsT=v_half[jt // 4][:, P * (jt % 4) : P * (jt % 4 + 1)].bitcast(FP8X4),
                     lhsT_scale=v_scales[:, js],
                     rhs=wsw_p[:, 1024 * hh : 1024 * (hh + 1)].bitcast(FP4X4),
                     rhs_scale=wss_p[:, 512 * hh : 512 * (hh + 1)],
@@ -173,19 +185,42 @@ def tile_list_quadrature_magnitude_mel_kernel(
                 )
 
         def sine_sq(hh, jt):
+            if (hh, jt) in LATE:
+                if "tile" not in late:
+                    late["tile"] = ring.tile([P, 4, 512], F32, name="late", tag=SLOT["late"], bufs=1)
+                bsq[(hh, jt)] = late["tile"][:, LATE.index((hh, jt)), :]
+            else:
+                bsq[(hh, jt)] = held.tile([P, 512], F32, name="bsq%d_%d" % (hh, jt))[:]
             bank = bbank[(hh, jt)]
-            if form(hh, jt) == "A":
+            if form(hh, jt) in "AD":
                 nc.scalar.activation(
-                    out=bsq[hh][jt][:].rearrange("p (j t) -> p j t", t=4),
+                    out=bsq[(hh, jt)].rearrange("p (j t) -> p j t", t=4),
                     in_=bank[:].rearrange("p (t j) -> p j t", t=4),
                     func=ACT.Square,
                 )
             else:
-                nc.scalar.activation(out=bsq[hh][jt][:], in_=bank[:], func=ACT.Square)
+                nc.scalar.activation(out=bsq[(hh, jt)], in_=bank[:], func=ACT.Square)
 
-        xg_codes = held.tile([P, 2, S], U32, name="xg_codes", align_bytes=64)
+        codes = {}
+
+        def code_tile(key):
+            if key not in codes:
+                if key in CODE_SLOT:
+                    slot, place = CODE_SLOT[key]
+                    if slot not in codes:
+                        codes[slot] = ring.tile([P, 2, 512], U32, name="codes_" + slot, tag=slot, bufs=1, align_bytes=64)
+                    codes[key] = codes[slot][:, place, :]
+                else:
+                    codes[key] = held.tile([P, 512], U32, name="codes_" + key, align_bytes=64)[:]
+            return codes[key]
+
+        def xg_code(a, j0, w):
+            return code_tile("xg%d%d" % (a, j0 // 512))[:, j0 % 512 : j0 % 512 + w]
+
+        def wc_code(a, c0, w):
+            return code_tile("wc%d%d" % (a, c0 // 512))[:, c0 % 512 : c0 % 512 + w]
+
         xg_scales = held.tile([P, 2, S], U8, name="xg_scales", align_bytes=64)
-        wc_codes = held.tile([P, 2, H], U32, name="wc_codes", align_bytes=64)
         wc_scales = held.tile([P, 2, H], U8, name="wc_scales", align_bytes=64)
         wm_codes = held.tile([P, 2, N], U32, name="wm_codes", align_bytes=64)
         wm_scales = held.tile([P, 2, N], U8, name="wm_scales", align_bytes=64)
@@ -198,7 +233,11 @@ def tile_list_quadrature_magnitude_mel_kernel(
 
         def table_words(j0, w):
             sel = offs_t[:, j0 // 16 : (j0 + w) // 16]
-            nc.vector.tensor_copy(out=v_words[:, j0 : j0 + w], in_=tabw[:].bitcast(U32).indirect(sel))
+            if j0 == 0:
+                v_half[0] = held.tile([P, 512], U32, name="v_words0", align_bytes=64)
+            else:
+                v_half[1] = ring.tile([P, 512], U32, name="v_words1", tag="wss", bufs=1, align_bytes=64)
+            nc.vector.tensor_copy(out=v_half[j0 // 512][:], in_=tabw[:].bitcast(U32).indirect(sel))
 
         def table_scales(j0, w):
             sel = offs_t[:, j0 // 16 : (j0 + w) // 16]
@@ -208,7 +247,7 @@ def tile_list_quadrature_magnitude_mel_kernel(
             a, i = divmod(q, 4)
             half = j0 // 512
             if (a, half) not in picked:
-                picked[(a, half)] = ring.tile([P, 4, 512], F32, name="picked", tag=SLOT["pk%d%d" % (a, half)], bufs=1)
+                picked[(a, half)] = ring.tile([P, 4, 512], F32, name="picked", tag=SLOT["pk%d%d" % (a, half)], bufs=1, align_bytes=64)
             sel = offs2_t[:, j0 // 16 : (j0 + w) // 16]
             dst = picked[(a, half)][:, i, j0 % 512 : j0 % 512 + w]
             nc.vector.tensor_tensor(dst, xp[q][:].indirect(sel), wgt_t[:, j0 : j0 + w], ALU.mult)
@@ -224,7 +263,7 @@ def tile_list_quadrature_magnitude_mel_kernel(
 
         def quant_xg(a, j0, w):
             nc.vector.quantize_mx(
-                out=xg_codes[:, a, j0 : j0 + w].bitcast(FP8X4),
+                out=xg_code(a, j0, w).bitcast(FP8X4),
                 scales=xg_scales[:, a, j0 : j0 + w],
                 in_=xg16[(a, j0)][:].rearrange("p j i -> p (j i)"),
             )
@@ -238,7 +277,7 @@ def tile_list_quadrature_magnitude_mel_kernel(
 
         def quant_wc(a, hh):
             cols = slice(512 * hh, 512 * (hh + 1))
-            nc.vector.quantize_mx(out=wc_codes[:, a, cols].bitcast(FP8X4), scales=wc_scales[:, a, cols], in_=w16[(a, hh)][:])
+            nc.vector.quantize_mx(out=wc_code(a, cols.start, cols.stop - cols.start).bitcast(FP8X4), scales=wc_scales[:, a, cols], in_=w16[(a, hh)][:])
 
         def group_wm(a, eng):
             if "wm" not in w16:
@@ -266,15 +305,15 @@ def tile_list_quadrature_magnitude_mel_kernel(
             if (hh, jt) not in abank:
                 abank[(hh, jt)] = psum.tile([P, 512], F32, name="bank_a", tag="bank%d" % bk, bufs=1)
             bank = abank[(hh, jt)]
-            if form(hh, jt) == "A":
+            if form(hh, jt) in "AD":
                 for t in range(4):
                     cols = slice(512 * hh + P * t, 512 * hh + P * (t + 1))
                     for a in (1, 0):
                         nc.tensor.matmul_mx(
                             out=bank[:, P * t : P * (t + 1)],
-                            lhsT=wc_codes[:, a, cols].bitcast(FP8X4),
+                            lhsT=wc_code(a, cols.start, cols.stop - cols.start).bitcast(FP8X4),
                             lhsT_scale=wc_scales[:, a, cols],
-                            rhs=xg_codes[:, a, js].bitcast(FP8X4),
+                            rhs=xg_code(a, P * jt, P).bitcast(FP8X4),
                             rhs_scale=xg_scales[:, a, js],
                             start=(a == 1),
                             stop=(a == 0),
@@ -285,43 +324,56 @@ def tile_list_quadrature_magnitude_mel_kernel(
                 for a in ((1, 0) if passes == 2 else (passes,)):
                     nc.tensor.matmul_mx(
                         out=bank[:],
-                        lhsT=xg_codes[:, a, js].bitcast(FP8X4),
+                        lhsT=xg_code(a, P * jt, P).bitcast(FP8X4),
                         lhsT_scale=xg_scales[:, a, js],
-                        rhs=wc_codes[:, a, cols].bitcast(FP8X4),
+                        rhs=wc_code(a, cols.start, cols.stop - cols.start).bitcast(FP8X4),
                         rhs_scale=wc_scales[:, a, cols],
                         start=(a == first),
                         stop=(a != first),
                     )
 
+        acopy = {}
+
+        def a_view(hh, jt, tile_ap):
+            if form(hh, jt) in "AD":
+                return tile_ap.rearrange("p (j t) -> p j t", t=4), abank[(hh, jt)][:].rearrange("p (t j) -> p j t", t=4)
+            return tile_ap, abank[(hh, jt)][:]
+
+        def a_cp(hh, jt):
+            acopy[(hh, jt)] = ring.tile([P, 512], F32, name="acopy", tag="acopy", bufs=2)
+            dst, src = a_view(hh, jt, acopy[(hh, jt)][:])
+            nc.vector.tensor_copy(out=dst, in_=src)
+
         def a_sq(hh, jt):
-            bank = abank[(hh, jt)]
             asq[(hh, jt)] = ring.tile([P, 512], F32, name="asq", tag="asq", bufs=4)
-            if form(hh, jt) == "A":
-                nc.scalar.activation(
-                    out=asq[(hh, jt)][:].rearrange("p (j t) -> p j t", t=4),
-                    in_=bank[:].rearrange("p (t j) -> p j t", t=4),
-                    func=ACT.Square,
-                )
+            if form(hh, jt) in "CD":
+                nc.vector.tensor_tensor(asq[(hh, jt)][:], acopy[(hh, jt)][:], acopy[(hh, jt)][:], ALU.mult)
             else:
-                nc.scalar.activation(out=asq[(hh, jt)][:], in_=bank[:], func=ACT.Square)
+                dst, src = a_view(hh, jt, asq[(hh, jt)][:])
+                nc.scalar.activation(out=dst, in_=src, func=ACT.Square)
+
+        def turn_b(hh, jt, bk):
+            total = psum.tile([P, 512], F32, name="bank_t", tag="bank%d" % bk, bufs=1)
+            tbank[(hh, jt)] = total
+            for t in range(4):
+                ts = slice(P * t, P * (t + 1))
+                nc.tensor.matmul(total[:, ts], lhsT=bsq[(hh, jt)][:, ts], rhs=ident[:], start=(t == 0), stop=False, is_transpose=True)
 
         def add_sq(hh, jt, bk):
-            if form(hh, jt) == "A":
-                nc.vector.tensor_tensor(bsq[hh][jt][:], asq[(hh, jt)][:], bsq[hh][jt][:], ALU.add)
+            if form(hh, jt) in "AD":
+                nc.vector.tensor_tensor(bsq[(hh, jt)], asq[(hh, jt)][:], bsq[(hh, jt)], ALU.add)
             else:
-                total = psum.tile([P, 512], F32, name="bank_t", tag="bank%d" % bk, bufs=1)
-                tbank[(hh, jt)] = total
+                total = tbank[(hh, jt)]
                 for t in range(4):
                     ts = slice(P * t, P * (t + 1))
-                    nc.tensor.matmul(total[:, ts], lhsT=asq[(hh, jt)][:, ts], rhs=ident[:], start=True, stop=False, is_transpose=True)
-                    nc.tensor.matmul(total[:, ts], lhsT=bsq[hh][jt][:, ts], rhs=ident[:], start=False, stop=True, is_transpose=True)
+                    nc.tensor.matmul(total[:, ts], lhsT=asq[(hh, jt)][:, ts], rhs=ident[:], start=False, stop=(t == 3), is_transpose=True)
 
         h16 = [held.tile([P, 4 * S], BF16, name="h16_%d" % hh, align_bytes=64) for hh in range(2)]
 
         def root(hh, jt):
             dst = h16[hh][:, 512 * jt : 512 * (jt + 1)]
-            if form(hh, jt) == "A":
-                nc.scalar.activation(out=dst, in_=bsq[hh][jt][:], func=ACT.Sqrt)
+            if form(hh, jt) in "AD":
+                nc.scalar.activation(out=dst, in_=bsq[(hh, jt)], func=ACT.Sqrt)
             else:
                 nc.scalar.activation(
                     out=dst.rearrange("p (j t) -> p j t", t=4),
@@ -354,7 +406,7 @@ def tile_list_quadrature_magnitude_mel_kernel(
 
         def y_out(j0, w, eng):
             bank = ybank[j0]
-            res = ring.tile([P, 2, w], F32, name="res", tag="res", bufs=3)
+            res = ring.tile([P, 2, w], F32, name="res", tag="res", bufs=5)
             if eng == "V":
                 nc.vector.tensor_tensor(res[:], bank[:], bias[:].unsqueeze(2).to_broadcast([P, 2, w]), ALU.add)
             else:
@@ -362,175 +414,184 @@ def tile_list_quadrature_magnitude_mel_kernel(
                     nc.scalar.activation(out=res[:, c, :], in_=bank[:, c, :], func=ACT.Identity, bias=bias[:, c : c + 1])
             nc.sync.dma_start(out=out.rearrange("(c p) j -> p c j", p=P)[:, :, j0 : j0 + w], in_=res[:])
 
-        perm_words()
         table_scales(0, 512)
+        table_scales(512, 512)
+        perm_words()
         table_words(0, 512)
         perm_scales()
         table_words(512, 512)
-        table_scales(512, 512)
-        gather(0, 0, 512)
-        sine_mm(0, 1, 1)
-        gather(0, 512, 512)
-        sine_mm(0, 2, 2)
-        sine_mm(0, 3, 3)
-        gather(1, 512, 512)
-        sine_mm(0, 0, 0)
-        sine_mm(0, 5, 5)
-        sine_sq(0, 1)
-        gather(1, 0, 512)
+        sine_mm(0, 2, 0)
+        sine_mm(0, 0, 4)
         sine_sq(0, 2)
-        gather(2, 0, 512)
-        sine_sq(0, 3)
+        sine_mm(1, 2, 1)
         sine_sq(0, 0)
-        sine_mm(0, 4, 4)
-        sine_mm(1, 2, 2)
-        sine_mm(0, 7, 7)
-        sine_sq(0, 5)
+        sine_mm(0, 1, 6)
+        sine_mm(0, 3, 2)
         sine_sq(1, 2)
-        sine_mm(1, 0, 0)
-        sine_mm(1, 1, 1)
+        sine_mm(1, 3, 3)
+        sine_mm(1, 0, 5)
+        sine_sq(0, 1)
+        gather(0, 0, 512)
+        sine_mm(1, 1, 7)
+        sine_sq(1, 3)
+        sine_mm(0, 6, 0)
+        sine_mm(0, 4, 4)
+        sine_sq(1, 0)
+        sine_mm(1, 7, 3)
+        gather(0, 512, 512)
+        sine_sq(1, 1)
+        sine_mm(0, 5, 6)
+        sine_mm(1, 4, 5)
+        sine_sq(0, 4)
+        sine_mm(1, 6, 1)
+        gather(1, 0, 512)
+        sine_mm(1, 5, 7)
+        sine_sq(0, 3)
+        turn_b(0, 0, 4)
+        sine_sq(1, 5)
+        sine_mm(0, 7, 2)
+        gather(1, 512, 512)
+        sine_sq(1, 4)
+        turn_b(0, 3, 7)
+        sine_sq(1, 7)
+        turn_b(0, 1, 5)
+        gather(2, 512, 512)
+        sine_sq(0, 5)
+        sine_sq(1, 6)
+        turn_b(0, 2, 6)
+        gather(2, 0, 512)
+        sine_sq(0, 7)
+        sine_sq(0, 6)
         gather(3, 0, 512)
         gather(3, 512, 512)
-        sine_mm(1, 3, 3)
-        gather(4, 0, 512)
-        sine_sq(1, 3)
-        sine_mm(0, 6, 6)
-        sine_sq(1, 1)
-        sine_sq(0, 4)
-        sine_mm(1, 6, 2)
-        sine_sq(1, 0)
-        sine_sq(1, 6)
-        sine_mm(1, 5, 1)
         group_xg(0, 0, 512, "S")
-        gather(2, 512, 512)
-        quant_xg(0, 0, 512)
-        sine_mm(1, 7, 3)
-        sine_mm(1, 4, 0)
-        gather(4, 512, 512)
-        group_wc(0, 0, "S", 0, 128)
-        quant_wc(0, 0)
-        gather(5, 512, 512)
+        load("wm")
+        gather(4, 0, 512)
         group_xg(0, 512, 512, "S")
+        gather(4, 512, 512)
+        load("wc01")
+        quant_xg(0, 0, 512)
+        group_wc(0, 0, "S", 0, 128)
+        load("wc11")
         gather(5, 0, 512)
-        sine_sq(1, 7)
-        quant_xg(0, 512, 512)
+        gather(5, 512, 512)
         gather(6, 512, 512)
-        sine_sq(1, 5)
         gather(6, 0, 512)
-        group_wc(1, 0, "S", 0, 128)
-        sine_sq(1, 4)
+        quant_wc(0, 0)
+        gather(7, 0, 128)
         a_mm(0, 3, 3, 0)
         gather(7, 128, 128)
-        gather(7, 0, 128)
-        quant_wc(1, 0)
-        group_xg(1, 0, 128, "V")
-        sine_sq(0, 6)
-        a_mm(0, 2, 2, 0)
-        load("wc01")
         a_mm(0, 1, 1, 0)
-        group_xg(1, 128, 128, "S")
-        quant_xg(1, 128, 128)
+        group_xg(1, 0, 128, "S")
+        group_wc(1, 0, "V", 0, 64)
         a_mm(0, 0, 0, 0)
+        group_xg(1, 128, 128, "S")
+        a_mm(0, 2, 2, 0)
         gather(7, 256, 256)
+        group_wc(1, 0, "V", 64, 128)
+        group_xg(1, 256, 256, "S")
+        quant_xg(1, 128, 128)
+        quant_wc(1, 0)
         quant_xg(1, 0, 128)
         a_mm(0, 1, 1, 1)
-        a_mm(0, 0, 0, 1)
-        a_sq(0, 1)
-        gather(7, 512, 256)
-        add_sq(0, 1, 5)
-        a_sq(0, 0)
-        add_sq(0, 0, 4)
-        sine_sq(0, 7)
-        group_xg(1, 256, 256, "V")
-        group_xg(1, 512, 256, "V")
         quant_xg(1, 256, 256)
-        a_mm(0, 2, 2, 1)
-        quant_xg(1, 512, 256)
-        load("wc11")
+        a_mm(0, 0, 0, 1)
+        gather(7, 512, 256)
+        a_sq(0, 1)
         a_mm(0, 3, 3, 1)
-        a_mm(0, 4, 0, 2)
-        group_wc(1, 1, "V", 0, 128)
-        root(0, 1)
-        root(0, 0)
+        a_mm(0, 2, 2, 1)
+        a_sq(0, 0)
+        quant_xg(0, 512, 512)
+        add_sq(0, 1, 5)
+        a_sq(0, 3)
+        group_xg(1, 512, 256, "V")
+        add_sq(0, 0, 4)
         a_sq(0, 2)
+        gather(7, 768, 256)
+        add_sq(0, 3, 7)
+        root(0, 1)
+        quant_xg(1, 512, 256)
+        add_sq(0, 2, 6)
+        group_xg(1, 768, 256, "V")
+        root(0, 3)
         a_mm(0, 5, 1, 2)
         group_wc(0, 1, "V", 0, 128)
-        quant_wc(1, 1)
-        a_sq(0, 3)
-        add_sq(0, 2, 4)
-        a_sq(0, 4)
+        root(0, 0)
+        a_mm(0, 4, 0, 2)
         a_sq(0, 5)
-        root(0, 2)
-        quant_wc(0, 1)
-        add_sq(0, 3, 5)
-        add_sq(0, 4, 0)
-        root(0, 4)
-        root(0, 3)
-        load("wm")
-        gather(7, 768, 256)
-        group_xg(1, 768, 256, "V")
-        a_mm(1, 0, 2, 2)
+        turn_b(0, 5, 5)
         quant_xg(1, 768, 256)
-        a_mm(1, 2, 0, 2)
-        a_mm(1, 1, 3, 2)
-        a_mm(1, 3, 1, 2)
-        a_sq(1, 0)
-        a_sq(1, 2)
-        add_sq(0, 5, 4)
-        add_sq(1, 0, 0)
-        a_sq(1, 1)
-        group_wm(1, "V")
+        a_sq(0, 4)
+        turn_b(0, 4, 4)
+        quant_wc(0, 1)
+        turn_b(0, 7, 7)
+        root(0, 2)
+        group_wc(1, 1, "V", 0, 128)
+        a_mm(0, 7, 3, 2)
         a_mm(0, 6, 2, 2)
-        root(1, 0)
-        add_sq(1, 2, 0)
-        a_sq(1, 3)
-        a_mm(1, 5, 0, 2)
-        add_sq(1, 1, 5)
-        quant_h(0, 0, 4)
-        group_wm(0, "V")
-        root(0, 5)
-        root(1, 2)
-        a_sq(0, 6)
-        root(1, 1)
-        add_sq(0, 6, 0)
-        quant_h(1, 0, 2)
-        a_mm(1, 4, 3, 2)
-        quant_wm()
-        a_sq(1, 4)
-        a_sq(1, 5)
-        a_mm(1, 6, 1, 2)
-        add_sq(1, 3, 4)
-        root(1, 3)
-        add_sq(1, 5, 0)
-        a_mm(0, 7, 2, 2)
         a_sq(0, 7)
-        quant_h(1, 2, 2)
-        add_sq(1, 4, 5)
-        y_mm(0, 256, 6)
-        root(1, 5)
-        quant_h(0, 4, 2)
-        a_sq(1, 6)
-        a_mm(1, 7, 3, 2)
-        add_sq(0, 7, 0)
-        root(1, 4)
-        y_out(0, 256, "V")
-        y_mm(256, 256, 7)
-        quant_h(1, 4, 2)
-        root(0, 6)
-        y_out(256, 256, "V")
-        a_sq(1, 7)
+        group_wm(1, "V")
+        add_sq(0, 4, 4)
+        a_sq(0, 6)
+        quant_wc(1, 1)
+        add_sq(0, 5, 5)
+        root(0, 4)
+        group_wm(0, "V")
+        add_sq(0, 7, 7)
+        root(0, 5)
+        turn_b(0, 6, 6)
+        quant_h(0, 0, 4)
         root(0, 7)
-        add_sq(1, 6, 4)
-        root(1, 6)
-        quant_h(0, 6, 1)
-        y_mm(512, 256, 6)
+        a_mm(1, 1, 1, 2)
+        quant_wm()
+        a_mm(1, 0, 0, 2)
+        a_sq(1, 1)
+        add_sq(0, 6, 6)
+        a_sq(1, 0)
+        a_mm(1, 3, 3, 2)
+        root(0, 6)
+        add_sq(1, 0, 0)
+        turn_b(1, 1, 4)
+        a_sq(1, 3)
+        quant_h(0, 4, 4)
+        a_mm(1, 2, 2, 2)
+        root(1, 0)
+        add_sq(1, 3, 0)
+        add_sq(1, 1, 4)
+        a_sq(1, 2)
+        turn_b(1, 4, 5)
+        root(1, 1)
+        add_sq(1, 2, 0)
+        a_mm(1, 4, 0, 2)
+        root(1, 3)
+        quant_h(1, 0, 2)
+        a_mm(1, 5, 1, 2)
+        root(1, 2)
+        a_mm(1, 7, 3, 2)
+        a_sq(1, 4)
+        quant_h(1, 2, 2)
+        y_mm(0, 256, 7)
+        a_sq(1, 5)
+        a_mm(1, 6, 2, 2)
+        a_sq(1, 7)
+        y_out(0, 256, "V")
+        add_sq(1, 4, 5)
+        add_sq(1, 5, 0)
+        a_sq(1, 6)
+        y_mm(256, 256, 7)
         add_sq(1, 7, 0)
+        root(1, 4)
+        add_sq(1, 6, 0)
+        root(1, 5)
+        y_out(256, 256, "V")
         root(1, 7)
-        y_out(512, 256, "V")
-        quant_h(0, 7, 1)
-        quant_h(1, 6, 1)
+        quant_h(1, 4, 2)
+        root(1, 6)
         quant_h(1, 7, 1)
-        y_mm(768, 128, 7)
+        y_mm(512, 256, 7)
+        quant_h(1, 6, 1)
+        y_mm(896, 128, 1)
+        y_out(512, 256, "V")
+        y_mm(768, 128, 0)
+        y_out(896, 128, "S")
         y_out(768, 128, "V")
-        y_mm(896, 128, 4)
-        y_out(896, 128, "V")

@@ -18,30 +18,22 @@ ACT = mybir.ActivationFunctionType
 ALU = mybir.AluOpType
 
 P = 128
-GATHER_CHUNKS = [256,256,256,256]
-TABLE_CHUNKS = [512,512]
-Y_CHUNKS = [256,256,256,128,128]
-FORM = "BABBBABABBBABABA"
-XG_ENG = "SSSSSSSV"
-WC_ENG = "SSSVVVVV"
-WM_ENG = "VV"
-Y_ENG = "VVVSS"
-LOADS = ["offs","tabs","wsw","tabw","wgt","wss","offs2","x0","x1","x2","x3","x4","wc00","x5","x6","x7","wc10a","wc10b","bm"]
-PERM16 = True
-WARM = True
-SLOT = {"tabw":"s0","pk10":"s0","pk00":"s1","pk11":"xp3","pk01":"s2","wc00":"s3","wc01":"xp0","wm":"xp2","wc10":"s4","wc11":"xp1","xg0_0":"u0","xg0_512":"u1","w16_00":"u2","w16_10":"u5","xg1_0":"u3","xg1_128":"u4","xg1_256":"u0","w16_01":"u2","w16_11":"u1","xg1_512":"u3","xg1_768":"u4","w16_m":"u2"}
-LATE = []
-CODE_SLOT = {"xg00":["xp4",0],"wc00":["xp6",0],"xg01":["u5",0]}
-A_BUFS, B_BUFS, T_BUFS, Y_BUFS = 4, 2, 1, 2
+PACK = 4
+PASS = P * PACK
+ROW = 16
+J_HALF = S // 2
+BANKS = 8
+A_BANKS = 4
 
-
-def spans(widths):
-    result = []
-    start = 0
-    for w in widths:
-        result.append((start, w))
-        start += w
-    return result
+UNITS = [(half, jt) for half in range(2) for jt in range(S // P)]
+TURNED = {(0, 0): 4, (0, 1): 5, (0, 2): 6, (0, 3): 7, (1, 6): 6, (1, 7): 7}
+LAST_PIECES = [(0, 128, "vector", "c"), (128, 128, "scalar", "d"), (256, 256, "scalar", "a"), (512, 256, "vector", "c"), (768, 256, "vector", "d")]
+WC_SPLIT = 96
+OUT_PIECES = [(0, 256, 4), (256, 256, 5), (512, 256, 4), (768, 128, 5), (896, 128, 0)]
+SQUARE_LAG, ADD_LAG, ROOT_LAG = 1, 2, 3
+WM_STEP = 9
+LATE_TURN_STEP = 10
+FIRST_STORE_LAG = 3
 
 
 def tile_list_quadrature_magnitude_mel_kernel(
@@ -50,548 +42,365 @@ def tile_list_quadrature_magnitude_mel_kernel(
     nc = tc.nc
     with ExitStack() as ctx:
         held = ctx.enter_context(tc.tile_pool(name="held", bufs=1))
-        ring = ctx.enter_context(tc.tile_pool(name="ring", bufs=2))
+        shared = ctx.enter_context(tc.tile_pool(name="shared", bufs=1))
         psum = ctx.enter_context(tc.psum_pool(name="psum", bufs=1))
 
-        def copy_on(eng, dst, src):
-            if eng == "V":
+        def buffer(tag, shape, dtype):
+            return shared.tile(shape, dtype, name=tag, tag=tag, bufs=1, align_bytes=64)
+
+        def bank(number, shape):
+            return psum.tile(shape, F32, name="bank%d" % number, tag="bank%d" % number, bufs=1)
+
+        def round_copy(engine, dst, src):
+            if engine == "vector":
                 nc.vector.tensor_copy(out=dst, in_=src)
             else:
                 nc.scalar.copy(out=dst, in_=src)
 
-        offs_t = held.tile([P, S // 16], U16, name="offs_t")
-        offs2_t = held.tile([P, S // 16], U16, name="offs2_t")
-        wgt_t = held.tile([P, S], F32, name="wgt_t")
-        tabw = ring.tile([P, T], I32, name="tabw", tag=SLOT["tabw"], bufs=1, align_bytes=64)
-        tabs = held.tile([P, T // 4], I32, name="tabs")
-        wsw = held.tile([P, H // 2], I32, name="wsw")
-        wss = ring.tile([P, H // 4], I32, name="wss", tag="wss", bufs=1, align_bytes=64)
-        bias = held.tile([P, 2], F32, name="bias")
-        xp = [ring.tile([P, T], F32, name="xp%d" % q, tag="xp%d" % q, bufs=1, align_bytes=64) for q in range(8)]
-        raw = {}
-        ident = held.tile([P, P], F32, name="ident")
+        def load_scale_rows(dst, rows):
+            for q in range(4):
+                nc.sync.dma_start(out=dst[32 * q : 32 * q + 4, :], in_=rows[4 * q : 4 * q + 4, :].bitcast(I32))
 
-        if WARM:
-            warm_in = held.tile([P, 1], F32, name="warm_in")
-            warm_out = held.tile([P, 1], F32, name="warm_out")
-            nc.vector.memset(warm_in[:], 1.0)
-            nc.scalar.activation(out=warm_out[:], in_=warm_in[:], func=ACT.Sqrt)
-        nc.gpsimd.memset(tabs[:], 0)
-        nc.vector.memset(wss[:], 0)
-        if "B" in FORM or "C" in FORM:
-            make_identity(nc, ident[:])
+        def load_plane(plane):
+            g, i = divmod(plane, PACK)
+            rows = xT[PASS * g : PASS * (g + 1), :].rearrange("(p i) t -> p i t", i=PACK)
+            x_plane[plane] = buffer("plane%d" % plane, [P, T], F32)
+            nc.sync.dma_start(out=x_plane[plane][:], in_=rows[:, i, :])
 
-        def load(name):
-            if name == "offs":
-                nc.sync.dma_start(offs_t[:], offs)
-            elif name == "offs2":
-                nc.sync.dma_start(offs2_t[:], offs2)
-            elif name == "wgt":
-                nc.sync.dma_start(out=wgt_t[:], in_=wgt)
-            elif name == "wgt0":
-                nc.sync.dma_start(out=wgt_t[:, : S // 2], in_=wgt[:, : S // 2])
-            elif name == "wgt1":
-                nc.sync.dma_start(out=wgt_t[:, S // 2 :], in_=wgt[:, S // 2 :])
-            elif name == "tabw":
-                nc.sync.dma_start(out=tabw[:], in_=tab_words[0].rearrange("p t i -> p (t i)").bitcast(I32))
-            elif name == "tabs":
-                for q in range(4):
-                    nc.sync.dma_start(out=tabs[32 * q : 32 * q + 4, :], in_=tab_scales[0, 4 * q : 4 * q + 4, :].bitcast(I32))
-            elif name == "wsw":
-                nc.sync.dma_start(out=wsw[:], in_=ws_words[0].bitcast(I32))
-            elif name == "wss":
-                for q in range(4):
-                    nc.sync.dma_start(out=wss[32 * q : 32 * q + 4, :], in_=ws_scales[0, 4 * q : 4 * q + 4, :].bitcast(I32))
-            elif name == "bm":
-                with nc.allow_non_contiguous_dma(reason="one bias value for each partition and band tile"):
-                    nc.sync.dma_start(out=bias[:], in_=bm.rearrange("(c p) -> p c", p=P))
-            elif name[0] == "x":
-                q = int(name[1])
-                a, i = divmod(q, 4)
-                nc.sync.dma_start(out=xp[q][:], in_=xT[512 * a : 512 * (a + 1), :].rearrange("(p i) t -> p i t", i=4)[:, i, :])
-            elif name[:2] == "wc" and len(name) == 5:
-                a, hh, part = int(name[2]), int(name[3]), "ab".index(name[4])
-                if name[:4] not in raw:
-                    raw[name[:4]] = ring.tile([P, 4, 512], F32, name="raw", tag=SLOT[name[:4]], bufs=1, align_bytes=64)
-                c0 = 512 * hh + 256 * part
-                nc.sync.dma_start(
-                    out=raw[name[:4]][:, :, 256 * part : 256 * (part + 1)],
-                    in_=wc[512 * a : 512 * (a + 1), c0 : c0 + 256].rearrange("(p i) r -> p i r", i=4),
-                )
-            elif name[:2] == "wc":
-                a, hh = int(name[2]), int(name[3])
-                raw[name] = ring.tile([P, 4, 512], F32, name="raw", tag=SLOT[name], bufs=1, align_bytes=64)
-                nc.sync.dma_start(
-                    out=raw[name][:],
-                    in_=wc[512 * a : 512 * (a + 1), 512 * hh : 512 * (hh + 1)].rearrange("(p i) r -> p i r", i=4),
-                )
-            elif name == "wm":
-                raw[name] = ring.tile([P, 2, 4 * N], F32, name="raw", tag=SLOT[name], bufs=1, align_bytes=64)
-                nc.sync.dma_start(out=raw[name][:], in_=wm.rearrange("(a p i) n -> p a (i n)", a=2, i=4))
+        def load_wc(g, half, tag):
+            block = wc[PASS * g : PASS * (g + 1), PASS * half : PASS * (half + 1)]
+            wc_raw[g, half] = buffer(tag, [P, PACK, PASS], F32)
+            nc.sync.dma_start(out=wc_raw[g, half][:], in_=block.rearrange("(p i) r -> p i r", i=PACK))
 
-        for name in LOADS:
-            load(name)
+        x_plane, wc_raw = {}, {}
+        table_list = held.tile([P, S // ROW], U16, name="table_list")
+        frame_lists = held.tile([P, S // ROW], U16, name="frame_lists")
+        weights = held.tile([P, S], F32, name="weights")
+        table_words = buffer("table", [P, T], I32)
+        table_scales = held.tile([P, T // 4], I32, name="table_scales")
+        ws_words_raw = held.tile([P, H // 2], I32, name="ws_words_raw")
+        ws_scales_raw = buffer("ws_scales", [P, H // 4], I32)
+        bias = held.tile([P, N // P], F32, name="bias")
+        identity = held.tile([P, P], F32, name="identity")
 
-        wsw_p = held.tile([P, 2 * H], U8, name="wsw_p", align_bytes=64)
-        wss_p = held.tile([P, H], U8, name="wss_p", align_bytes=64)
+        warm_in = held.tile([P, 1], F32, name="warm_in")
+        warm_out = held.tile([P, 1], F32, name="warm_out")
+        nc.vector.memset(warm_in[:], 1.0)
+        nc.scalar.activation(out=warm_out[:], in_=warm_in[:], func=ACT.Sqrt)
 
-        def perm_words():
-            nc.vector.tensor_copy(
-                out=wsw_p[:].bitcast(U16).rearrange("p (h t m) -> p h m t", h=2, t=4),
-                in_=wsw[:].bitcast(U16).rearrange("p (h m t) -> p h m t", h=2, t=4),
-            )
+        nc.gpsimd.memset(table_scales[:], 0)
+        nc.vector.memset(ws_scales_raw[:], 0)
+        make_identity(nc, identity[:])
 
-        def perm_scales():
-            nc.vector.tensor_copy(
-                out=wss_p[:].rearrange("p (h t m) -> p h m t", h=2, t=4),
-                in_=wss[:].bitcast(U8).rearrange("p (h m t) -> p h m t", h=2, t=4),
-            )
+        nc.sync.dma_start(table_list[:], offs)
+        load_scale_rows(table_scales, tab_scales[0])
+        nc.sync.dma_start(out=ws_words_raw[:], in_=ws_words[0].bitcast(I32))
+        nc.sync.dma_start(out=table_words[:], in_=tab_words[0].rearrange("p t i -> p (t i)").bitcast(I32))
+        nc.sync.dma_start(out=weights[:], in_=wgt)
+        load_scale_rows(ws_scales_raw, ws_scales[0])
+        nc.sync.dma_start(frame_lists[:], offs2)
+        for plane in range(5):
+            load_plane(plane)
+        load_wc(0, 0, "wc_a")
+        load_plane(5)
+        load_plane(6)
+        load_wc(1, 0, "wc_b")
+        load_plane(7)
+        with nc.allow_non_contiguous_dma(reason="band 128 c + p's bias goes to partition p, column c"):
+            nc.sync.dma_start(out=bias[:], in_=bm.rearrange("(c p) -> p c", p=P))
 
-        v_half = {}
         v_scales = held.tile([P, S], U8, name="v_scales", align_bytes=64)
-        bsq = {}
-        late = {}
+        ws_codes = held.tile([P, 2 * H], U8, name="ws_codes", align_bytes=64)
+        ws_scale = held.tile([P, H], U8, name="ws_scale", align_bytes=64)
+        v_words = [held.tile([P, J_HALF], U32, name="v_words0", align_bytes=64)]
 
-        def form(hh, jt):
-            return FORM[2 * jt + hh]
+        def entries(lists, j0, width):
+            return lists[:, j0 // ROW : (j0 + width) // ROW]
 
-        bbank = {}
+        for j0 in (0, J_HALF):
+            picks = table_scales[:].bitcast(U8).indirect(entries(table_list, j0, J_HALF))
+            nc.vector.tensor_copy(out=v_scales[:, j0 : j0 + J_HALF], in_=picks)
+        nc.vector.tensor_copy(
+            out=ws_codes[:].bitcast(U16).rearrange("p (h t m) -> p h m t", h=2, t=PACK),
+            in_=ws_words_raw[:].bitcast(U16).rearrange("p (h m t) -> p h m t", h=2, t=PACK),
+        )
+        nc.vector.tensor_copy(out=v_words[0][:], in_=table_words[:].bitcast(U32).indirect(entries(table_list, 0, J_HALF)))
+        nc.vector.tensor_copy(
+            out=ws_scale[:].rearrange("p (h t m) -> p h m t", h=2, t=PACK),
+            in_=ws_scales_raw[:].bitcast(U8).rearrange("p (h m t) -> p h m t", h=2, t=PACK),
+        )
+        v_words.append(buffer("ws_scales", [P, J_HALF], U32))
+        nc.vector.tensor_copy(
+            out=v_words[1][:], in_=table_words[:].bitcast(U32).indirect(entries(table_list, J_HALF, J_HALF))
+        )
 
-        def sine_mm(hh, jt, bk):
-            js = slice(P * jt, P * (jt + 1))
-            bank = psum.tile([P, 512], F32, name="bank_b", tag="bank%d" % bk, bufs=1)
-            bbank[(hh, jt)] = bank
-            if form(hh, jt) in "AD":
-                for t in range(4):
-                    c0 = 512 * hh + P * t
+        def product(unit, sums, passes, start, stop):
+            groups = [slice(0, PASS)] if unit in TURNED else [slice(P * t, P * (t + 1)) for t in range(PACK)]
+            for cols in groups:
+                for n, (w_codes, w_scales, per_col, w_dtype, codes, scales) in enumerate(passes):
+                    weight = (w_codes[:, per_col * cols.start : per_col * cols.stop].bitcast(w_dtype), w_scales[:, cols])
+                    picked = (codes.bitcast(FP8X4), scales)
+                    still, moving = (picked, weight) if unit in TURNED else (weight, picked)
                     nc.tensor.matmul_mx(
-                        out=bank[:, P * t : P * (t + 1)],
-                        lhsT=wsw_p[:, 2 * c0 : 2 * c0 + 2 * P].bitcast(FP4X4),
-                        lhsT_scale=wss_p[:, c0 : c0 + P],
-                        rhs=v_half[jt // 4][:, P * (jt % 4) : P * (jt % 4 + 1)].bitcast(FP8X4),
-                        rhs_scale=v_scales[:, js],
-                        start=True,
-                        stop=True,
+                        out=sums[:, cols],
+                        lhsT=still[0],
+                        lhsT_scale=still[1],
+                        rhs=moving[0],
+                        rhs_scale=moving[1],
+                        start=start and n == 0,
+                        stop=stop and n == len(passes) - 1,
                     )
-            else:
-                nc.tensor.matmul_mx(
-                    out=bank[:],
-                    lhsT=v_half[jt // 4][:, P * (jt % 4) : P * (jt % 4 + 1)].bitcast(FP8X4),
-                    lhsT_scale=v_scales[:, js],
-                    rhs=wsw_p[:, 1024 * hh : 1024 * (hh + 1)].bitcast(FP4X4),
-                    rhs_scale=wss_p[:, 512 * hh : 512 * (hh + 1)],
-                    start=True,
-                    stop=True,
-                )
 
-        def sine_sq(hh, jt):
-            if (hh, jt) in LATE:
-                if "tile" not in late:
-                    late["tile"] = ring.tile([P, 4, 512], F32, name="late", tag=SLOT["late"], bufs=1)
-                bsq[(hh, jt)] = late["tile"][:, LATE.index((hh, jt)), :]
+        def square(unit, dst, sums):
+            if unit in TURNED:
+                nc.scalar.activation(out=dst[:], in_=sums[:], func=ACT.Square)
             else:
-                bsq[(hh, jt)] = held.tile([P, 512], F32, name="bsq%d_%d" % (hh, jt))[:]
-            bank = bbank[(hh, jt)]
-            if form(hh, jt) in "AD":
                 nc.scalar.activation(
-                    out=bsq[(hh, jt)].rearrange("p (j t) -> p j t", t=4),
-                    in_=bank[:].rearrange("p (t j) -> p j t", t=4),
+                    out=dst[:].rearrange("p (j t) -> p j t", t=PACK),
+                    in_=sums[:].rearrange("p (t j) -> p j t", t=PACK),
                     func=ACT.Square,
                 )
-            else:
-                nc.scalar.activation(out=bsq[(hh, jt)], in_=bank[:], func=ACT.Square)
 
-        codes = {}
+        def turn(unit, squares, start):
+            for t in range(PACK):
+                cols = slice(P * t, P * (t + 1))
+                nc.tensor.matmul(
+                    turned_sum[unit][:, cols],
+                    lhsT=squares[:, cols],
+                    rhs=identity[:],
+                    start=start and t == 0,
+                    stop=not start and t == PACK - 1,
+                    is_transpose=True,
+                )
 
-        def code_tile(key):
-            if key not in codes:
-                if key in CODE_SLOT:
-                    slot, place = CODE_SLOT[key]
-                    if slot not in codes:
-                        codes[slot] = ring.tile([P, 2, 512], U32, name="codes_" + slot, tag=slot, bufs=1, align_bytes=64)
-                    codes[key] = codes[slot][:, place, :]
-                else:
-                    codes[key] = held.tile([P, 512], U32, name="codes_" + key, align_bytes=64)[:]
-            return codes[key]
+        def turn_b(unit):
+            turned_sum[unit] = bank(TURNED[unit], [P, PASS])
+            turn(unit, b_square[unit], start=True)
 
-        def xg_code(a, j0, w):
-            return code_tile("xg%d%d" % (a, j0 // 512))[:, j0 % 512 : j0 % 512 + w]
+        b_square, turned_sum = {}, {}
+        for n, (jt, half) in enumerate((jt, half) for jt in range(S // P) for half in range(2)):
+            unit = (half, jt)
+            sums = bank(n % BANKS, [P, PASS])
+            j_in_half = P * jt % J_HALF
+            ws_pass = (
+                ws_codes[:, 2 * PASS * half : 2 * PASS * (half + 1)],
+                ws_scale[:, PASS * half : PASS * (half + 1)],
+                2,
+                FP4X4,
+                v_words[P * jt // J_HALF][:, j_in_half : j_in_half + P],
+                v_scales[:, P * jt : P * (jt + 1)],
+            )
+            product(unit, sums, [ws_pass], start=True, stop=True)
+            b_square[unit] = held.tile([P, PASS], F32, name="b_square%d" % n)
+            square(unit, b_square[unit], sums)
+        for unit in UNITS[:A_BANKS]:
+            turn_b(unit)
 
-        def wc_code(a, c0, w):
-            return code_tile("wc%d%d" % (a, c0 // 512))[:, c0 % 512 : c0 % 512 + w]
-
+        picked_planes, xg_rounded, w_rounded = {}, {}, {}
+        xg_codes, wc_codes = {}, {}
         xg_scales = held.tile([P, 2, S], U8, name="xg_scales", align_bytes=64)
         wc_scales = held.tile([P, 2, H], U8, name="wc_scales", align_bytes=64)
         wm_codes = held.tile([P, 2, N], U32, name="wm_codes", align_bytes=64)
         wm_scales = held.tile([P, 2, N], U8, name="wm_scales", align_bytes=64)
-        h_codes = held.tile([P, 2, S], U32, name="h_codes", align_bytes=64)
-        h_scales = held.tile([P, 2, S], U8, name="h_scales", align_bytes=64)
 
-        picked = {}
-        xg16 = {}
-        w16 = {}
+        def gather(plane, j0, width):
+            g, i = divmod(plane, PACK)
+            dst = picked_planes[g, j0 // J_HALF][:, i, j0 % J_HALF : j0 % J_HALF + width]
+            picks = x_plane[plane][:].indirect(entries(frame_lists, j0, width))
+            nc.vector.tensor_tensor(dst, picks, weights[:, j0 : j0 + width], ALU.mult)
 
-        def table_words(j0, w):
-            sel = offs_t[:, j0 // 16 : (j0 + w) // 16]
-            if j0 == 0:
-                v_half[0] = held.tile([P, 512], U32, name="v_words0", align_bytes=64)
-            else:
-                v_half[1] = ring.tile([P, 512], U32, name="v_words1", tag="wss", bufs=1, align_bytes=64)
-            nc.vector.tensor_copy(out=v_half[j0 // 512][:], in_=tabw[:].bitcast(U32).indirect(sel))
+        def gather_plane(plane):
+            for j0 in (0, J_HALF):
+                gather(plane, j0, J_HALF)
 
-        def table_scales(j0, w):
-            sel = offs_t[:, j0 // 16 : (j0 + w) // 16]
-            nc.vector.tensor_copy(out=v_scales[:, j0 : j0 + w], in_=tabs[:].bitcast(U8).indirect(sel))
-
-        def gather(q, j0, w):
-            a, i = divmod(q, 4)
-            half = j0 // 512
-            if (a, half) not in picked:
-                picked[(a, half)] = ring.tile([P, 4, 512], F32, name="picked", tag=SLOT["pk%d%d" % (a, half)], bufs=1, align_bytes=64)
-            sel = offs2_t[:, j0 // 16 : (j0 + w) // 16]
-            dst = picked[(a, half)][:, i, j0 % 512 : j0 % 512 + w]
-            nc.vector.tensor_tensor(dst, xp[q][:].indirect(sel), wgt_t[:, j0 : j0 + w], ALU.mult)
-
-        def group_xg(a, j0, w, eng):
-            xg16[(a, j0)] = ring.tile([P, w, 4], BF16, name="xg16", tag=SLOT["xg%d_%d" % (a, j0)], bufs=1, align_bytes=64)
-            src = picked[(a, j0 // 512)][:, :, j0 % 512 : j0 % 512 + w]
-            copy_on(
-                eng,
-                xg16[(a, j0)][:].rearrange("p (c e) i -> p c i e", e=4),
+        def round_xg(g, j0, width, engine, tag):
+            xg_rounded[g, j0] = buffer(tag, [P, width, PACK], BF16)
+            src = picked_planes[g, j0 // J_HALF][:, :, j0 % J_HALF : j0 % J_HALF + width]
+            round_copy(
+                engine,
+                xg_rounded[g, j0][:].rearrange("p (c e) i -> p c i e", e=4),
                 src.rearrange("p i (c e) -> p c i e", e=4),
             )
 
-        def quant_xg(a, j0, w):
+        def quantize_xg(g, j0, width):
             nc.vector.quantize_mx(
-                out=xg_code(a, j0, w).bitcast(FP8X4),
-                scales=xg_scales[:, a, j0 : j0 + w],
-                in_=xg16[(a, j0)][:].rearrange("p j i -> p (j i)"),
+                out=xg_codes[g, j0 // J_HALF][:, j0 % J_HALF : j0 % J_HALF + width].bitcast(FP8X4),
+                scales=xg_scales[:, g, j0 : j0 + width],
+                in_=xg_rounded[g, j0][:].rearrange("p j i -> p (j i)"),
             )
 
-        def group_wc(a, hh, eng, m0, m1):
-            if (a, hh) not in w16:
-                w16[(a, hh)] = ring.tile([P, 2048], BF16, name="w16", tag=SLOT["w16_%d%d" % (a, hh)], bufs=1, align_bytes=64)
-            src = raw["wc%d%d" % (a, hh)][:].rearrange("p i (m t) -> p m i t", t=4)
-            dst = w16[(a, hh)][:].rearrange("p (t m i) -> p m i t", t=4, i=4)
-            copy_on(eng, dst[:, m0:m1], src[:, m0:m1])
+        def round_wc(g, half, engine, m0, m1):
+            src = wc_raw[g, half][:].rearrange("p i (m t) -> p m i t", t=PACK)
+            dst = w_rounded[g, half][:].rearrange("p (t m i) -> p m i t", t=PACK, i=PACK)
+            round_copy(engine, dst[:, m0:m1], src[:, m0:m1])
 
-        def quant_wc(a, hh):
-            cols = slice(512 * hh, 512 * (hh + 1))
-            nc.vector.quantize_mx(out=wc_code(a, cols.start, cols.stop - cols.start).bitcast(FP8X4), scales=wc_scales[:, a, cols], in_=w16[(a, hh)][:])
-
-        def group_wm(a, eng):
-            if "wm" not in w16:
-                w16["wm"] = ring.tile([P, 2048], BF16, name="w16", tag=SLOT["w16_m"], bufs=1, align_bytes=64)
-            copy_on(
-                eng,
-                w16["wm"][:, 1024 * a : 1024 * (a + 1)].rearrange("p (c e i) -> p c i e", e=4, i=4),
-                raw["wm"][:, a, :].rearrange("p (i c e) -> p c i e", i=4, e=4),
-            )
-
-        def quant_wm():
+        def quantize_wc(g, half):
             nc.vector.quantize_mx(
-                out=wm_codes[:].rearrange("p a n -> p (a n)").bitcast(FP8X4),
-                scales=wm_scales[:].rearrange("p a n -> p (a n)"),
-                in_=w16["wm"][:],
+                out=wc_codes[g, half].bitcast(FP8X4),
+                scales=wc_scales[:, g, PASS * half : PASS * (half + 1)],
+                in_=w_rounded[g, half][:],
             )
 
-        abank = {}
-        asq = {}
-        tbank = {}
-        ybank = {}
+        def prepare_wm():
+            wm_rounded = buffer("round_b", [P, 2, N * PACK], BF16)
+            for half in range(2):
+                nc.vector.tensor_copy(
+                    out=wm_rounded[:, half, :].rearrange("p (c e i) -> p c i e", e=4, i=PACK),
+                    in_=wm_raw[:, half, :].rearrange("p (i c e) -> p c i e", i=PACK, e=4),
+                )
+            nc.vector.quantize_mx(
+                out=wm_codes[:].rearrange("p g n -> p (g n)").bitcast(FP8X4),
+                scales=wm_scales[:].rearrange("p g n -> p (g n)"),
+                in_=wm_rounded[:].rearrange("p g c -> p (g c)"),
+            )
 
-        def a_mm(hh, jt, bk, passes):
-            js = slice(P * jt, P * (jt + 1))
-            if (hh, jt) not in abank:
-                abank[(hh, jt)] = psum.tile([P, 512], F32, name="bank_a", tag="bank%d" % bk, bufs=1)
-            bank = abank[(hh, jt)]
-            if form(hh, jt) in "AD":
-                for t in range(4):
-                    cols = slice(512 * hh + P * t, 512 * hh + P * (t + 1))
-                    for a in (1, 0):
-                        nc.tensor.matmul_mx(
-                            out=bank[:, P * t : P * (t + 1)],
-                            lhsT=wc_code(a, cols.start, cols.stop - cols.start).bitcast(FP8X4),
-                            lhsT_scale=wc_scales[:, a, cols],
-                            rhs=xg_code(a, P * jt, P).bitcast(FP8X4),
-                            rhs_scale=xg_scales[:, a, js],
-                            start=(a == 1),
-                            stop=(a == 0),
-                        )
+        a_sums, a_square = {}, {}
+
+        def multiply_a(index, passes, start, stop):
+            unit = half, jt = UNITS[index]
+            if start:
+                a_sums[unit] = bank(index % A_BANKS, [P, PASS])
+            j_in_half = P * jt % J_HALF
+            operands = [
+                (
+                    wc_codes[g, half],
+                    wc_scales[:, g, PASS * half : PASS * (half + 1)],
+                    1,
+                    FP8X4,
+                    xg_codes[g, P * jt // J_HALF][:, j_in_half : j_in_half + P],
+                    xg_scales[:, g, P * jt : P * (jt + 1)],
+                )
+                for g in passes
+            ]
+            product(unit, a_sums[unit], operands, start, stop)
+
+        picked_planes[0, 0] = buffer("picked_a", [P, PACK, J_HALF], F32)
+        picked_planes[0, 1] = buffer("picked_b", [P, PACK, J_HALF], F32)
+        gather_plane(0)
+        load_wc(0, 1, "plane0")
+        gather_plane(1)
+        load_wc(1, 1, "plane1")
+        gather_plane(2)
+        wm_raw = buffer("plane2", [P, 2, PACK * N], F32)
+        nc.sync.dma_start(out=wm_raw[:], in_=wm.rearrange("(g p i) n -> p g (i n)", g=2, i=PACK))
+        gather(3, 0, J_HALF)
+        round_xg(0, 0, J_HALF, "scalar", "round_a")
+        gather(3, J_HALF, J_HALF)
+        round_xg(0, J_HALF, J_HALF, "scalar", "round_e")
+
+        picked_planes[1, 0] = buffer("table", [P, PACK, J_HALF], F32)
+        picked_planes[1, 1] = buffer("plane3", [P, PACK, J_HALF], F32)
+        gather_plane(4)
+        xg_codes[0, 0] = buffer("plane4", [P, J_HALF], U32)[:]
+        quantize_xg(0, 0, J_HALF)
+        w_rounded[0, 0] = buffer("round_b", [P, PASS * PACK], BF16)
+        round_wc(0, 0, "scalar", 0, P)
+        gather_plane(5)
+        gather_plane(6)
+        on_plane6 = buffer("plane6", [P, 2, PASS], U32)
+        wc_codes[0, 0], xg_codes[0, 1] = on_plane6[:, 0, :], on_plane6[:, 1, :]
+        quantize_wc(0, 0)
+        w_rounded[1, 0] = buffer("round_f", [P, PASS * PACK], BF16)
+        round_wc(1, 0, "scalar", 0, WC_SPLIT)
+        round_wc(1, 0, "vector", WC_SPLIT, P)
+        quantize_xg(0, J_HALF, J_HALF)
+        for index in range(A_BANKS):
+            multiply_a(index, [0], start=True, stop=False)
+        for g, half in ((1, 0), (0, 1), (1, 1)):
+            wc_codes[g, half] = held.tile([P, PASS], U32, name="wc_codes%d%d" % (g, half), align_bytes=64)[:]
+        for j_half in range(2):
+            xg_codes[1, j_half] = held.tile([P, J_HALF], U32, name="xg_codes1%d" % j_half, align_bytes=64)[:]
+        quantize_wc(1, 0)
+
+        for c in range(len(LAST_PIECES) + 2):
+            if c < len(LAST_PIECES):
+                gather(7, *LAST_PIECES[c][:2])
+            if 1 <= c <= len(LAST_PIECES):
+                j0, width, engine, letter = LAST_PIECES[c - 1]
+                round_xg(1, j0, width, engine, "round_" + letter)
+            if c >= 2:
+                quantize_xg(1, *LAST_PIECES[c - 2][:2])
+        for g, tag in ((0, "round_b"), (1, "round_e")):
+            w_rounded[g, 1] = buffer(tag, [P, PASS * PACK], BF16)
+            round_wc(g, 1, "vector", 0, P)
+        for g in range(2):
+            quantize_wc(g, 1)
+
+        h_rounded = [held.tile([P, S * PACK], BF16, name="h_rounded%d" % half, align_bytes=64) for half in range(2)]
+        h_codes = held.tile([P, 2, S], U32, name="h_codes", align_bytes=64)
+        h_scales = held.tile([P, 2, S], U8, name="h_scales", align_bytes=64)
+        mel_sums = {}
+
+        def square_a(unit):
+            a_square[unit] = shared.tile([P, PASS], F32, name="a_square", tag="a_square", bufs=4)
+            square(unit, a_square[unit], a_sums[unit])
+
+        def add_squares(unit):
+            if unit in TURNED:
+                turn(unit, a_square[unit], start=False)
             else:
-                cols = slice(512 * hh, 512 * (hh + 1))
-                first = 1 if passes == 2 else 0
-                for a in ((1, 0) if passes == 2 else (passes,)):
-                    nc.tensor.matmul_mx(
-                        out=bank[:],
-                        lhsT=xg_code(a, P * jt, P).bitcast(FP8X4),
-                        lhsT_scale=xg_scales[:, a, js],
-                        rhs=wc_code(a, cols.start, cols.stop - cols.start).bitcast(FP8X4),
-                        rhs_scale=wc_scales[:, a, cols],
-                        start=(a == first),
-                        stop=(a != first),
-                    )
+                nc.vector.tensor_tensor(b_square[unit][:], a_square[unit][:], b_square[unit][:], ALU.add)
 
-        acopy = {}
-
-        def a_view(hh, jt, tile_ap):
-            if form(hh, jt) in "AD":
-                return tile_ap.rearrange("p (j t) -> p j t", t=4), abank[(hh, jt)][:].rearrange("p (t j) -> p j t", t=4)
-            return tile_ap, abank[(hh, jt)][:]
-
-        def a_cp(hh, jt):
-            acopy[(hh, jt)] = ring.tile([P, 512], F32, name="acopy", tag="acopy", bufs=2)
-            dst, src = a_view(hh, jt, acopy[(hh, jt)][:])
-            nc.vector.tensor_copy(out=dst, in_=src)
-
-        def a_sq(hh, jt):
-            asq[(hh, jt)] = ring.tile([P, 512], F32, name="asq", tag="asq", bufs=4)
-            if form(hh, jt) in "CD":
-                nc.vector.tensor_tensor(asq[(hh, jt)][:], acopy[(hh, jt)][:], acopy[(hh, jt)][:], ALU.mult)
-            else:
-                dst, src = a_view(hh, jt, asq[(hh, jt)][:])
-                nc.scalar.activation(out=dst, in_=src, func=ACT.Square)
-
-        def turn_b(hh, jt, bk):
-            total = psum.tile([P, 512], F32, name="bank_t", tag="bank%d" % bk, bufs=1)
-            tbank[(hh, jt)] = total
-            for t in range(4):
-                ts = slice(P * t, P * (t + 1))
-                nc.tensor.matmul(total[:, ts], lhsT=bsq[(hh, jt)][:, ts], rhs=ident[:], start=(t == 0), stop=False, is_transpose=True)
-
-        def add_sq(hh, jt, bk):
-            if form(hh, jt) in "AD":
-                nc.vector.tensor_tensor(bsq[(hh, jt)], asq[(hh, jt)][:], bsq[(hh, jt)], ALU.add)
-            else:
-                total = tbank[(hh, jt)]
-                for t in range(4):
-                    ts = slice(P * t, P * (t + 1))
-                    nc.tensor.matmul(total[:, ts], lhsT=asq[(hh, jt)][:, ts], rhs=ident[:], start=False, stop=(t == 3), is_transpose=True)
-
-        h16 = [held.tile([P, 4 * S], BF16, name="h16_%d" % hh, align_bytes=64) for hh in range(2)]
-
-        def root(hh, jt):
-            dst = h16[hh][:, 512 * jt : 512 * (jt + 1)]
-            if form(hh, jt) in "AD":
-                nc.scalar.activation(out=dst, in_=bsq[(hh, jt)], func=ACT.Sqrt)
-            else:
+        def root(unit):
+            half, jt = unit
+            dst = h_rounded[half][:, PASS * jt : PASS * (jt + 1)]
+            if unit in TURNED:
                 nc.scalar.activation(
-                    out=dst.rearrange("p (j t) -> p j t", t=4),
-                    in_=tbank[(hh, jt)][:].rearrange("p (t j) -> p j t", t=4),
+                    out=dst.rearrange("p (j t) -> p j t", t=PACK),
+                    in_=turned_sum[unit][:].rearrange("p (t j) -> p j t", t=PACK),
                     func=ACT.Sqrt,
                 )
+            else:
+                nc.scalar.activation(out=dst, in_=b_square[unit][:], func=ACT.Sqrt)
 
-        def quant_h(hh, jt, n):
-            js = slice(P * jt, P * (jt + n))
+        def quantize_h(half, j0, width):
             nc.vector.quantize_mx(
-                out=h_codes[:, hh, js].bitcast(FP8X4),
-                scales=h_scales[:, hh, js],
-                in_=h16[hh][:, 512 * jt : 512 * (jt + n)],
+                out=h_codes[:, half, j0 : j0 + width].bitcast(FP8X4),
+                scales=h_scales[:, half, j0 : j0 + width],
+                in_=h_rounded[half][:, PACK * j0 : PACK * (j0 + width)],
             )
 
-        def y_mm(j0, w, bk):
-            bank = psum.tile([P, 2, w], F32, name="bank_y", tag="bank%d" % bk, bufs=1)
-            ybank[j0] = bank
-            for c in range(2):
-                for hh in (1, 0):
+        def multiply_mel(j0, width, number):
+            mel_sums[j0] = bank(number, [P, N // P, width])
+            for c in range(N // P):
+                for half in (1, 0):
                     nc.tensor.matmul_mx(
-                        out=bank[:, c, :],
-                        lhsT=wm_codes[:, hh, P * c : P * (c + 1)].bitcast(FP8X4),
-                        lhsT_scale=wm_scales[:, hh, P * c : P * (c + 1)],
-                        rhs=h_codes[:, hh, j0 : j0 + w].bitcast(FP8X4),
-                        rhs_scale=h_scales[:, hh, j0 : j0 + w],
-                        start=(hh == 1),
-                        stop=(hh == 0),
+                        out=mel_sums[j0][:, c, :],
+                        lhsT=wm_codes[:, half, P * c : P * (c + 1)].bitcast(FP8X4),
+                        lhsT_scale=wm_scales[:, half, P * c : P * (c + 1)],
+                        rhs=h_codes[:, half, j0 : j0 + width].bitcast(FP8X4),
+                        rhs_scale=h_scales[:, half, j0 : j0 + width],
+                        start=half == 1,
+                        stop=half == 0,
                     )
 
-        def y_out(j0, w, eng):
-            bank = ybank[j0]
-            res = ring.tile([P, 2, w], F32, name="res", tag="res", bufs=5)
-            if eng == "V":
-                nc.vector.tensor_tensor(res[:], bank[:], bias[:].unsqueeze(2).to_broadcast([P, 2, w]), ALU.add)
-            else:
-                for c in range(2):
-                    nc.scalar.activation(out=res[:, c, :], in_=bank[:, c, :], func=ACT.Identity, bias=bias[:, c : c + 1])
-            nc.sync.dma_start(out=out.rearrange("(c p) j -> p c j", p=P)[:, :, j0 : j0 + w], in_=res[:])
+        def store(j0, width):
+            result = held.tile([P, N // P, width], F32, name="result%d" % j0)
+            spread = bias[:].unsqueeze(2).to_broadcast([P, N // P, width])
+            nc.vector.tensor_tensor(result[:], mel_sums[j0][:], spread, ALU.add)
+            nc.sync.dma_start(out=out.rearrange("(c p) j -> p c j", p=P)[:, :, j0 : j0 + width], in_=result[:])
 
-        table_scales(0, 512)
-        table_scales(512, 512)
-        perm_words()
-        table_words(0, 512)
-        perm_scales()
-        table_words(512, 512)
-        sine_mm(0, 2, 0)
-        sine_mm(0, 0, 4)
-        sine_sq(0, 2)
-        sine_mm(1, 2, 1)
-        sine_sq(0, 0)
-        sine_mm(0, 1, 6)
-        sine_mm(0, 3, 2)
-        sine_sq(1, 2)
-        sine_mm(1, 3, 3)
-        sine_mm(1, 0, 5)
-        sine_sq(0, 1)
-        gather(0, 0, 512)
-        sine_mm(1, 1, 7)
-        sine_sq(1, 3)
-        sine_mm(0, 6, 0)
-        sine_mm(0, 4, 4)
-        sine_sq(1, 0)
-        sine_mm(1, 7, 3)
-        gather(0, 512, 512)
-        sine_sq(1, 1)
-        sine_mm(0, 5, 6)
-        sine_mm(1, 4, 5)
-        sine_sq(0, 4)
-        sine_mm(1, 6, 1)
-        gather(1, 0, 512)
-        sine_mm(1, 5, 7)
-        sine_sq(0, 3)
-        turn_b(0, 0, 4)
-        sine_sq(1, 5)
-        sine_mm(0, 7, 2)
-        gather(1, 512, 512)
-        sine_sq(1, 4)
-        turn_b(0, 3, 7)
-        sine_sq(1, 7)
-        turn_b(0, 1, 5)
-        gather(2, 512, 512)
-        sine_sq(0, 5)
-        sine_sq(1, 6)
-        turn_b(0, 2, 6)
-        gather(2, 0, 512)
-        sine_sq(0, 7)
-        sine_sq(0, 6)
-        gather(3, 0, 512)
-        gather(3, 512, 512)
-        group_xg(0, 0, 512, "S")
-        load("wm")
-        gather(4, 0, 512)
-        group_xg(0, 512, 512, "S")
-        gather(4, 512, 512)
-        load("wc01")
-        quant_xg(0, 0, 512)
-        group_wc(0, 0, "S", 0, 128)
-        load("wc11")
-        gather(5, 0, 512)
-        gather(5, 512, 512)
-        gather(6, 512, 512)
-        gather(6, 0, 512)
-        quant_wc(0, 0)
-        gather(7, 0, 128)
-        a_mm(0, 3, 3, 0)
-        gather(7, 128, 128)
-        a_mm(0, 1, 1, 0)
-        group_xg(1, 0, 128, "S")
-        group_wc(1, 0, "V", 0, 64)
-        a_mm(0, 0, 0, 0)
-        group_xg(1, 128, 128, "S")
-        a_mm(0, 2, 2, 0)
-        gather(7, 256, 256)
-        group_wc(1, 0, "V", 64, 128)
-        group_xg(1, 256, 256, "S")
-        quant_xg(1, 128, 128)
-        quant_wc(1, 0)
-        quant_xg(1, 0, 128)
-        a_mm(0, 1, 1, 1)
-        quant_xg(1, 256, 256)
-        a_mm(0, 0, 0, 1)
-        gather(7, 512, 256)
-        a_sq(0, 1)
-        a_mm(0, 3, 3, 1)
-        a_mm(0, 2, 2, 1)
-        a_sq(0, 0)
-        quant_xg(0, 512, 512)
-        add_sq(0, 1, 5)
-        a_sq(0, 3)
-        group_xg(1, 512, 256, "V")
-        add_sq(0, 0, 4)
-        a_sq(0, 2)
-        gather(7, 768, 256)
-        add_sq(0, 3, 7)
-        root(0, 1)
-        quant_xg(1, 512, 256)
-        add_sq(0, 2, 6)
-        group_xg(1, 768, 256, "V")
-        root(0, 3)
-        a_mm(0, 5, 1, 2)
-        group_wc(0, 1, "V", 0, 128)
-        root(0, 0)
-        a_mm(0, 4, 0, 2)
-        a_sq(0, 5)
-        turn_b(0, 5, 5)
-        quant_xg(1, 768, 256)
-        a_sq(0, 4)
-        turn_b(0, 4, 4)
-        quant_wc(0, 1)
-        turn_b(0, 7, 7)
-        root(0, 2)
-        group_wc(1, 1, "V", 0, 128)
-        a_mm(0, 7, 3, 2)
-        a_mm(0, 6, 2, 2)
-        a_sq(0, 7)
-        group_wm(1, "V")
-        add_sq(0, 4, 4)
-        a_sq(0, 6)
-        quant_wc(1, 1)
-        add_sq(0, 5, 5)
-        root(0, 4)
-        group_wm(0, "V")
-        add_sq(0, 7, 7)
-        root(0, 5)
-        turn_b(0, 6, 6)
-        quant_h(0, 0, 4)
-        root(0, 7)
-        a_mm(1, 1, 1, 2)
-        quant_wm()
-        a_mm(1, 0, 0, 2)
-        a_sq(1, 1)
-        add_sq(0, 6, 6)
-        a_sq(1, 0)
-        a_mm(1, 3, 3, 2)
-        root(0, 6)
-        add_sq(1, 0, 0)
-        turn_b(1, 1, 4)
-        a_sq(1, 3)
-        quant_h(0, 4, 4)
-        a_mm(1, 2, 2, 2)
-        root(1, 0)
-        add_sq(1, 3, 0)
-        add_sq(1, 1, 4)
-        a_sq(1, 2)
-        turn_b(1, 4, 5)
-        root(1, 1)
-        add_sq(1, 2, 0)
-        a_mm(1, 4, 0, 2)
-        root(1, 3)
-        quant_h(1, 0, 2)
-        a_mm(1, 5, 1, 2)
-        root(1, 2)
-        a_mm(1, 7, 3, 2)
-        a_sq(1, 4)
-        quant_h(1, 2, 2)
-        y_mm(0, 256, 7)
-        a_sq(1, 5)
-        a_mm(1, 6, 2, 2)
-        a_sq(1, 7)
-        y_out(0, 256, "V")
-        add_sq(1, 4, 5)
-        add_sq(1, 5, 0)
-        a_sq(1, 6)
-        y_mm(256, 256, 7)
-        add_sq(1, 7, 0)
-        root(1, 4)
-        add_sq(1, 6, 0)
-        root(1, 5)
-        y_out(256, 256, "V")
-        root(1, 7)
-        quant_h(1, 4, 2)
-        root(1, 6)
-        quant_h(1, 7, 1)
-        y_mm(512, 256, 7)
-        quant_h(1, 6, 1)
-        y_mm(896, 128, 1)
-        y_out(512, 256, "V")
-        y_mm(768, 128, 0)
-        y_out(896, 128, "S")
-        y_out(768, 128, "V")
+        mel_step = {j0: S // P + (j0 + width) // P + ROOT_LAG for j0, width, number in OUT_PIECES}
+        store_step = {j0: step + (FIRST_STORE_LAG if j0 == 0 else 1) for j0, step in mel_step.items()}
+        for step in range(max(store_step.values()) + 1):
+            if step == WM_STEP:
+                prepare_wm()
+            if step == LATE_TURN_STEP:
+                for unit in UNITS[-2:]:
+                    turn_b(unit)
+                quantize_h(0, 0, J_HALF)
+            if step == S // P + ROOT_LAG:
+                quantize_h(0, J_HALF, J_HALF)
+            for j0, width, number in OUT_PIECES:
+                if step == mel_step[j0]:
+                    quantize_h(1, j0, width)
+                    multiply_mel(j0, width, number)
+                if step == store_step[j0]:
+                    store(j0, width)
+            if step < A_BANKS:
+                multiply_a(step, [1], start=False, stop=True)
+            elif step < len(UNITS):
+                multiply_a(step, [1, 0], start=True, stop=True)
+            for lag, stage in ((SQUARE_LAG, square_a), (ADD_LAG, add_squares), (ROOT_LAG, root)):
+                if 0 <= step - lag < len(UNITS):
+                    stage(UNITS[step - lag])

@@ -28,7 +28,7 @@ A_BANKS = 4
 UNITS = [(half, jt) for half in range(2) for jt in range(S // P)]
 TURNED = {(0, 0): 4, (0, 1): 5, (0, 2): 6, (0, 3): 7, (1, 6): 6, (1, 7): 7}
 LAST_PIECES = [(0, 128, "vector", "c"), (128, 128, "scalar", "d"), (256, 256, "scalar", "a"), (512, 256, "vector", "c"), (768, 256, "vector", "d")]
-WC_SPLIT = 96
+WC_SPLIT = 2
 OUT_PIECES = [(0, 256, 4), (256, 256, 5), (512, 256, 4), (768, 128, 5), (896, 128, 0)]
 SQUARE_LAG, ADD_LAG, ROOT_LAG = 1, 2, 3
 WM_STEP = 9
@@ -83,11 +83,6 @@ def tile_list_quadrature_magnitude_mel_kernel(
         bias = held.tile([P, N // P], F32, name="bias")
         identity = held.tile([P, P], F32, name="identity")
 
-        warm_in = held.tile([P, 1], F32, name="warm_in")
-        warm_out = held.tile([P, 1], F32, name="warm_out")
-        nc.vector.memset(warm_in[:], 1.0)
-        nc.scalar.activation(out=warm_out[:], in_=warm_in[:], func=ACT.Sqrt)
-
         nc.gpsimd.memset(table_scales[:], 0)
         nc.vector.memset(ws_scales_raw[:], 0)
         make_identity(nc, identity[:])
@@ -106,8 +101,6 @@ def tile_list_quadrature_magnitude_mel_kernel(
         load_plane(6)
         load_wc(1, 0, "wc_b")
         load_plane(7)
-        with nc.allow_non_contiguous_dma(reason="band 128 c + p's bias goes to partition p, column c"):
-            nc.sync.dma_start(out=bias[:], in_=bm.rearrange("(c p) -> p c", p=P))
 
         v_scales = held.tile([P, S], U8, name="v_scales", align_bytes=64)
         ws_codes = held.tile([P, 2 * H], U8, name="ws_codes", align_bytes=64)
@@ -121,13 +114,13 @@ def tile_list_quadrature_magnitude_mel_kernel(
             picks = table_scales[:].bitcast(U8).indirect(entries(table_list, j0, J_HALF))
             nc.vector.tensor_copy(out=v_scales[:, j0 : j0 + J_HALF], in_=picks)
         nc.vector.tensor_copy(
-            out=ws_codes[:].bitcast(U16).rearrange("p (h t m) -> p h m t", h=2, t=PACK),
-            in_=ws_words_raw[:].bitcast(U16).rearrange("p (h m t) -> p h m t", h=2, t=PACK),
+            out=ws_codes[:].bitcast(I32).rearrange("p (h t u) -> p h u t", h=2, t=PACK),
+            in_=ws_words_raw[:].rearrange("p (h u t) -> p h u t", h=2, t=PACK),
         )
         nc.vector.tensor_copy(out=v_words[0][:], in_=table_words[:].bitcast(U32).indirect(entries(table_list, 0, J_HALF)))
         nc.vector.tensor_copy(
-            out=ws_scale[:].rearrange("p (h t m) -> p h m t", h=2, t=PACK),
-            in_=ws_scales_raw[:].bitcast(U8).rearrange("p (h m t) -> p h m t", h=2, t=PACK),
+            out=ws_scale[:].bitcast(U16).rearrange("p (h t u) -> p h u t", h=2, t=PACK),
+            in_=ws_scales_raw[:].bitcast(U16).rearrange("p (h u t) -> p h u t", h=2, t=PACK),
         )
         v_words.append(buffer("ws_scales", [P, J_HALF], U32))
         nc.vector.tensor_copy(
@@ -218,8 +211,8 @@ def tile_list_quadrature_magnitude_mel_kernel(
             src = picked_planes[g, j0 // J_HALF][:, :, j0 % J_HALF : j0 % J_HALF + width]
             round_copy(
                 engine,
-                xg_rounded[g, j0][:].rearrange("p (c e) i -> p c i e", e=4),
-                src.rearrange("p i (c e) -> p c i e", e=4),
+                xg_rounded[g, j0][:].rearrange("p (c d) i -> p c i d", d=4),
+                src.rearrange("p i (c d) -> p c i d", d=4),
             )
 
         def quantize_xg(g, j0, width):
@@ -229,10 +222,14 @@ def tile_list_quadrature_magnitude_mel_kernel(
                 in_=xg_rounded[g, j0][:].rearrange("p j i -> p (j i)"),
             )
 
-        def round_wc(g, half, engine, m0, m1):
-            src = wc_raw[g, half][:].rearrange("p i (m t) -> p m i t", t=PACK)
-            dst = w_rounded[g, half][:].rearrange("p (t m i) -> p m i t", t=PACK, i=PACK)
-            round_copy(engine, dst[:, m0:m1], src[:, m0:m1])
+        def round_wc(g, half, engine, places):
+            src = wc_raw[g, half][:].rearrange("p i (u t e) -> p t u i e", t=PACK, e=2)
+            dst = w_rounded[g, half][:].rearrange("p (t u e i) -> p t u i e", t=PACK, e=2, i=PACK)
+            if engine == "vector" and len(places) == PACK:
+                round_copy(engine, dst, src)
+            else:
+                for t in places:
+                    round_copy(engine, dst[:, t], src[:, t])
 
         def quantize_wc(g, half):
             nc.vector.quantize_mx(
@@ -245,8 +242,8 @@ def tile_list_quadrature_magnitude_mel_kernel(
             wm_rounded = buffer("round_b", [P, 2, N * PACK], BF16)
             for half in range(2):
                 nc.vector.tensor_copy(
-                    out=wm_rounded[:, half, :].rearrange("p (c e i) -> p c i e", e=4, i=PACK),
-                    in_=wm_raw[:, half, :].rearrange("p (i c e) -> p c i e", i=PACK, e=4),
+                    out=wm_rounded[:, half, :].rearrange("p (c d t) -> p c t d", d=4, t=PACK),
+                    in_=wm_raw[:, half, :, :].rearrange("p t (c d) -> p c t d", d=4),
                 )
             nc.vector.quantize_mx(
                 out=wm_codes[:].rearrange("p g n -> p (g n)").bitcast(FP8X4),
@@ -281,8 +278,13 @@ def tile_list_quadrature_magnitude_mel_kernel(
         gather_plane(1)
         load_wc(1, 1, "plane1")
         gather_plane(2)
-        wm_raw = buffer("plane2", [P, 2, PACK * N], F32)
-        nc.sync.dma_start(out=wm_raw[:], in_=wm.rearrange("(g p i) n -> p g (i n)", g=2, i=PACK))
+        wm_raw = buffer("plane2", [P, 2, PACK, N], F32)
+        wm_rows = wm.rearrange("(half u t e) n -> half e u t n", half=2, t=PACK, e=2)
+        for half in range(2):
+            for e in range(2):
+                nc.sync.dma_start(out=wm_raw[e:P:2, half, :, :], in_=wm_rows[half, e])
+        with nc.allow_non_contiguous_dma(reason="band 128 c + p's bias goes to partition p, column c"):
+            nc.sync.dma_start(out=bias[:], in_=bm.rearrange("(c p) -> p c", p=P))
         gather(3, 0, J_HALF)
         round_xg(0, 0, J_HALF, "scalar", "round_a")
         gather(3, J_HALF, J_HALF)
@@ -294,15 +296,15 @@ def tile_list_quadrature_magnitude_mel_kernel(
         xg_codes[0, 0] = buffer("plane4", [P, J_HALF], U32)[:]
         quantize_xg(0, 0, J_HALF)
         w_rounded[0, 0] = buffer("round_b", [P, PASS * PACK], BF16)
-        round_wc(0, 0, "scalar", 0, P)
+        round_wc(0, 0, "scalar", range(PACK))
         gather_plane(5)
         gather_plane(6)
         on_plane6 = buffer("plane6", [P, 2, PASS], U32)
         wc_codes[0, 0], xg_codes[0, 1] = on_plane6[:, 0, :], on_plane6[:, 1, :]
         quantize_wc(0, 0)
         w_rounded[1, 0] = buffer("round_f", [P, PASS * PACK], BF16)
-        round_wc(1, 0, "scalar", 0, WC_SPLIT)
-        round_wc(1, 0, "vector", WC_SPLIT, P)
+        round_wc(1, 0, "scalar", range(WC_SPLIT))
+        round_wc(1, 0, "vector", range(WC_SPLIT, PACK))
         quantize_xg(0, J_HALF, J_HALF)
         for index in range(A_BANKS):
             multiply_a(index, [0], start=True, stop=False)
@@ -322,7 +324,7 @@ def tile_list_quadrature_magnitude_mel_kernel(
                 quantize_xg(1, *LAST_PIECES[c - 2][:2])
         for g, tag in ((0, "round_b"), (1, "round_e")):
             w_rounded[g, 1] = buffer(tag, [P, PASS * PACK], BF16)
-            round_wc(g, 1, "vector", 0, P)
+            round_wc(g, 1, "vector", range(PACK))
         for g in range(2):
             quantize_wc(g, 1)
 

@@ -21,13 +21,20 @@ P = 128
 PACK = 4
 PASS = P * PACK
 ROW = 16
+RUN = 4
 J_HALF = S // 2
 BANKS = 8
 A_BANKS = 4
 
 UNITS = [(half, jt) for half in range(2) for jt in range(S // P)]
 TURNED = {(0, 0): 4, (0, 1): 5, (0, 2): 6, (0, 3): 7, (1, 6): 6, (1, 7): 7}
-LAST_PIECES = [(0, 128, "vector", "c"), (128, 128, "scalar", "d"), (256, 256, "scalar", "a"), (512, 256, "vector", "c"), (768, 256, "vector", "d")]
+LAST_PIECES = [
+    (0, 128, "vector", "round_c"),
+    (128, 128, "scalar", "round_d"),
+    (256, 256, "scalar", "round_a"),
+    (512, 256, "vector", "round_c"),
+    (768, 256, "vector", "round_d"),
+]
 WC_SPLIT = 2
 OUT_PIECES = [(0, 256, 4), (256, 256, 5), (512, 256, 4), (768, 128, 5), (896, 128, 0)]
 SQUARE_LAG, ADD_LAG, ROOT_LAG = 1, 2, 3
@@ -58,8 +65,8 @@ def tile_list_quadrature_magnitude_mel_kernel(
                 nc.scalar.copy(out=dst, in_=src)
 
         def load_scale_rows(dst, rows):
-            for q in range(4):
-                nc.sync.dma_start(out=dst[32 * q : 32 * q + 4, :], in_=rows[4 * q : 4 * q + 4, :].bitcast(I32))
+            for row in range(4):
+                nc.sync.dma_start(out=dst[row:P:32, :], in_=rows[row:16:4, :].bitcast(I32))
 
         def load_plane(plane):
             g, i = divmod(plane, PACK)
@@ -82,6 +89,11 @@ def tile_list_quadrature_magnitude_mel_kernel(
         ws_scales_raw = buffer("ws_scales", [P, H // 4], I32)
         bias = held.tile([P, N // P], F32, name="bias")
         identity = held.tile([P, P], F32, name="identity")
+
+        warm_in = held.tile([P, 1], F32, name="warm_in")
+        warm_out = held.tile([P, 1], F32, name="warm_out")
+        nc.vector.memset(warm_in[:], 1.0)
+        nc.scalar.activation(out=warm_out[:], in_=warm_in[:], func=ACT.Sqrt)
 
         nc.gpsimd.memset(table_scales[:], 0)
         nc.vector.memset(ws_scales_raw[:], 0)
@@ -114,13 +126,13 @@ def tile_list_quadrature_magnitude_mel_kernel(
             picks = table_scales[:].bitcast(U8).indirect(entries(table_list, j0, J_HALF))
             nc.vector.tensor_copy(out=v_scales[:, j0 : j0 + J_HALF], in_=picks)
         nc.vector.tensor_copy(
-            out=ws_codes[:].bitcast(I32).rearrange("p (h t u) -> p h u t", h=2, t=PACK),
-            in_=ws_words_raw[:].rearrange("p (h u t) -> p h u t", h=2, t=PACK),
+            out=ws_codes[:].bitcast(I32).rearrange("p (half t u) -> p half u t", half=2, t=PACK),
+            in_=ws_words_raw[:].rearrange("p (half u t) -> p half u t", half=2, t=PACK),
         )
         nc.vector.tensor_copy(out=v_words[0][:], in_=table_words[:].bitcast(U32).indirect(entries(table_list, 0, J_HALF)))
         nc.vector.tensor_copy(
-            out=ws_scale[:].bitcast(U16).rearrange("p (h t u) -> p h u t", h=2, t=PACK),
-            in_=ws_scales_raw[:].bitcast(U16).rearrange("p (h u t) -> p h u t", h=2, t=PACK),
+            out=ws_scale[:].bitcast(U16).rearrange("p (half t u) -> p half u t", half=2, t=PACK),
+            in_=ws_scales_raw[:].bitcast(U16).rearrange("p (half u t) -> p half u t", half=2, t=PACK),
         )
         v_words.append(buffer("ws_scales", [P, J_HALF], U32))
         nc.vector.tensor_copy(
@@ -130,7 +142,7 @@ def tile_list_quadrature_magnitude_mel_kernel(
         def product(unit, sums, passes, start, stop):
             groups = [slice(0, PASS)] if unit in TURNED else [slice(P * t, P * (t + 1)) for t in range(PACK)]
             for cols in groups:
-                for n, (w_codes, w_scales, per_col, w_dtype, codes, scales) in enumerate(passes):
+                for order, (w_codes, w_scales, per_col, w_dtype, codes, scales) in enumerate(passes):
                     weight = (w_codes[:, per_col * cols.start : per_col * cols.stop].bitcast(w_dtype), w_scales[:, cols])
                     picked = (codes.bitcast(FP8X4), scales)
                     still, moving = (picked, weight) if unit in TURNED else (weight, picked)
@@ -140,8 +152,8 @@ def tile_list_quadrature_magnitude_mel_kernel(
                         lhsT_scale=still[1],
                         rhs=moving[0],
                         rhs_scale=moving[1],
-                        start=start and n == 0,
-                        stop=stop and n == len(passes) - 1,
+                        start=start and order == 0,
+                        stop=stop and order == len(passes) - 1,
                     )
 
         def square(unit, dst, sums):
@@ -171,9 +183,9 @@ def tile_list_quadrature_magnitude_mel_kernel(
             turn(unit, b_square[unit], start=True)
 
         b_square, turned_sum = {}, {}
-        for n, (jt, half) in enumerate((jt, half) for jt in range(S // P) for half in range(2)):
+        for serial, (jt, half) in enumerate((jt, half) for jt in range(S // P) for half in range(2)):
             unit = (half, jt)
-            sums = bank(n % BANKS, [P, PASS])
+            sums = bank(serial % BANKS, [P, PASS])
             j_in_half = P * jt % J_HALF
             ws_pass = (
                 ws_codes[:, 2 * PASS * half : 2 * PASS * (half + 1)],
@@ -184,7 +196,7 @@ def tile_list_quadrature_magnitude_mel_kernel(
                 v_scales[:, P * jt : P * (jt + 1)],
             )
             product(unit, sums, [ws_pass], start=True, stop=True)
-            b_square[unit] = held.tile([P, PASS], F32, name="b_square%d" % n)
+            b_square[unit] = held.tile([P, PASS], F32, name="b_square%d" % serial)
             square(unit, b_square[unit], sums)
         for unit in UNITS[:A_BANKS]:
             turn_b(unit)
@@ -211,8 +223,8 @@ def tile_list_quadrature_magnitude_mel_kernel(
             src = picked_planes[g, j0 // J_HALF][:, :, j0 % J_HALF : j0 % J_HALF + width]
             round_copy(
                 engine,
-                xg_rounded[g, j0][:].rearrange("p (c d) i -> p c i d", d=4),
-                src.rearrange("p i (c d) -> p c i d", d=4),
+                xg_rounded[g, j0][:].rearrange("p (run d) i -> p run i d", d=RUN),
+                src.rearrange("p i (run d) -> p run i d", d=RUN),
             )
 
         def quantize_xg(g, j0, width):
@@ -222,13 +234,13 @@ def tile_list_quadrature_magnitude_mel_kernel(
                 in_=xg_rounded[g, j0][:].rearrange("p j i -> p (j i)"),
             )
 
-        def round_wc(g, half, engine, places):
+        def round_wc(g, half, engine, t_values):
             src = wc_raw[g, half][:].rearrange("p i (u t e) -> p t u i e", t=PACK, e=2)
             dst = w_rounded[g, half][:].rearrange("p (t u e i) -> p t u i e", t=PACK, e=2, i=PACK)
-            if engine == "vector" and len(places) == PACK:
+            if engine == "vector" and len(t_values) == PACK:
                 round_copy(engine, dst, src)
             else:
-                for t in places:
+                for t in t_values:
                     round_copy(engine, dst[:, t], src[:, t])
 
         def quantize_wc(g, half):
@@ -242,13 +254,13 @@ def tile_list_quadrature_magnitude_mel_kernel(
             wm_rounded = buffer("round_b", [P, 2, N * PACK], BF16)
             for half in range(2):
                 nc.vector.tensor_copy(
-                    out=wm_rounded[:, half, :].rearrange("p (c d t) -> p c t d", d=4, t=PACK),
-                    in_=wm_raw[:, half, :, :].rearrange("p t (c d) -> p c t d", d=4),
+                    out=wm_rounded[:, half, :].rearrange("p (run d t) -> p run t d", d=RUN, t=PACK),
+                    in_=wm_raw[:, half, :, :].rearrange("p t (run d) -> p run t d", d=RUN),
                 )
             nc.vector.quantize_mx(
-                out=wm_codes[:].rearrange("p g n -> p (g n)").bitcast(FP8X4),
-                scales=wm_scales[:].rearrange("p g n -> p (g n)"),
-                in_=wm_rounded[:].rearrange("p g c -> p (g c)"),
+                out=wm_codes[:].rearrange("p half n -> p (half n)").bitcast(FP8X4),
+                scales=wm_scales[:].rearrange("p half n -> p (half n)"),
+                in_=wm_rounded[:].rearrange("p half x -> p (half x)"),
             )
 
         a_sums, a_square = {}, {}
@@ -314,14 +326,13 @@ def tile_list_quadrature_magnitude_mel_kernel(
             xg_codes[1, j_half] = held.tile([P, J_HALF], U32, name="xg_codes1%d" % j_half, align_bytes=64)[:]
         quantize_wc(1, 0)
 
-        for c in range(len(LAST_PIECES) + 2):
-            if c < len(LAST_PIECES):
-                gather(7, *LAST_PIECES[c][:2])
-            if 1 <= c <= len(LAST_PIECES):
-                j0, width, engine, letter = LAST_PIECES[c - 1]
-                round_xg(1, j0, width, engine, "round_" + letter)
-            if c >= 2:
-                quantize_xg(1, *LAST_PIECES[c - 2][:2])
+        for piece in range(len(LAST_PIECES) + 2):
+            if piece < len(LAST_PIECES):
+                gather(7, *LAST_PIECES[piece][:2])
+            if 1 <= piece <= len(LAST_PIECES):
+                round_xg(1, *LAST_PIECES[piece - 1])
+            if piece >= 2:
+                quantize_xg(1, *LAST_PIECES[piece - 2][:2])
         for g, tag in ((0, "round_b"), (1, "round_e")):
             w_rounded[g, 1] = buffer(tag, [P, PASS * PACK], BF16)
             round_wc(g, 1, "vector", range(PACK))

@@ -27,20 +27,19 @@ BANKS = 8
 A_BANKS = 4
 
 UNITS = [(half, jt) for half in range(2) for jt in range(S // P)]
-TURNED = {(0, 0): 4, (0, 1): 5, (0, 2): 6, (0, 3): 7, (1, 6): 6, (1, 7): 7}
-LAST_PIECES = [
-    (0, 128, "vector", "round_c"),
-    (128, 128, "scalar", "round_d"),
-    (256, 256, "scalar", "round_a"),
-    (512, 256, "vector", "round_c"),
-    (768, 256, "vector", "round_d"),
-]
+TURNED = dict([((0, jt), A_BANKS + jt % A_BANKS) for jt in range(S // P)] + [((1, 6), 6), ((1, 7), 7)])
+NARROW = 128
+WIDE = 256
 WC_SPLIT = 2
-OUT_PIECES = [(0, 256, 4), (256, 256, 5), (512, 256, 4), (768, 128, 5), (896, 128, 0)]
+OUT_PIECES = [
+    (0, 256, 4, "vector"),
+    (256, 256, 5, "vector"),
+    (512, 256, 4, "scalar"),
+    (768, 128, 5, "vector"),
+    (896, 128, 0, "vector"),
+]
 SQUARE_LAG, ADD_LAG, ROOT_LAG = 1, 2, 3
-WM_STEP = 9
-LATE_TURN_STEP = 10
-FIRST_STORE_LAG = 3
+WM_STEP = 8
 
 
 def tile_list_quadrature_magnitude_mel_kernel(
@@ -74,10 +73,10 @@ def tile_list_quadrature_magnitude_mel_kernel(
             x_plane[plane] = buffer("plane%d" % plane, [P, T], F32)
             nc.sync.dma_start(out=x_plane[plane][:], in_=rows[:, i, :])
 
-        def load_wc(g, half, tag):
-            block = wc[PASS * g : PASS * (g + 1), PASS * half : PASS * (half + 1)]
-            wc_raw[g, half] = buffer(tag, [P, PACK, PASS], F32)
-            nc.sync.dma_start(out=wc_raw[g, half][:], in_=block.rearrange("(p i) r -> p i r", i=PACK))
+        def load_wc(g, bin0, bins, tag):
+            block = wc[PASS * g : PASS * (g + 1), bin0 : bin0 + bins]
+            wc_raw[g, bin0] = buffer(tag, [P, PACK, bins], F32)
+            nc.sync.dma_start(out=wc_raw[g, bin0][:], in_=block.rearrange("(p i) r -> p i r", i=PACK))
 
         x_plane, wc_raw = {}, {}
         table_list = held.tile([P, S // ROW], U16, name="table_list")
@@ -85,8 +84,8 @@ def tile_list_quadrature_magnitude_mel_kernel(
         weights = held.tile([P, S], F32, name="weights")
         table_words = buffer("table", [P, T], I32)
         table_scales = held.tile([P, T // 4], I32, name="table_scales")
-        ws_words_raw = held.tile([P, H // 2], I32, name="ws_words_raw")
-        ws_scales_raw = buffer("ws_scales", [P, H // 4], I32)
+        ws_words_raw = held.tile([P, H // 2], I32, name="ws_words_raw", align_bytes=64)
+        ws_scales_raw = held.tile([P, H // 4], I32, name="ws_scales_raw", align_bytes=64)
         bias = held.tile([P, N // P], F32, name="bias")
         identity = held.tile([P, P], F32, name="identity")
 
@@ -100,44 +99,46 @@ def tile_list_quadrature_magnitude_mel_kernel(
         make_identity(nc, identity[:])
 
         nc.sync.dma_start(table_list[:], offs)
-        load_scale_rows(table_scales, tab_scales[0])
-        nc.sync.dma_start(out=ws_words_raw[:], in_=ws_words[0].bitcast(I32))
-        nc.sync.dma_start(out=table_words[:], in_=tab_words[0].rearrange("p t i -> p (t i)").bitcast(I32))
-        nc.sync.dma_start(out=weights[:], in_=wgt)
-        load_scale_rows(ws_scales_raw, ws_scales[0])
         nc.sync.dma_start(frame_lists[:], offs2)
-        for plane in range(5):
+        load_scale_rows(table_scales, tab_scales[0])
+        nc.sync.dma_start(out=table_words[:], in_=tab_words[0].rearrange("p t i -> p (t i)").bitcast(I32))
+        nc.sync.dma_start(out=weights[:, 0:J_HALF], in_=wgt[:, 0:J_HALF])
+        load_plane(0)
+        nc.sync.dma_start(out=weights[:, J_HALF:S], in_=wgt[:, J_HALF:S])
+        nc.sync.dma_start(out=ws_words_raw[:], in_=ws_words[0].bitcast(I32))
+        load_scale_rows(ws_scales_raw, ws_scales[0])
+        for plane in range(1, 6):
             load_plane(plane)
-        load_wc(0, 0, "wc_a")
-        load_plane(5)
+        load_wc(0, 0, PASS, "wc_a")
         load_plane(6)
-        load_wc(1, 0, "wc_b")
+        load_wc(1, 0, PASS, "wc_b")
         load_plane(7)
 
         v_scales = held.tile([P, S], U8, name="v_scales", align_bytes=64)
-        ws_codes = held.tile([P, 2 * H], U8, name="ws_codes", align_bytes=64)
-        ws_scale = held.tile([P, H], U8, name="ws_scale", align_bytes=64)
-        v_words = [held.tile([P, J_HALF], U32, name="v_words0", align_bytes=64)]
+        ws_codes = held.tile([P, 2 * PASS], U8, name="ws_codes", align_bytes=64)
+        ws_scale = held.tile([P, PASS], U8, name="ws_scale", align_bytes=64)
+        v_words = [held.tile([P, J_HALF], U32, name="v_words%d" % part, align_bytes=64) for part in range(2)]
 
         def entries(lists, j0, width):
             return lists[:, j0 // ROW : (j0 + width) // ROW]
 
-        for j0 in (0, J_HALF):
-            picks = table_scales[:].bitcast(U8).indirect(entries(table_list, j0, J_HALF))
-            nc.vector.tensor_copy(out=v_scales[:, j0 : j0 + J_HALF], in_=picks)
-        nc.vector.tensor_copy(
-            out=ws_codes[:].bitcast(I32).rearrange("p (half t u) -> p half u t", half=2, t=PACK),
-            in_=ws_words_raw[:].rearrange("p (half u t) -> p half u t", half=2, t=PACK),
-        )
+        nc.vector.tensor_copy(out=v_scales[:], in_=table_scales[:].bitcast(U8).indirect(table_list[:]))
         nc.vector.tensor_copy(out=v_words[0][:], in_=table_words[:].bitcast(U32).indirect(entries(table_list, 0, J_HALF)))
-        nc.vector.tensor_copy(
-            out=ws_scale[:].bitcast(U16).rearrange("p (half t u) -> p half u t", half=2, t=PACK),
-            in_=ws_scales_raw[:].bitcast(U16).rearrange("p (half u t) -> p half u t", half=2, t=PACK),
-        )
-        v_words.append(buffer("ws_scales", [P, J_HALF], U32))
         nc.vector.tensor_copy(
             out=v_words[1][:], in_=table_words[:].bitcast(U32).indirect(entries(table_list, J_HALF, J_HALF))
         )
+        nc.vector.tensor_copy(
+            out=ws_codes[:].bitcast(I32).rearrange("p (t u) -> p u t", t=PACK),
+            in_=ws_words_raw[:, PASS // 2 : PASS].rearrange("p (u t) -> p u t", t=PACK),
+        )
+        nc.vector.tensor_copy(
+            out=ws_scale[:].bitcast(U16).rearrange("p (t u) -> p u t", t=PACK),
+            in_=ws_scales_raw[:].bitcast(U16)[:, PASS // 2 : PASS].rearrange("p (u t) -> p u t", t=PACK),
+        )
+        ws_half = [
+            (ws_words_raw[:].bitcast(U8)[:, 0 : 2 * PASS], ws_scales_raw[:].bitcast(U8)[:, 0:PASS]),
+            (ws_codes[:], ws_scale[:]),
+        ]
 
         def product(unit, sums, passes, start, stop):
             groups = [slice(0, PASS)] if unit in TURNED else [slice(P * t, P * (t + 1)) for t in range(PACK)]
@@ -183,13 +184,14 @@ def tile_list_quadrature_magnitude_mel_kernel(
             turn(unit, b_square[unit], start=True)
 
         b_square, turned_sum = {}, {}
-        for serial, (jt, half) in enumerate((jt, half) for jt in range(S // P) for half in range(2)):
-            unit = (half, jt)
+        b_order = [(half, jt0 + jt) for jt0 in (0, J_HALF // P) for half in range(2) for jt in range(J_HALF // P)]
+        for serial, unit in enumerate(b_order):
+            half, jt = unit
             sums = bank(serial % BANKS, [P, PASS])
             j_in_half = P * jt % J_HALF
             ws_pass = (
-                ws_codes[:, 2 * PASS * half : 2 * PASS * (half + 1)],
-                ws_scale[:, PASS * half : PASS * (half + 1)],
+                ws_half[half][0],
+                ws_half[half][1],
                 2,
                 FP4X4,
                 v_words[P * jt // J_HALF][:, j_in_half : j_in_half + P],
@@ -197,7 +199,14 @@ def tile_list_quadrature_magnitude_mel_kernel(
             )
             product(unit, sums, [ws_pass], start=True, stop=True)
             b_square[unit] = held.tile([P, PASS], F32, name="b_square%d" % serial)
-            square(unit, b_square[unit], sums)
+            if half == 0:
+                nc.scalar.activation(
+                    out=b_square[unit][:].rearrange("p (t u e) -> p t u e", t=PACK, e=2),
+                    in_=sums[:].rearrange("p (u t e) -> p t u e", t=PACK, e=2),
+                    func=ACT.Square,
+                )
+            else:
+                square(unit, b_square[unit], sums)
         for unit in UNITS[:A_BANKS]:
             turn_b(unit)
 
@@ -210,17 +219,16 @@ def tile_list_quadrature_magnitude_mel_kernel(
 
         def gather(plane, j0, width):
             g, i = divmod(plane, PACK)
-            dst = picked_planes[g, j0 // J_HALF][:, i, j0 % J_HALF : j0 % J_HALF + width]
+            dst = picked_planes[g][:, i, j0 : j0 + width]
             picks = x_plane[plane][:].indirect(entries(frame_lists, j0, width))
             nc.vector.tensor_tensor(dst, picks, weights[:, j0 : j0 + width], ALU.mult)
 
         def gather_plane(plane):
-            for j0 in (0, J_HALF):
-                gather(plane, j0, J_HALF)
+            gather(plane, 0, S)
 
         def round_xg(g, j0, width, engine, tag):
             xg_rounded[g, j0] = buffer(tag, [P, width, PACK], BF16)
-            src = picked_planes[g, j0 // J_HALF][:, :, j0 % J_HALF : j0 % J_HALF + width]
+            src = picked_planes[g][:, :, j0 : j0 + width]
             round_copy(
                 engine,
                 xg_rounded[g, j0][:].rearrange("p (run d) i -> p run i d", d=RUN),
@@ -234,24 +242,20 @@ def tile_list_quadrature_magnitude_mel_kernel(
                 in_=xg_rounded[g, j0][:].rearrange("p j i -> p (j i)"),
             )
 
-        def round_wc(g, half, engine, t_values):
-            src = wc_raw[g, half][:].rearrange("p i (u t e) -> p t u i e", t=PACK, e=2)
-            dst = w_rounded[g, half][:].rearrange("p (t u e i) -> p t u i e", t=PACK, e=2, i=PACK)
-            if engine == "vector" and len(t_values) == PACK:
-                round_copy(engine, dst, src)
-            else:
-                for t in t_values:
-                    round_copy(engine, dst[:, t], src[:, t])
+        def round_wc(g, half, engine, t0, t1):
+            src = wc_raw[g, PASS * half][:].rearrange("p i (u t e) -> p t u i e", t=PACK, e=2)
+            dst = w_rounded[g, half].rearrange("p (t u e i) -> p t u i e", t=PACK, e=2, i=PACK)
+            round_copy(engine, dst[:, t0:t1], src[:, t0:t1])
 
         def quantize_wc(g, half):
             nc.vector.quantize_mx(
                 out=wc_codes[g, half].bitcast(FP8X4),
                 scales=wc_scales[:, g, PASS * half : PASS * (half + 1)],
-                in_=w_rounded[g, half][:],
+                in_=w_rounded[g, half],
             )
 
         def prepare_wm():
-            wm_rounded = buffer("round_b", [P, 2, N * PACK], BF16)
+            wm_rounded = buffer("wc_a", [P, 2, N * PACK], BF16)
             for half in range(2):
                 nc.vector.tensor_copy(
                     out=wm_rounded[:, half, :].rearrange("p (run d t) -> p run t d", d=RUN, t=PACK),
@@ -283,12 +287,13 @@ def tile_list_quadrature_magnitude_mel_kernel(
             ]
             product(unit, a_sums[unit], operands, start, stop)
 
-        picked_planes[0, 0] = buffer("picked_a", [P, PACK, J_HALF], F32)
-        picked_planes[0, 1] = buffer("picked_b", [P, PACK, J_HALF], F32)
-        gather_plane(0)
-        load_wc(0, 1, "plane0")
+        for g in range(2):
+            picked_planes[g] = held.tile([P, PACK, S], F32, name="picked%d" % g)
+        gather(0, 0, J_HALF)
+        gather(0, J_HALF, J_HALF)
+        load_wc(0, PASS, PASS, "plane0")
         gather_plane(1)
-        load_wc(1, 1, "plane1")
+        load_wc(1, PASS, PASS, "plane1")
         gather_plane(2)
         wm_raw = buffer("plane2", [P, 2, PACK, N], F32)
         wm_rows = wm.rearrange("(half u t e) n -> half e u t n", half=2, t=PACK, e=2)
@@ -298,26 +303,26 @@ def tile_list_quadrature_magnitude_mel_kernel(
         with nc.allow_non_contiguous_dma(reason="band 128 c + p's bias goes to partition p, column c"):
             nc.sync.dma_start(out=bias[:], in_=bm.rearrange("(c p) -> p c", p=P))
         gather(3, 0, J_HALF)
-        round_xg(0, 0, J_HALF, "scalar", "round_a")
+        round_xg(0, 0, J_HALF, "scalar", "round_x0")
         gather(3, J_HALF, J_HALF)
-        round_xg(0, J_HALF, J_HALF, "scalar", "round_e")
+        round_xg(0, J_HALF, J_HALF, "scalar", "round_x1")
 
-        picked_planes[1, 0] = buffer("table", [P, PACK, J_HALF], F32)
-        picked_planes[1, 1] = buffer("plane3", [P, PACK, J_HALF], F32)
         gather_plane(4)
-        xg_codes[0, 0] = buffer("plane4", [P, J_HALF], U32)[:]
-        quantize_xg(0, 0, J_HALF)
-        w_rounded[0, 0] = buffer("round_b", [P, PASS * PACK], BF16)
-        round_wc(0, 0, "scalar", range(PACK))
         gather_plane(5)
-        gather_plane(6)
-        on_plane6 = buffer("plane6", [P, 2, PASS], U32)
-        wc_codes[0, 0], xg_codes[0, 1] = on_plane6[:, 0, :], on_plane6[:, 1, :]
-        quantize_wc(0, 0)
-        w_rounded[1, 0] = buffer("round_f", [P, PASS * PACK], BF16)
-        round_wc(1, 0, "scalar", range(WC_SPLIT))
-        round_wc(1, 0, "vector", range(WC_SPLIT, PACK))
+        on_plane5 = buffer("plane5", [P, T], U32)
+        xg_codes[0, 0], xg_codes[0, 1] = on_plane5[:, 0:J_HALF], on_plane5[:, J_HALF:S]
+        quantize_xg(0, 0, J_HALF)
         quantize_xg(0, J_HALF, J_HALF)
+        w_rounded[0, 0] = buffer("round_w0", [P, PASS * PACK], BF16)[:]
+        round_wc(0, 0, "scalar", 0, PACK)
+        gather_plane(6)
+        on_plane6 = buffer("plane6", [P, T], U32)
+        wc_codes[0, 0] = on_plane6[:, 0:PASS]
+        h_codes = [on_plane5[:, S:T], on_plane6[:, S:T]]
+        quantize_wc(0, 0)
+        w_rounded[1, 0] = buffer("round_w1", [P, PASS * PACK], BF16)[:]
+        round_wc(1, 0, "scalar", 0, WC_SPLIT)
+        round_wc(1, 0, "vector", WC_SPLIT, PACK)
         for index in range(A_BANKS):
             multiply_a(index, [0], start=True, stop=False)
         for g, half in ((1, 0), (0, 1), (1, 1)):
@@ -326,22 +331,31 @@ def tile_list_quadrature_magnitude_mel_kernel(
             xg_codes[1, j_half] = held.tile([P, J_HALF], U32, name="xg_codes1%d" % j_half, align_bytes=64)[:]
         quantize_wc(1, 0)
 
-        for piece in range(len(LAST_PIECES) + 2):
-            if piece < len(LAST_PIECES):
-                gather(7, *LAST_PIECES[piece][:2])
-            if 1 <= piece <= len(LAST_PIECES):
-                round_xg(1, *LAST_PIECES[piece - 1])
-            if piece >= 2:
-                quantize_xg(1, *LAST_PIECES[piece - 2][:2])
-        for g, tag in ((0, "round_b"), (1, "round_e")):
-            w_rounded[g, 1] = buffer(tag, [P, PASS * PACK], BF16)
-            round_wc(g, 1, "vector", range(PACK))
+        for j0 in (0, NARROW):
+            gather(7, j0, NARROW)
+        for j0 in (0, NARROW):
+            round_xg(1, j0, NARROW, "vector", "round_piece%d" % j0)
+        for j0 in (0, NARROW):
+            quantize_xg(1, j0, NARROW)
+        for j0 in (WIDE, WIDE + NARROW):
+            gather(7, j0, NARROW)
+        for j0 in range(WIDE, S + WIDE, WIDE):
+            if j0 < S:
+                round_xg(1, j0, WIDE, "vector", "round_piece%d" % j0)
+            if j0 + WIDE < S:
+                gather(7, j0 + WIDE, WIDE)
+            if j0 < S:
+                quantize_xg(1, j0, WIDE)
+        on_table = buffer("table", [P, 2, PASS * PACK], BF16)
+        for g in range(2):
+            w_rounded[g, 1] = on_table[:, g, :]
+            round_wc(g, 1, "vector", 0, PACK)
         for g in range(2):
             quantize_wc(g, 1)
 
-        h_rounded = [held.tile([P, S * PACK], BF16, name="h_rounded%d" % half, align_bytes=64) for half in range(2)]
-        h_codes = held.tile([P, 2, S], U32, name="h_codes", align_bytes=64)
+        h_rounded = [buffer(tag, [P, S * PACK], BF16) for tag in ("plane3", "plane4")]
         h_scales = held.tile([P, 2, S], U8, name="h_scales", align_bytes=64)
+        results = buffer("plane7", [P, N // P * S], F32)
         mel_sums = {}
 
         def square_a(unit):
@@ -368,7 +382,7 @@ def tile_list_quadrature_magnitude_mel_kernel(
 
         def quantize_h(half, j0, width):
             nc.vector.quantize_mx(
-                out=h_codes[:, half, j0 : j0 + width].bitcast(FP8X4),
+                out=h_codes[half][:, j0 : j0 + width].bitcast(FP8X4),
                 scales=h_scales[:, half, j0 : j0 + width],
                 in_=h_rounded[half][:, PACK * j0 : PACK * (j0 + width)],
             )
@@ -381,39 +395,50 @@ def tile_list_quadrature_magnitude_mel_kernel(
                         out=mel_sums[j0][:, c, :],
                         lhsT=wm_codes[:, half, P * c : P * (c + 1)].bitcast(FP8X4),
                         lhsT_scale=wm_scales[:, half, P * c : P * (c + 1)],
-                        rhs=h_codes[:, half, j0 : j0 + width].bitcast(FP8X4),
+                        rhs=h_codes[half][:, j0 : j0 + width].bitcast(FP8X4),
                         rhs_scale=h_scales[:, half, j0 : j0 + width],
                         start=half == 1,
                         stop=half == 0,
                     )
 
-        def store(j0, width):
-            result = held.tile([P, N // P, width], F32, name="result%d" % j0)
-            spread = bias[:].unsqueeze(2).to_broadcast([P, N // P, width])
-            nc.vector.tensor_tensor(result[:], mel_sums[j0][:], spread, ALU.add)
-            nc.sync.dma_start(out=out.rearrange("(c p) j -> p c j", p=P)[:, :, j0 : j0 + width], in_=result[:])
+        def store(j0, width, engine):
+            result = results[:, N // P * j0 : N // P * (j0 + width)].rearrange("p (c j) -> p c j", j=width)
+            if engine == "vector":
+                spread = bias[:].unsqueeze(2).to_broadcast([P, N // P, width])
+                nc.vector.tensor_tensor(result, mel_sums[j0][:], spread, ALU.add)
+            else:
+                for c in range(N // P):
+                    nc.scalar.activation(
+                        out=result[:, c, :], in_=mel_sums[j0][:, c, :], func=ACT.Identity, bias=bias[:, c : c + 1]
+                    )
+            nc.sync.dma_start(out=out.rearrange("(c p) j -> p c j", p=P)[:, :, j0 : j0 + width], in_=result)
 
-        mel_step = {j0: S // P + (j0 + width) // P + ROOT_LAG for j0, width, number in OUT_PIECES}
-        store_step = {j0: step + (FIRST_STORE_LAG if j0 == 0 else 1) for j0, step in mel_step.items()}
-        for step in range(max(store_step.values()) + 1):
+        mel_step = {j0: S // P + (j0 + width) // P + ROOT_LAG for j0, width, number, engine in OUT_PIECES}
+        last_step = max(mel_step.values())
+        store_step = {j0: step + 1 if step < len(UNITS) else last_step + 1 for j0, step in mel_step.items()}
+        for step in range(last_step + 2):
             if step == WM_STEP:
                 prepare_wm()
-            if step == LATE_TURN_STEP:
+            for j0 in (0, J_HALF):
+                if step == (j0 + J_HALF) // P + ROOT_LAG:
+                    quantize_h(0, j0, J_HALF)
+            if step == S // P + ROOT_LAG:
                 for unit in UNITS[-2:]:
                     turn_b(unit)
-                quantize_h(0, 0, J_HALF)
-            if step == S // P + ROOT_LAG:
-                quantize_h(0, J_HALF, J_HALF)
-            for j0, width, number in OUT_PIECES:
+            for j0, width, number, engine in OUT_PIECES:
                 if step == mel_step[j0]:
                     quantize_h(1, j0, width)
                     multiply_mel(j0, width, number)
                 if step == store_step[j0]:
-                    store(j0, width)
-            if step < A_BANKS:
+                    store(j0, width, engine)
+            if step < S // P:
                 multiply_a(step, [1], start=False, stop=True)
             elif step < len(UNITS):
                 multiply_a(step, [1, 0], start=True, stop=True)
+            if A_BANKS <= step - 1 < S // P:
+                turn_b(UNITS[step - 1])
             for lag, stage in ((SQUARE_LAG, square_a), (ADD_LAG, add_squares), (ROOT_LAG, root)):
                 if 0 <= step - lag < len(UNITS):
                     stage(UNITS[step - lag])
+            if 0 <= step - SQUARE_LAG < S // P - A_BANKS:
+                multiply_a(step - SQUARE_LAG + A_BANKS, [0], start=True, stop=False)

@@ -99,10 +99,10 @@ def tile_list_quadrature_magnitude_mel_kernel(
         make_identity(nc, identity[:])
 
         nc.sync.dma_start(table_list[:], offs)
+        nc.sync.dma_start(out=weights[:, 0:J_HALF], in_=wgt[:, 0:J_HALF])
         nc.sync.dma_start(frame_lists[:], offs2)
         load_scale_rows(table_scales, tab_scales[0])
         nc.sync.dma_start(out=table_words[:], in_=tab_words[0].rearrange("p t i -> p (t i)").bitcast(I32))
-        nc.sync.dma_start(out=weights[:, 0:J_HALF], in_=wgt[:, 0:J_HALF])
         load_plane(0)
         nc.sync.dma_start(out=weights[:, J_HALF:S], in_=wgt[:, J_HALF:S])
         nc.sync.dma_start(out=ws_words_raw[:], in_=ws_words[0].bitcast(I32))
@@ -128,12 +128,12 @@ def tile_list_quadrature_magnitude_mel_kernel(
             out=v_words[1][:], in_=table_words[:].bitcast(U32).indirect(entries(table_list, J_HALF, J_HALF))
         )
         nc.vector.tensor_copy(
-            out=ws_codes[:].bitcast(I32).rearrange("p (t u) -> p u t", t=PACK),
-            in_=ws_words_raw[:, PASS // 2 : PASS].rearrange("p (u t) -> p u t", t=PACK),
+            out=ws_codes[:].bitcast(I32).rearrange("p (t u w) -> p u t w", t=PACK, w=2),
+            in_=ws_words_raw[:, PASS // 2 : PASS].rearrange("p (u t w) -> p u t w", t=PACK, w=2),
         )
         nc.vector.tensor_copy(
-            out=ws_scale[:].bitcast(U16).rearrange("p (t u) -> p u t", t=PACK),
-            in_=ws_scales_raw[:].bitcast(U16)[:, PASS // 2 : PASS].rearrange("p (u t) -> p u t", t=PACK),
+            out=ws_scale[:].bitcast(I32).rearrange("p (t u) -> p u t", t=PACK),
+            in_=ws_scales_raw[:, PASS // 4 : PASS // 2].rearrange("p (u t) -> p u t", t=PACK),
         )
         ws_half = [
             (ws_words_raw[:].bitcast(U8)[:, 0 : 2 * PASS], ws_scales_raw[:].bitcast(U8)[:, 0:PASS]),
@@ -201,8 +201,8 @@ def tile_list_quadrature_magnitude_mel_kernel(
             b_square[unit] = held.tile([P, PASS], F32, name="b_square%d" % serial)
             if half == 0:
                 nc.scalar.activation(
-                    out=b_square[unit][:].rearrange("p (t u e) -> p t u e", t=PACK, e=2),
-                    in_=sums[:].rearrange("p (u t e) -> p t u e", t=PACK, e=2),
+                    out=b_square[unit][:].rearrange("p (t u e) -> p t u e", t=PACK, e=RUN),
+                    in_=sums[:].rearrange("p (u t e) -> p t u e", t=PACK, e=RUN),
                     func=ACT.Square,
                 )
             else:
@@ -243,8 +243,8 @@ def tile_list_quadrature_magnitude_mel_kernel(
             )
 
         def round_wc(g, half, engine, t0, t1):
-            src = wc_raw[g, PASS * half][:].rearrange("p i (u t e) -> p t u i e", t=PACK, e=2)
-            dst = w_rounded[g, half].rearrange("p (t u e i) -> p t u i e", t=PACK, e=2, i=PACK)
+            src = wc_raw[g, PASS * half][:].rearrange("p i (u t e) -> p t u i e", t=PACK, e=RUN)
+            dst = w_rounded[g, half].rearrange("p (t u e i) -> p t u i e", t=PACK, e=RUN, i=PACK)
             round_copy(engine, dst[:, t0:t1], src[:, t0:t1])
 
         def quantize_wc(g, half):
@@ -296,10 +296,10 @@ def tile_list_quadrature_magnitude_mel_kernel(
         load_wc(1, PASS, PASS, "plane1")
         gather_plane(2)
         wm_raw = buffer("plane2", [P, 2, PACK, N], F32)
-        wm_rows = wm.rearrange("(half u t e) n -> half e u t n", half=2, t=PACK, e=2)
+        wm_rows = wm.rearrange("(half u t e) n -> half e u t n", half=2, t=PACK, e=RUN)
         for half in range(2):
-            for e in range(2):
-                nc.sync.dma_start(out=wm_raw[e:P:2, half, :, :], in_=wm_rows[half, e])
+            for e in range(RUN):
+                nc.sync.dma_start(out=wm_raw[e:P:RUN, half, :, :], in_=wm_rows[half, e])
         with nc.allow_non_contiguous_dma(reason="band 128 c + p's bias goes to partition p, column c"):
             nc.sync.dma_start(out=bias[:], in_=bm.rearrange("(c p) -> p c", p=P))
         gather(3, 0, J_HALF)
@@ -310,9 +310,8 @@ def tile_list_quadrature_magnitude_mel_kernel(
         gather_plane(4)
         gather_plane(5)
         on_plane5 = buffer("plane5", [P, T], U32)
-        xg_codes[0, 0], xg_codes[0, 1] = on_plane5[:, 0:J_HALF], on_plane5[:, J_HALF:S]
+        xg_codes[0, 0] = on_plane5[:, 0:J_HALF]
         quantize_xg(0, 0, J_HALF)
-        quantize_xg(0, J_HALF, J_HALF)
         w_rounded[0, 0] = buffer("round_w0", [P, PASS * PACK], BF16)[:]
         round_wc(0, 0, "scalar", 0, PACK)
         gather_plane(6)
@@ -331,25 +330,26 @@ def tile_list_quadrature_magnitude_mel_kernel(
             xg_codes[1, j_half] = held.tile([P, J_HALF], U32, name="xg_codes1%d" % j_half, align_bytes=64)[:]
         quantize_wc(1, 0)
 
-        for j0 in (0, NARROW):
-            gather(7, j0, NARROW)
+        for j0, width in ((0, NARROW), (NARROW, NARROW), (WIDE, WIDE)):
+            gather(7, j0, width)
         for j0 in (0, NARROW):
             round_xg(1, j0, NARROW, "vector", "round_piece%d" % j0)
+        round_xg(1, WIDE, WIDE, "scalar", "round_piece%d" % WIDE)
         for j0 in (0, NARROW):
             quantize_xg(1, j0, NARROW)
-        for j0 in (WIDE, WIDE + NARROW):
-            gather(7, j0, NARROW)
-        for j0 in range(WIDE, S + WIDE, WIDE):
-            if j0 < S:
-                round_xg(1, j0, WIDE, "vector", "round_piece%d" % j0)
-            if j0 + WIDE < S:
-                gather(7, j0 + WIDE, WIDE)
-            if j0 < S:
-                quantize_xg(1, j0, WIDE)
+        xg_codes[0, 1] = shared.tile([P, J_HALF], U32, name="late_codes", tag="round_piece0", bufs=1, align_bytes=64)[:]
+        quantize_xg(0, J_HALF, J_HALF)
+        quantize_xg(1, WIDE, WIDE)
+        for j0 in (J_HALF, J_HALF + WIDE):
+            gather(7, j0, WIDE)
         on_table = buffer("table", [P, 2, PASS * PACK], BF16)
-        for g in range(2):
-            w_rounded[g, 1] = on_table[:, g, :]
-            round_wc(g, 1, "vector", 0, PACK)
+        w_rounded[0, 1], w_rounded[1, 1] = on_table[:, 0, :], on_table[:, 1, :]
+        round_xg(1, J_HALF, WIDE, "vector", "round_piece%d" % J_HALF)
+        round_xg(1, J_HALF + WIDE, WIDE, "vector", "round_w0")
+        quantize_xg(1, J_HALF, WIDE)
+        round_wc(0, 1, "vector", 0, PACK)
+        quantize_xg(1, J_HALF + WIDE, WIDE)
+        round_wc(1, 1, "vector", 0, PACK)
         for g in range(2):
             quantize_wc(g, 1)
 

@@ -24,19 +24,21 @@ ROW = 16
 RUN = 4
 J_HALF = S // 2
 BANKS = 8
-A_BANKS = 4
+EARLY_SUMS = 2
+EARLY_TURNED = BANKS - EARLY_SUMS
+A_BANK = [0, 1, 0, 1, 2, 0, 1, 2, 0, 1, 2, 0, 1, 0, 1, 0]
 
 UNITS = [(half, jt) for half in range(2) for jt in range(S // P)]
-TURNED = dict([((0, jt), A_BANKS + jt % A_BANKS) for jt in range(S // P)] + [((1, 6), 6), ((1, 7), 7)])
+TURNED = dict(zip(UNITS[:EARLY_TURNED], range(EARLY_SUMS, BANKS)))
 NARROW = 128
 WIDE = 256
 WC_SPLIT = 2
 OUT_PIECES = [
-    (0, 256, 4, "vector"),
-    (256, 256, 5, "vector"),
-    (512, 256, 4, "scalar"),
-    (768, 128, 5, "vector"),
-    (896, 128, 0, "vector"),
+    (0, 256, 5, "vector"),
+    (256, 256, 6, "scalar"),
+    (512, 256, 1, "scalar"),
+    (768, 128, 0, "vector"),
+    (896, 128, 7, "vector"),
 ]
 SQUARE_LAG, ADD_LAG, ROOT_LAG = 1, 2, 3
 WM_STEP = 8
@@ -103,20 +105,20 @@ def tile_list_quadrature_magnitude_mel_kernel(
         nc.sync.dma_start(frame_lists[:], offs2)
         load_scale_rows(table_scales, tab_scales[0])
         nc.sync.dma_start(out=table_words[:], in_=tab_words[0].rearrange("p t i -> p (t i)").bitcast(I32))
-        load_plane(0)
-        nc.sync.dma_start(out=weights[:, J_HALF:S], in_=wgt[:, J_HALF:S])
         nc.sync.dma_start(out=ws_words_raw[:], in_=ws_words[0].bitcast(I32))
         load_scale_rows(ws_scales_raw, ws_scales[0])
+        load_plane(0)
+        nc.sync.dma_start(out=weights[:, J_HALF:S], in_=wgt[:, J_HALF:S])
         for plane in range(1, 6):
             load_plane(plane)
-        load_wc(0, 0, PASS, "wc_a")
+        load_wc(1, 0, PASS, "wc_a")
         load_plane(6)
-        load_wc(1, 0, PASS, "wc_b")
+        load_wc(0, 0, PASS, "wc_b")
         load_plane(7)
 
         v_scales = held.tile([P, S], U8, name="v_scales", align_bytes=64)
-        ws_codes = held.tile([P, 2 * PASS], U8, name="ws_codes", align_bytes=64)
-        ws_scale = held.tile([P, PASS], U8, name="ws_scale", align_bytes=64)
+        ws_codes = held.tile([P, 2 * H], U8, name="ws_codes", align_bytes=64)
+        ws_scale = held.tile([P, H], U8, name="ws_scale", align_bytes=64)
         v_words = [held.tile([P, J_HALF], U32, name="v_words%d" % part, align_bytes=64) for part in range(2)]
 
         def entries(lists, j0, width):
@@ -128,17 +130,13 @@ def tile_list_quadrature_magnitude_mel_kernel(
             out=v_words[1][:], in_=table_words[:].bitcast(U32).indirect(entries(table_list, J_HALF, J_HALF))
         )
         nc.vector.tensor_copy(
-            out=ws_codes[:].bitcast(I32).rearrange("p (t u w) -> p u t w", t=PACK, w=2),
-            in_=ws_words_raw[:, PASS // 2 : PASS].rearrange("p (u t w) -> p u t w", t=PACK, w=2),
+            out=ws_codes[:].bitcast(I32).rearrange("p (half t u) -> p half u t", half=2, t=PACK),
+            in_=ws_words_raw[:].rearrange("p (half u t) -> p half u t", half=2, t=PACK),
         )
         nc.vector.tensor_copy(
-            out=ws_scale[:].bitcast(I32).rearrange("p (t u) -> p u t", t=PACK),
-            in_=ws_scales_raw[:, PASS // 4 : PASS // 2].rearrange("p (u t) -> p u t", t=PACK),
+            out=ws_scale[:].bitcast(U16).rearrange("p (half t u) -> p half u t", half=2, t=PACK),
+            in_=ws_scales_raw[:].bitcast(U16).rearrange("p (half u t) -> p half u t", half=2, t=PACK),
         )
-        ws_half = [
-            (ws_words_raw[:].bitcast(U8)[:, 0 : 2 * PASS], ws_scales_raw[:].bitcast(U8)[:, 0:PASS]),
-            (ws_codes[:], ws_scale[:]),
-        ]
 
         def product(unit, sums, passes, start, stop):
             groups = [slice(0, PASS)] if unit in TURNED else [slice(P * t, P * (t + 1)) for t in range(PACK)]
@@ -190,8 +188,8 @@ def tile_list_quadrature_magnitude_mel_kernel(
             sums = bank(serial % BANKS, [P, PASS])
             j_in_half = P * jt % J_HALF
             ws_pass = (
-                ws_half[half][0],
-                ws_half[half][1],
+                ws_codes[:, 2 * PASS * half : 2 * PASS * (half + 1)],
+                ws_scale[:, PASS * half : PASS * (half + 1)],
                 2,
                 FP4X4,
                 v_words[P * jt // J_HALF][:, j_in_half : j_in_half + P],
@@ -199,23 +197,18 @@ def tile_list_quadrature_magnitude_mel_kernel(
             )
             product(unit, sums, [ws_pass], start=True, stop=True)
             b_square[unit] = held.tile([P, PASS], F32, name="b_square%d" % serial)
-            if half == 0:
-                nc.scalar.activation(
-                    out=b_square[unit][:].rearrange("p (t u e) -> p t u e", t=PACK, e=RUN),
-                    in_=sums[:].rearrange("p (u t e) -> p t u e", t=PACK, e=RUN),
-                    func=ACT.Square,
-                )
-            else:
-                square(unit, b_square[unit], sums)
-        for unit in UNITS[:A_BANKS]:
+            square(unit, b_square[unit], sums)
+        for unit in UNITS[:EARLY_TURNED]:
             turn_b(unit)
 
         picked_planes, xg_rounded, w_rounded = {}, {}, {}
         xg_codes, wc_codes = {}, {}
-        xg_scales = held.tile([P, 2, S], U8, name="xg_scales", align_bytes=64)
-        wc_scales = held.tile([P, 2, H], U8, name="wc_scales", align_bytes=64)
+        xg_scales, wc_scales = {}, {}
         wm_codes = held.tile([P, 2, N], U32, name="wm_codes", align_bytes=64)
         wm_scales = held.tile([P, 2, N], U8, name="wm_scales", align_bytes=64)
+
+        def rounded(tag, width):
+            return buffer(tag, [P, width * PACK], BF16)
 
         def gather(plane, j0, width):
             g, i = divmod(plane, PACK)
@@ -226,31 +219,36 @@ def tile_list_quadrature_magnitude_mel_kernel(
         def gather_plane(plane):
             gather(plane, 0, S)
 
-        def round_xg(g, j0, width, engine, tag):
-            xg_rounded[g, j0] = buffer(tag, [P, width, PACK], BF16)
+        def round_xg(g, j0, width, engine, dst):
+            xg_rounded[g, j0] = dst
             src = picked_planes[g][:, :, j0 : j0 + width]
             round_copy(
                 engine,
-                xg_rounded[g, j0][:].rearrange("p (run d) i -> p run i d", d=RUN),
+                dst.rearrange("p (run d i) -> p run i d", d=RUN, i=PACK),
                 src.rearrange("p i (run d) -> p run i d", d=RUN),
             )
 
-        def quantize_xg(g, j0, width):
-            nc.vector.quantize_mx(
-                out=xg_codes[g, j0 // J_HALF][:, j0 % J_HALF : j0 % J_HALF + width].bitcast(FP8X4),
-                scales=xg_scales[:, g, j0 : j0 + width],
-                in_=xg_rounded[g, j0][:].rearrange("p j i -> p (j i)"),
-            )
+        def quantize_xg(g, j0, width, codes):
+            scales = held.tile([P, width], U8, name="xg_scales%d_%d" % (g, j0), align_bytes=64)
+            nc.vector.quantize_mx(out=codes.bitcast(FP8X4), scales=scales[:], in_=xg_rounded[g, j0])
+            for j in range(0, width, P):
+                xg_codes[g, (j0 + j) // P] = codes[:, j : j + P]
+                xg_scales[g, (j0 + j) // P] = scales[:, j : j + P]
+
+        def quantize_last(j0, width):
+            codes = held.tile([P, width], U32, name="xg_codes1_%d" % j0, align_bytes=64)
+            quantize_xg(1, j0, width, codes[:])
 
         def round_wc(g, half, engine, t0, t1):
-            src = wc_raw[g, PASS * half][:].rearrange("p i (u t e) -> p t u i e", t=PACK, e=RUN)
-            dst = w_rounded[g, half].rearrange("p (t u e i) -> p t u i e", t=PACK, e=RUN, i=PACK)
+            src = wc_raw[g, PASS * half][:].rearrange("p i (u t e) -> p t u i e", t=PACK, e=2)
+            dst = w_rounded[g, half].rearrange("p (t u e i) -> p t u i e", t=PACK, e=2, i=PACK)
             round_copy(engine, dst[:, t0:t1], src[:, t0:t1])
 
         def quantize_wc(g, half):
+            wc_scales[g, half] = held.tile([P, PASS], U8, name="wc_scales%d%d" % (g, half), align_bytes=64)[:]
             nc.vector.quantize_mx(
                 out=wc_codes[g, half].bitcast(FP8X4),
-                scales=wc_scales[:, g, PASS * half : PASS * (half + 1)],
+                scales=wc_scales[g, half],
                 in_=w_rounded[g, half],
             )
 
@@ -272,18 +270,9 @@ def tile_list_quadrature_magnitude_mel_kernel(
         def multiply_a(index, passes, start, stop):
             unit = half, jt = UNITS[index]
             if start:
-                a_sums[unit] = bank(index % A_BANKS, [P, PASS])
-            j_in_half = P * jt % J_HALF
+                a_sums[unit] = bank(A_BANK[index], [P, PASS])
             operands = [
-                (
-                    wc_codes[g, half],
-                    wc_scales[:, g, PASS * half : PASS * (half + 1)],
-                    1,
-                    FP8X4,
-                    xg_codes[g, P * jt // J_HALF][:, j_in_half : j_in_half + P],
-                    xg_scales[:, g, P * jt : P * (jt + 1)],
-                )
-                for g in passes
+                (wc_codes[g, half], wc_scales[g, half], 1, FP8X4, xg_codes[g, jt], xg_scales[g, jt]) for g in passes
             ]
             product(unit, a_sums[unit], operands, start, stop)
 
@@ -296,70 +285,70 @@ def tile_list_quadrature_magnitude_mel_kernel(
         load_wc(1, PASS, PASS, "plane1")
         gather_plane(2)
         wm_raw = buffer("plane2", [P, 2, PACK, N], F32)
-        wm_rows = wm.rearrange("(half u t e) n -> half e u t n", half=2, t=PACK, e=RUN)
+        wm_rows = wm.rearrange("(half u t e) n -> half e u t n", half=2, t=PACK, e=2)
         for half in range(2):
-            for e in range(RUN):
-                nc.sync.dma_start(out=wm_raw[e:P:RUN, half, :, :], in_=wm_rows[half, e])
+            for e in range(2):
+                nc.sync.dma_start(out=wm_raw[e:P:2, half, :, :], in_=wm_rows[half, e])
         with nc.allow_non_contiguous_dma(reason="band 128 c + p's bias goes to partition p, column c"):
             nc.sync.dma_start(out=bias[:], in_=bm.rearrange("(c p) -> p c", p=P))
         gather(3, 0, J_HALF)
-        round_xg(0, 0, J_HALF, "scalar", "round_x0")
+        round_xg(0, 0, J_HALF, "scalar", rounded("round_x0", J_HALF)[:])
         gather(3, J_HALF, J_HALF)
-        round_xg(0, J_HALF, J_HALF, "scalar", "round_x1")
+        round_xg(0, J_HALF, J_HALF, "scalar", rounded("round_x1", J_HALF)[:])
 
         gather_plane(4)
         gather_plane(5)
-        on_plane5 = buffer("plane5", [P, T], U32)
-        xg_codes[0, 0] = on_plane5[:, 0:J_HALF]
-        quantize_xg(0, 0, J_HALF)
-        w_rounded[0, 0] = buffer("round_w0", [P, PASS * PACK], BF16)[:]
-        round_wc(0, 0, "scalar", 0, PACK)
+        on_plane5 = buffer("plane5", [P, S], U32)
+        for j0 in (0, J_HALF):
+            quantize_xg(0, j0, J_HALF, on_plane5[:, j0 : j0 + J_HALF])
+        w_rounded[1, 0] = buffer("round_w0", [P, PASS * PACK], BF16)[:]
+        round_wc(1, 0, "scalar", 0, PACK)
         gather_plane(6)
-        on_plane6 = buffer("plane6", [P, T], U32)
-        wc_codes[0, 0] = on_plane6[:, 0:PASS]
-        h_codes = [on_plane5[:, S:T], on_plane6[:, S:T]]
-        quantize_wc(0, 0)
-        w_rounded[1, 0] = buffer("round_w1", [P, PASS * PACK], BF16)[:]
-        round_wc(1, 0, "scalar", 0, WC_SPLIT)
-        round_wc(1, 0, "vector", WC_SPLIT, PACK)
-        for index in range(A_BANKS):
-            multiply_a(index, [0], start=True, stop=False)
-        for g, half in ((1, 0), (0, 1), (1, 1)):
-            wc_codes[g, half] = held.tile([P, PASS], U32, name="wc_codes%d%d" % (g, half), align_bytes=64)[:]
-        for j_half in range(2):
-            xg_codes[1, j_half] = held.tile([P, J_HALF], U32, name="xg_codes1%d" % j_half, align_bytes=64)[:]
+        wc_codes[1, 0] = buffer("plane6", [P, PASS], U32)[:]
         quantize_wc(1, 0)
+        w_rounded[0, 0] = buffer("round_w1", [P, PASS * PACK], BF16)[:]
+        round_wc(0, 0, "scalar", 0, WC_SPLIT)
+        round_wc(0, 0, "vector", WC_SPLIT, PACK)
+        for g, half in ((0, 0), (0, 1), (1, 1)):
+            wc_codes[g, half] = held.tile([P, PASS], U32, name="wc_codes%d%d" % (g, half), align_bytes=64)[:]
+        quantize_wc(0, 0)
+        for index in range(EARLY_SUMS):
+            multiply_a(index, [0], start=True, stop=False)
 
-        for j0, width in ((0, NARROW), (NARROW, NARROW), (WIDE, WIDE)):
-            gather(7, j0, width)
+        gather(7, 0, NARROW)
+        gather(7, NARROW, WIDE)
         for j0 in (0, NARROW):
-            round_xg(1, j0, NARROW, "vector", "round_piece%d" % j0)
-        round_xg(1, WIDE, WIDE, "scalar", "round_piece%d" % WIDE)
-        for j0 in (0, NARROW):
-            quantize_xg(1, j0, NARROW)
-        xg_codes[0, 1] = shared.tile([P, J_HALF], U32, name="late_codes", tag="round_piece0", bufs=1, align_bytes=64)[:]
-        quantize_xg(0, J_HALF, J_HALF)
-        quantize_xg(1, WIDE, WIDE)
+            round_xg(1, j0, NARROW, "vector", rounded("round_piece%d" % j0, NARROW)[:])
+        round_xg(1, WIDE, NARROW, "scalar", rounded("round_piece%d" % WIDE, NARROW)[:])
+        quantize_last(0, NARROW)
+        gather(7, WIDE + NARROW, NARROW)
+        round_xg(1, WIDE + NARROW, NARROW, "vector", rounded("round_x0", NARROW)[:])
+        for j0 in (NARROW, WIDE, WIDE + NARROW):
+            quantize_last(j0, NARROW)
         for j0 in (J_HALF, J_HALF + WIDE):
             gather(7, j0, WIDE)
         on_table = buffer("table", [P, 2, PASS * PACK], BF16)
         w_rounded[0, 1], w_rounded[1, 1] = on_table[:, 0, :], on_table[:, 1, :]
-        round_xg(1, J_HALF, WIDE, "vector", "round_piece%d" % J_HALF)
-        round_xg(1, J_HALF + WIDE, WIDE, "vector", "round_w0")
-        quantize_xg(1, J_HALF, WIDE)
+        late = rounded("round_x1", J_HALF)
+        round_xg(1, J_HALF, WIDE, "vector", late[:, 0 : PACK * WIDE])
+        round_xg(1, J_HALF + WIDE, WIDE, "vector", late[:, PACK * WIDE : PACK * J_HALF])
+        quantize_last(J_HALF, WIDE)
         round_wc(0, 1, "vector", 0, PACK)
-        quantize_xg(1, J_HALF + WIDE, WIDE)
+        quantize_last(J_HALF + WIDE, WIDE)
         round_wc(1, 1, "vector", 0, PACK)
         for g in range(2):
             quantize_wc(g, 1)
 
         h_rounded = [buffer(tag, [P, S * PACK], BF16) for tag in ("plane3", "plane4")]
-        h_scales = held.tile([P, 2, S], U8, name="h_scales", align_bytes=64)
+        h_codes, h_scales = {}, {}
         results = buffer("plane7", [P, N // P * S], F32)
         mel_sums = {}
 
         def square_a(unit):
-            a_square[unit] = shared.tile([P, PASS], F32, name="a_square", tag="a_square", bufs=4)
+            if unit in (UNITS[0], UNITS[2]):
+                a_square[unit] = buffer("first_square", [P, PASS], F32)
+            else:
+                a_square[unit] = shared.tile([P, PASS], F32, name="a_square", tag="a_square", bufs=4)
             square(unit, a_square[unit], a_sums[unit])
 
         def add_squares(unit):
@@ -381,25 +370,29 @@ def tile_list_quadrature_magnitude_mel_kernel(
                 nc.scalar.activation(out=dst, in_=b_square[unit][:], func=ACT.Sqrt)
 
         def quantize_h(half, j0, width):
+            codes = held.tile([P, width], U32, name="h_codes%d_%d" % (half, j0), align_bytes=64)
+            scales = held.tile([P, width], U8, name="h_scales%d_%d" % (half, j0), align_bytes=64)
             nc.vector.quantize_mx(
-                out=h_codes[half][:, j0 : j0 + width].bitcast(FP8X4),
-                scales=h_scales[:, half, j0 : j0 + width],
+                out=codes[:].bitcast(FP8X4),
+                scales=scales[:],
                 in_=h_rounded[half][:, PACK * j0 : PACK * (j0 + width)],
             )
+            for j in range(0, width, P):
+                h_codes[half, j0 + j], h_scales[half, j0 + j] = codes[:, j:width], scales[:, j:width]
 
-        def multiply_mel(j0, width, number):
-            mel_sums[j0] = bank(number, [P, N // P, width])
+        def multiply_mel(j0, width, number, half):
+            if half == 0:
+                mel_sums[j0] = bank(number, [P, N // P, width])
             for c in range(N // P):
-                for half in (1, 0):
-                    nc.tensor.matmul_mx(
-                        out=mel_sums[j0][:, c, :],
-                        lhsT=wm_codes[:, half, P * c : P * (c + 1)].bitcast(FP8X4),
-                        lhsT_scale=wm_scales[:, half, P * c : P * (c + 1)],
-                        rhs=h_codes[half][:, j0 : j0 + width].bitcast(FP8X4),
-                        rhs_scale=h_scales[:, half, j0 : j0 + width],
-                        start=half == 1,
-                        stop=half == 0,
-                    )
+                nc.tensor.matmul_mx(
+                    out=mel_sums[j0][:, c, :],
+                    lhsT=wm_codes[:, half, P * c : P * (c + 1)].bitcast(FP8X4),
+                    lhsT_scale=wm_scales[:, half, P * c : P * (c + 1)],
+                    rhs=h_codes[half, j0][:, 0:width].bitcast(FP8X4),
+                    rhs_scale=h_scales[half, j0][:, 0:width],
+                    start=half == 0 and c == 0,
+                    stop=half == 1 and c == N // P - 1,
+                )
 
         def store(j0, width, engine):
             result = results[:, N // P * j0 : N // P * (j0 + width)].rearrange("p (c j) -> p c j", j=width)
@@ -415,30 +408,30 @@ def tile_list_quadrature_magnitude_mel_kernel(
 
         mel_step = {j0: S // P + (j0 + width) // P + ROOT_LAG for j0, width, number, engine in OUT_PIECES}
         last_step = max(mel_step.values())
-        store_step = {j0: step + 1 if step < len(UNITS) else last_step + 1 for j0, step in mel_step.items()}
+        store_step = {j0: step + 1 if j0 == 0 else last_step + 1 for j0, step in mel_step.items()}
+        open_step = {j0: min(step, len(UNITS) + 1) for j0, step in mel_step.items()}
+        open_step[S - NARROW] = last_step
         for step in range(last_step + 2):
             if step == WM_STEP:
                 prepare_wm()
             for j0 in (0, J_HALF):
                 if step == (j0 + J_HALF) // P + ROOT_LAG:
                     quantize_h(0, j0, J_HALF)
-            if step == S // P + ROOT_LAG:
-                for unit in UNITS[-2:]:
-                    turn_b(unit)
             for j0, width, number, engine in OUT_PIECES:
+                if step == open_step[j0]:
+                    multiply_mel(j0, width, number, 0)
                 if step == mel_step[j0]:
                     quantize_h(1, j0, width)
-                    multiply_mel(j0, width, number)
+                    multiply_mel(j0, width, number, 1)
                 if step == store_step[j0]:
                     store(j0, width, engine)
-            if step < S // P:
+            if 0 <= step - ADD_LAG < len(UNITS):
+                add_squares(UNITS[step - ADD_LAG])
+            if step < EARLY_SUMS:
                 multiply_a(step, [1], start=False, stop=True)
             elif step < len(UNITS):
-                multiply_a(step, [1, 0], start=True, stop=True)
-            if A_BANKS <= step - 1 < S // P:
-                turn_b(UNITS[step - 1])
-            for lag, stage in ((SQUARE_LAG, square_a), (ADD_LAG, add_squares), (ROOT_LAG, root)):
+                multiply_a(step, [0, 1], start=True, stop=True)
+            stages = [(SQUARE_LAG, square_a), (ROOT_LAG, root)]
+            for lag, stage in reversed(stages) if step == ROOT_LAG else stages:
                 if 0 <= step - lag < len(UNITS):
                     stage(UNITS[step - lag])
-            if 0 <= step - SQUARE_LAG < S // P - A_BANKS:
-                multiply_a(step - SQUARE_LAG + A_BANKS, [0], start=True, stop=False)

@@ -29,10 +29,10 @@ EARLY_TURNED = BANKS - EARLY_SUMS
 A_BANK = [0, 1, 0, 1, 2, 0, 1, 2, 0, 1, 2, 0, 1, 0, 1, 0]
 
 UNITS = [(half, jt) for half in range(2) for jt in range(S // P)]
-TURNED = dict(zip(UNITS[:EARLY_TURNED], range(EARLY_SUMS, BANKS)))
+LATE_TURNED, LATE_BANK = 10, 3
+TURNED = dict(list(zip(UNITS[:EARLY_TURNED], range(EARLY_SUMS, BANKS))) + [(UNITS[LATE_TURNED], LATE_BANK)])
 NARROW = 128
 WIDE = 256
-WC_SPLIT = 2
 OUT_PIECES = [
     (0, 256, 5, "vector"),
     (256, 256, 6, "scalar"),
@@ -96,25 +96,42 @@ def tile_list_quadrature_magnitude_mel_kernel(
         nc.vector.memset(warm_in[:], 1.0)
         nc.scalar.activation(out=warm_out[:], in_=warm_in[:], func=ACT.Sqrt)
 
-        nc.gpsimd.memset(table_scales[:], 0)
+        group_rows = buffer("picked1", [P, S], F32)
+        nc.gpsimd.memset(group_rows[:], 0.0)
+        nc.vector.memset(table_scales[:], 0)
         nc.vector.memset(ws_scales_raw[:], 0)
         make_identity(nc, identity[:])
 
         nc.sync.dma_start(table_list[:], offs)
-        nc.sync.dma_start(out=weights[:, 0:J_HALF], in_=wgt[:, 0:J_HALF])
-        nc.sync.dma_start(frame_lists[:], offs2)
-        load_scale_rows(table_scales, tab_scales[0])
-        nc.sync.dma_start(out=table_words[:], in_=tab_words[0].rearrange("p t i -> p (t i)").bitcast(I32))
         nc.sync.dma_start(out=ws_words_raw[:], in_=ws_words[0].bitcast(I32))
+        load_scale_rows(table_scales, tab_scales[0])
+        nc.sync.dma_start(out=group_rows[0:P:ROW, :], in_=wgt[0:P:ROW, :])
+        nc.sync.dma_start(out=table_words[:], in_=tab_words[0].rearrange("p t i -> p (t i)").bitcast(I32))
+        nc.sync.dma_start(frame_lists[:], offs2)
         load_scale_rows(ws_scales_raw, ws_scales[0])
-        load_plane(0)
-        nc.sync.dma_start(out=weights[:, J_HALF:S], in_=wgt[:, J_HALF:S])
-        for plane in range(1, 6):
+        for plane in range(6):
             load_plane(plane)
         load_wc(1, 0, PASS, "wc_a")
         load_plane(6)
         load_wc(0, 0, PASS, "wc_b")
         load_plane(7)
+
+        repeated = buffer("round_x0", [P, S], F32)
+        for part in range(2):
+            turned = bank(4 + part, [P, J_HALF])
+            for j0 in range(0, J_HALF, P):
+                j = J_HALF * part + j0
+                nc.tensor.transpose(turned[:, j0 : j0 + P], group_rows[:, j : j + P], identity[:])
+            nc.scalar.copy(
+                out=repeated[:, J_HALF * part : J_HALF * (part + 1)].rearrange("p (column x) -> p column x", x=ROW),
+                in_=turned[:, 0:J_HALF:ROW].unsqueeze(2).to_broadcast([P, J_HALF // ROW, ROW]),
+            )
+        for part in range(2):
+            turned = bank(6 + part, [P, J_HALF])
+            for j0 in range(0, J_HALF, P):
+                j = J_HALF * part + j0
+                nc.tensor.transpose(turned[:, j0 : j0 + P], repeated[:, j : j + P], identity[:])
+            nc.scalar.copy(out=weights[:, J_HALF * part : J_HALF * (part + 1)], in_=turned[:])
 
         v_scales = held.tile([P, S], U8, name="v_scales", align_bytes=64)
         ws_codes = held.tile([P, 2 * H], U8, name="ws_codes", align_bytes=64)
@@ -277,7 +294,7 @@ def tile_list_quadrature_magnitude_mel_kernel(
             product(unit, a_sums[unit], operands, start, stop)
 
         for g in range(2):
-            picked_planes[g] = held.tile([P, PACK, S], F32, name="picked%d" % g)
+            picked_planes[g] = buffer("picked%d" % g, [P, PACK, S], F32)
         gather(0, 0, J_HALF)
         gather(0, J_HALF, J_HALF)
         load_wc(0, PASS, PASS, "plane0")
@@ -298,17 +315,14 @@ def tile_list_quadrature_magnitude_mel_kernel(
 
         gather_plane(4)
         gather_plane(5)
-        on_plane5 = buffer("plane5", [P, S], U32)
-        for j0 in (0, J_HALF):
-            quantize_xg(0, j0, J_HALF, on_plane5[:, j0 : j0 + J_HALF])
+        quantize_xg(0, 0, J_HALF, held.tile([P, J_HALF], U32, name="xg_codes0", align_bytes=64)[:])
         w_rounded[1, 0] = buffer("round_w0", [P, PASS * PACK], BF16)[:]
         round_wc(1, 0, "scalar", 0, PACK)
         gather_plane(6)
         wc_codes[1, 0] = buffer("plane6", [P, PASS], U32)[:]
         quantize_wc(1, 0)
         w_rounded[0, 0] = buffer("round_w1", [P, PASS * PACK], BF16)[:]
-        round_wc(0, 0, "scalar", 0, WC_SPLIT)
-        round_wc(0, 0, "vector", WC_SPLIT, PACK)
+        round_wc(0, 0, "scalar", 0, PACK)
         for g, half in ((0, 0), (0, 1), (1, 1)):
             wc_codes[g, half] = held.tile([P, PASS], U32, name="wc_codes%d%d" % (g, half), align_bytes=64)[:]
         quantize_wc(0, 0)
@@ -329,7 +343,8 @@ def tile_list_quadrature_magnitude_mel_kernel(
             gather(7, j0, WIDE)
         on_table = buffer("table", [P, 2, PASS * PACK], BF16)
         w_rounded[0, 1], w_rounded[1, 1] = on_table[:, 0, :], on_table[:, 1, :]
-        late = rounded("round_x1", J_HALF)
+        quantize_xg(0, J_HALF, J_HALF, buffer("round_piece0", [P, J_HALF], U32)[:])
+        late = rounded("round_w0", J_HALF)
         round_xg(1, J_HALF, WIDE, "vector", late[:, 0 : PACK * WIDE])
         round_xg(1, J_HALF + WIDE, WIDE, "vector", late[:, PACK * WIDE : PACK * J_HALF])
         quantize_last(J_HALF, WIDE)
@@ -345,10 +360,7 @@ def tile_list_quadrature_magnitude_mel_kernel(
         mel_sums = {}
 
         def square_a(unit):
-            if unit in (UNITS[0], UNITS[2]):
-                a_square[unit] = buffer("first_square", [P, PASS], F32)
-            else:
-                a_square[unit] = shared.tile([P, PASS], F32, name="a_square", tag="a_square", bufs=4)
+            a_square[unit] = shared.tile([P, PASS], F32, name="a_square", tag="a_square", bufs=4)
             square(unit, a_square[unit], a_sums[unit])
 
         def add_squares(unit):
@@ -425,13 +437,14 @@ def tile_list_quadrature_magnitude_mel_kernel(
                     multiply_mel(j0, width, number, 1)
                 if step == store_step[j0]:
                     store(j0, width, engine)
+            if step == LATE_TURNED:
+                turn_b(UNITS[LATE_TURNED])
             if 0 <= step - ADD_LAG < len(UNITS):
                 add_squares(UNITS[step - ADD_LAG])
             if step < EARLY_SUMS:
                 multiply_a(step, [1], start=False, stop=True)
             elif step < len(UNITS):
                 multiply_a(step, [0, 1], start=True, stop=True)
-            stages = [(SQUARE_LAG, square_a), (ROOT_LAG, root)]
-            for lag, stage in reversed(stages) if step == ROOT_LAG else stages:
+            for lag, stage in ((SQUARE_LAG, square_a), (ROOT_LAG, root)):
                 if 0 <= step - lag < len(UNITS):
                     stage(UNITS[step - lag])

@@ -29,10 +29,11 @@ EARLY_TURNED = BANKS - EARLY_SUMS
 A_BANK = [0, 1, 0, 1, 2, 0, 1, 2, 0, 1, 2, 0, 1, 0, 1, 0]
 
 UNITS = [(half, jt) for half in range(2) for jt in range(S // P)]
-LATE_TURNED, LATE_BANK = 10, 3
-TURNED = dict(list(zip(UNITS[:EARLY_TURNED], range(EARLY_SUMS, BANKS))) + [(UNITS[LATE_TURNED], LATE_BANK)])
+LATE_TURNED = {6: 3, 10: 4}
+TURNED = dict(list(zip(UNITS[:EARLY_TURNED], range(EARLY_SUMS, BANKS))) + [(UNITS[i], b) for i, b in LATE_TURNED.items()])
 NARROW = 128
 WIDE = 256
+WC_SPLIT = 2
 OUT_PIECES = [
     (0, 256, 5, "vector"),
     (256, 256, 6, "scalar"),
@@ -41,7 +42,7 @@ OUT_PIECES = [
     (896, 128, 7, "vector"),
 ]
 SQUARE_LAG, ADD_LAG, ROOT_LAG = 1, 2, 3
-WM_STEP = 8
+WM_BEHIND = (6, 7)
 
 
 def tile_list_quadrature_magnitude_mel_kernel(
@@ -97,8 +98,8 @@ def tile_list_quadrature_magnitude_mel_kernel(
         nc.scalar.activation(out=warm_out[:], in_=warm_in[:], func=ACT.Sqrt)
 
         group_rows = buffer("picked1", [P, S], F32)
-        nc.gpsimd.memset(group_rows[:], 0.0)
-        nc.vector.memset(table_scales[:], 0)
+        nc.gpsimd.memset(table_scales[:], 0)
+        nc.vector.memset(group_rows[:], 0.0)
         nc.vector.memset(ws_scales_raw[:], 0)
         make_identity(nc, identity[:])
 
@@ -204,17 +205,26 @@ def tile_list_quadrature_magnitude_mel_kernel(
             half, jt = unit
             sums = bank(serial % BANKS, [P, PASS])
             j_in_half = P * jt % J_HALF
+            as_loaded = unit in UNITS[:EARLY_TURNED]
+            codes, scales = (ws_words_raw[:].bitcast(U8), ws_scales_raw[:].bitcast(U8)) if as_loaded else (ws_codes, ws_scale)
             ws_pass = (
-                ws_codes[:, 2 * PASS * half : 2 * PASS * (half + 1)],
-                ws_scale[:, PASS * half : PASS * (half + 1)],
+                codes[:, 2 * PASS * half : 2 * PASS * (half + 1)],
+                scales[:, PASS * half : PASS * (half + 1)],
                 2,
                 FP4X4,
                 v_words[P * jt // J_HALF][:, j_in_half : j_in_half + P],
                 v_scales[:, P * jt : P * (jt + 1)],
             )
             product(unit, sums, [ws_pass], start=True, stop=True)
-            b_square[unit] = held.tile([P, PASS], F32, name="b_square%d" % serial)
-            square(unit, b_square[unit], sums)
+            b_square[unit] = buffer("b_square%d%d" % unit, [P, PASS], F32)
+            if as_loaded:
+                nc.scalar.activation(
+                    out=b_square[unit][:].rearrange("p (t u e) -> p t u e", t=PACK, e=2),
+                    in_=sums[:].rearrange("p (u t e) -> p t u e", t=PACK, e=2),
+                    func=ACT.Square,
+                )
+            else:
+                square(unit, b_square[unit], sums)
         for unit in UNITS[:EARLY_TURNED]:
             turn_b(unit)
 
@@ -269,18 +279,13 @@ def tile_list_quadrature_magnitude_mel_kernel(
                 in_=w_rounded[g, half],
             )
 
-        def prepare_wm():
-            wm_rounded = buffer("wc_a", [P, 2, N * PACK], BF16)
-            for half in range(2):
-                nc.vector.tensor_copy(
-                    out=wm_rounded[:, half, :].rearrange("p (run d t) -> p run t d", d=RUN, t=PACK),
-                    in_=wm_raw[:, half, :, :].rearrange("p t (run d) -> p run t d", d=RUN),
-                )
-            nc.vector.quantize_mx(
-                out=wm_codes[:].rearrange("p half n -> p (half n)").bitcast(FP8X4),
-                scales=wm_scales[:].rearrange("p half n -> p (half n)"),
-                in_=wm_rounded[:].rearrange("p half x -> p (half x)"),
+        def prepare_wm(half, tag):
+            wm_rounded = buffer(tag, [P, N * PACK], BF16)
+            nc.vector.tensor_copy(
+                out=wm_rounded[:].rearrange("p (run d t) -> p run t d", d=RUN, t=PACK),
+                in_=wm_raw[:, half, :, :].rearrange("p t (run d) -> p run t d", d=RUN),
             )
+            nc.vector.quantize_mx(out=wm_codes[:, half, :].bitcast(FP8X4), scales=wm_scales[:, half, :], in_=wm_rounded[:])
 
         a_sums, a_square = {}, {}
 
@@ -322,7 +327,8 @@ def tile_list_quadrature_magnitude_mel_kernel(
         wc_codes[1, 0] = buffer("plane6", [P, PASS], U32)[:]
         quantize_wc(1, 0)
         w_rounded[0, 0] = buffer("round_w1", [P, PASS * PACK], BF16)[:]
-        round_wc(0, 0, "scalar", 0, PACK)
+        round_wc(0, 0, "scalar", 0, WC_SPLIT)
+        round_wc(0, 0, "vector", WC_SPLIT, PACK)
         for g, half in ((0, 0), (0, 1), (1, 1)):
             wc_codes[g, half] = held.tile([P, PASS], U32, name="wc_codes%d%d" % (g, half), align_bytes=64)[:]
         quantize_wc(0, 0)
@@ -424,8 +430,9 @@ def tile_list_quadrature_magnitude_mel_kernel(
         open_step = {j0: min(step, len(UNITS) + 1) for j0, step in mel_step.items()}
         open_step[S - NARROW] = last_step
         for step in range(last_step + 2):
-            if step == WM_STEP:
-                prepare_wm()
+            for half, index in enumerate(WM_BEHIND):
+                if step == index + ROOT_LAG + 1:
+                    prepare_wm(half, "b_square%d%d" % UNITS[index])
             for j0 in (0, J_HALF):
                 if step == (j0 + J_HALF) // P + ROOT_LAG:
                     quantize_h(0, j0, J_HALF)
@@ -437,8 +444,8 @@ def tile_list_quadrature_magnitude_mel_kernel(
                     multiply_mel(j0, width, number, 1)
                 if step == store_step[j0]:
                     store(j0, width, engine)
-            if step == LATE_TURNED:
-                turn_b(UNITS[LATE_TURNED])
+            if step in LATE_TURNED:
+                turn_b(UNITS[step])
             if 0 <= step - ADD_LAG < len(UNITS):
                 add_squares(UNITS[step - ADD_LAG])
             if step < EARLY_SUMS:

@@ -24,19 +24,19 @@ ROW = 16
 RUN = 4
 J_HALF = S // 2
 BANKS = 8
-EARLY_SUMS = 2
+EARLY_SUMS = 3
 EARLY_TURNED = BANKS - EARLY_SUMS
-A_BANK = [0, 1, 0, 1, 2, 0, 1, 2, 0, 1, 2, 0, 1, 0, 1, 0]
+A_BANK = [index % 3 for index in range(12)] + [1, 0] * 2
 
 UNITS = [(half, jt) for half in range(2) for jt in range(S // P)]
-LATE_TURNED = {6: 3, 10: 4}
+LATE_TURNED = {5: 3, 10: 4}
 TURNED = dict(list(zip(UNITS[:EARLY_TURNED], range(EARLY_SUMS, BANKS))) + [(UNITS[i], b) for i, b in LATE_TURNED.items()])
 NARROW = 128
 WIDE = 256
 WC_SPLIT = 2
 OUT_PIECES = [
     (0, 256, 5, "vector"),
-    (256, 256, 6, "scalar"),
+    (256, 256, 6, "vector"),
     (512, 256, 1, "scalar"),
     (768, 128, 0, "vector"),
     (896, 128, 7, "vector"),
@@ -349,11 +349,11 @@ def tile_list_quadrature_magnitude_mel_kernel(
             gather(7, j0, WIDE)
         on_table = buffer("table", [P, 2, PASS * PACK], BF16)
         w_rounded[0, 1], w_rounded[1, 1] = on_table[:, 0, :], on_table[:, 1, :]
-        quantize_xg(0, J_HALF, J_HALF, buffer("round_piece0", [P, J_HALF], U32)[:])
         late = rounded("round_w0", J_HALF)
         round_xg(1, J_HALF, WIDE, "vector", late[:, 0 : PACK * WIDE])
-        round_xg(1, J_HALF + WIDE, WIDE, "vector", late[:, PACK * WIDE : PACK * J_HALF])
+        quantize_xg(0, J_HALF, J_HALF, buffer("round_piece0", [P, J_HALF], U32)[:])
         quantize_last(J_HALF, WIDE)
+        round_xg(1, J_HALF + WIDE, WIDE, "vector", late[:, PACK * WIDE : PACK * J_HALF])
         round_wc(0, 1, "vector", 0, PACK)
         quantize_last(J_HALF + WIDE, WIDE)
         round_wc(1, 1, "vector", 0, PACK)
@@ -366,7 +366,10 @@ def tile_list_quadrature_magnitude_mel_kernel(
         mel_sums = {}
 
         def square_a(unit):
-            a_square[unit] = shared.tile([P, PASS], F32, name="a_square", tag="a_square", bufs=4)
+            if unit == UNITS[-1]:
+                a_square[unit] = buffer("last_square", [P, PASS], F32)
+            else:
+                a_square[unit] = shared.tile([P, PASS], F32, name="a_square", tag="a_square", bufs=4)
             square(unit, a_square[unit], a_sums[unit])
 
         def add_squares(unit):
@@ -413,7 +416,10 @@ def tile_list_quadrature_magnitude_mel_kernel(
                 )
 
         def store(j0, width, engine):
-            result = results[:, N // P * j0 : N // P * (j0 + width)].rearrange("p (c j) -> p c j", j=width)
+            if j0 == WIDE:
+                result = buffer("last_square", [P, N // P, width], F32)[:]
+            else:
+                result = results[:, N // P * j0 : N // P * (j0 + width)].rearrange("p (c j) -> p c j", j=width)
             if engine == "vector":
                 spread = bias[:].unsqueeze(2).to_broadcast([P, N // P, width])
                 nc.vector.tensor_tensor(result, mel_sums[j0][:], spread, ALU.add)
@@ -427,6 +433,7 @@ def tile_list_quadrature_magnitude_mel_kernel(
         mel_step = {j0: S // P + (j0 + width) // P + ROOT_LAG for j0, width, number, engine in OUT_PIECES}
         last_step = max(mel_step.values())
         store_step = {j0: step + 1 if j0 == 0 else last_step + 1 for j0, step in mel_step.items()}
+        store_step[WIDE] = len(UNITS) + ADD_LAG
         open_step = {j0: min(step, len(UNITS) + 1) for j0, step in mel_step.items()}
         open_step[S - NARROW] = last_step
         for step in range(last_step + 2):

@@ -21,7 +21,7 @@ P = 128
 PACK = 4
 PASS = P * PACK
 ROW = 16
-RUN = 4
+RUN = 2
 J_HALF = S // 2
 BANKS = 8
 EARLY_SUMS = 3

@@ -24,13 +24,14 @@ ROW = 16
 RUN = 2
 J_HALF = S // 2
 BANKS = 8
-EARLY_SUMS = 3
-EARLY_TURNED = BANKS - EARLY_SUMS
-A_BANK = [index % 3 for index in range(12)] + [1, 0] * 2
+A_BANKS = 3
+EARLY_TURNED = BANKS - A_BANKS
 
 UNITS = [(half, jt) for half in range(2) for jt in range(S // P)]
-LATE_TURNED = {5: 3, 10: 4}
-TURNED = dict(list(zip(UNITS[:EARLY_TURNED], range(EARLY_SUMS, BANKS))) + [(UNITS[i], b) for i, b in LATE_TURNED.items()])
+LAST_UNITS = 4
+A_BANK = [index % A_BANKS for index in range(len(UNITS) - LAST_UNITS)] + [1, 0] * (LAST_UNITS // 2)
+LATE_TURNED = {EARLY_TURNED: A_BANKS, 10: A_BANKS + 1}
+TURNED = dict(list(zip(UNITS[:EARLY_TURNED], range(A_BANKS, BANKS))) + [(UNITS[i], b) for i, b in LATE_TURNED.items()])
 NARROW = 128
 WIDE = 256
 WC_SPLIT = 2
@@ -42,7 +43,9 @@ OUT_PIECES = [
     (896, 128, 7, "vector"),
 ]
 SQUARE_LAG, ADD_LAG, ROOT_LAG = 1, 2, 3
-WM_BEHIND = (6, 7)
+SQUARE_BUFFERS = 4
+FIRST_DIRECT = EARLY_TURNED + 1
+WM_BEHIND = (FIRST_DIRECT + 1, FIRST_DIRECT + 2)
 
 
 def tile_list_quadrature_magnitude_mel_kernel(
@@ -205,7 +208,7 @@ def tile_list_quadrature_magnitude_mel_kernel(
             half, jt = unit
             sums = bank(serial % BANKS, [P, PASS])
             j_in_half = P * jt % J_HALF
-            as_loaded = unit in UNITS[:EARLY_TURNED]
+            as_loaded = unit in TURNED
             codes, scales = (ws_words_raw[:].bitcast(U8), ws_scales_raw[:].bitcast(U8)) if as_loaded else (ws_codes, ws_scale)
             ws_pass = (
                 codes[:, 2 * PASS * half : 2 * PASS * (half + 1)],
@@ -332,7 +335,7 @@ def tile_list_quadrature_magnitude_mel_kernel(
         for g, half in ((0, 0), (0, 1), (1, 1)):
             wc_codes[g, half] = held.tile([P, PASS], U32, name="wc_codes%d%d" % (g, half), align_bytes=64)[:]
         quantize_wc(0, 0)
-        for index in range(EARLY_SUMS):
+        for index in range(A_BANKS):
             multiply_a(index, [0], start=True, stop=False)
 
         gather(7, 0, NARROW)
@@ -369,7 +372,7 @@ def tile_list_quadrature_magnitude_mel_kernel(
             if unit == UNITS[-1]:
                 a_square[unit] = buffer("last_square", [P, PASS], F32)
             else:
-                a_square[unit] = shared.tile([P, PASS], F32, name="a_square", tag="a_square", bufs=4)
+                a_square[unit] = shared.tile([P, PASS], F32, name="a_square", tag="a_square", bufs=SQUARE_BUFFERS)
             square(unit, a_square[unit], a_sums[unit])
 
         def add_squares(unit):
@@ -391,7 +394,10 @@ def tile_list_quadrature_magnitude_mel_kernel(
                 nc.scalar.activation(out=dst, in_=b_square[unit][:], func=ACT.Sqrt)
 
         def quantize_h(half, j0, width):
-            codes = held.tile([P, width], U32, name="h_codes%d_%d" % (half, j0), align_bytes=64)
+            if (half, j0) == (0, 0):
+                codes = buffer("b_square%d%d" % UNITS[FIRST_DIRECT], [P, width], U32)
+            else:
+                codes = held.tile([P, width], U32, name="h_codes%d_%d" % (half, j0), align_bytes=64)
             scales = held.tile([P, width], U8, name="h_scales%d_%d" % (half, j0), align_bytes=64)
             nc.vector.quantize_mx(
                 out=codes[:].bitcast(FP8X4),
@@ -432,16 +438,17 @@ def tile_list_quadrature_magnitude_mel_kernel(
 
         mel_step = {j0: S // P + (j0 + width) // P + ROOT_LAG for j0, width, number, engine in OUT_PIECES}
         last_step = max(mel_step.values())
+        open_step = {j0: min(step, len(UNITS) + SQUARE_LAG) for j0, step in mel_step.items()}
+        open_step[S - NARROW] = last_step
         store_step = {j0: step + 1 if j0 == 0 else last_step + 1 for j0, step in mel_step.items()}
         store_step[WIDE] = len(UNITS) + ADD_LAG
-        open_step = {j0: min(step, len(UNITS) + 1) for j0, step in mel_step.items()}
-        open_step[S - NARROW] = last_step
+        h_step = {J_HALF: S // P + ROOT_LAG, 0: S // P + ROOT_LAG + 1}
         for step in range(last_step + 2):
             for half, index in enumerate(WM_BEHIND):
                 if step == index + ROOT_LAG + 1:
                     prepare_wm(half, "b_square%d%d" % UNITS[index])
             for j0 in (0, J_HALF):
-                if step == (j0 + J_HALF) // P + ROOT_LAG:
+                if step == h_step[j0]:
                     quantize_h(0, j0, J_HALF)
             for j0, width, number, engine in OUT_PIECES:
                 if step == open_step[j0]:
@@ -455,7 +462,7 @@ def tile_list_quadrature_magnitude_mel_kernel(
                 turn_b(UNITS[step])
             if 0 <= step - ADD_LAG < len(UNITS):
                 add_squares(UNITS[step - ADD_LAG])
-            if step < EARLY_SUMS:
+            if step < A_BANKS:
                 multiply_a(step, [1], start=False, stop=True)
             elif step < len(UNITS):
                 multiply_a(step, [0, 1], start=True, stop=True)

@@ -26,26 +26,24 @@ J_HALF = S // 2
 BANKS = 8
 A_BANKS = 3
 EARLY_TURNED = BANKS - A_BANKS
+QUARTER = PASS // 2
+NARROW = P
+WIDE = 2 * P
 
-UNITS = [(half, jt) for half in range(2) for jt in range(S // P)]
-LAST_UNITS = 4
-A_BANK = [index % A_BANKS for index in range(len(UNITS) - LAST_UNITS)] + [1, 0] * (LAST_UNITS // 2)
-LATE_TURNED = {EARLY_TURNED: A_BANKS, 10: A_BANKS + 1}
-TURNED = dict(list(zip(UNITS[:EARLY_TURNED], range(A_BANKS, BANKS))) + [(UNITS[i], b) for i, b in LATE_TURNED.items()])
-NARROW = 128
-WIDE = 256
-WC_SPLIT = 2
+FRONT_TILES = 6
+BACK = FRONT_TILES * P
+UNITS = [(half, jt) for half in range(2) for jt in range(FRONT_TILES)]
+UNITS = UNITS + [(half, jt) for jt in range(FRONT_TILES, S // P) for half in (1, 0)]
+SUM_BANK = [A_BANKS + jt for jt in range(EARLY_TURNED)] + [A_BANKS, A_BANKS, 5]
 OUT_PIECES = [
-    (0, 256, 5, "vector"),
-    (256, 256, 6, "vector"),
-    (512, 256, 1, "scalar"),
-    (768, 128, 0, "vector"),
-    (896, 128, 7, "vector"),
+    (0, WIDE, (5,), ("vector",)),
+    (WIDE, WIDE, (6,), ("vector",)),
+    (2 * WIDE, WIDE, (2,), ("vector",)),
+    (BACK, NARROW, (4,), ("scalar",)),
+    (BACK + NARROW, NARROW, (7, 6), ("scalar", "vector")),
 ]
 SQUARE_LAG, ADD_LAG, ROOT_LAG = 1, 2, 3
 SQUARE_BUFFERS = 4
-FIRST_DIRECT = EARLY_TURNED + 1
-WM_BEHIND = (FIRST_DIRECT + 1, FIRST_DIRECT + 2)
 
 
 def tile_list_quadrature_magnitude_mel_kernel(
@@ -100,7 +98,7 @@ def tile_list_quadrature_magnitude_mel_kernel(
         nc.vector.memset(warm_in[:], 1.0)
         nc.scalar.activation(out=warm_out[:], in_=warm_in[:], func=ACT.Sqrt)
 
-        group_rows = buffer("picked1", [P, S], F32)
+        group_rows = buffer("picked1", [P, J_HALF], F32)
         nc.gpsimd.memset(table_scales[:], 0)
         nc.vector.memset(group_rows[:], 0.0)
         nc.vector.memset(ws_scales_raw[:], 0)
@@ -109,26 +107,27 @@ def tile_list_quadrature_magnitude_mel_kernel(
         nc.sync.dma_start(table_list[:], offs)
         nc.sync.dma_start(out=ws_words_raw[:], in_=ws_words[0].bitcast(I32))
         load_scale_rows(table_scales, tab_scales[0])
-        nc.sync.dma_start(out=group_rows[0:P:ROW, :], in_=wgt[0:P:ROW, :])
+        half_rows = wgt.rearrange("p (part j) -> (p part) j", part=2)
+        nc.sync.dma_start(out=group_rows[4:P:8, :], in_=half_rows[0 : 2 * P : ROW + 1, :])
         nc.sync.dma_start(out=table_words[:], in_=tab_words[0].rearrange("p t i -> p (t i)").bitcast(I32))
         nc.sync.dma_start(frame_lists[:], offs2)
         load_scale_rows(ws_scales_raw, ws_scales[0])
         for plane in range(6):
             load_plane(plane)
-        load_wc(1, 0, PASS, "wc_a")
+        load_wc(0, 0, PASS, "wc_a")
         load_plane(6)
-        load_wc(0, 0, PASS, "wc_b")
+        load_wc(1, 0, QUARTER, "wc_b")
         load_plane(7)
+        load_wc(1, QUARTER, QUARTER, "wc_c")
 
         repeated = buffer("round_x0", [P, S], F32)
+        turned = bank(4, [P, J_HALF])
+        for j0 in range(0, J_HALF, P):
+            nc.tensor.transpose(turned[:, j0 : j0 + P], group_rows[:, j0 : j0 + P], identity[:])
         for part in range(2):
-            turned = bank(4 + part, [P, J_HALF])
-            for j0 in range(0, J_HALF, P):
-                j = J_HALF * part + j0
-                nc.tensor.transpose(turned[:, j0 : j0 + P], group_rows[:, j : j + P], identity[:])
             nc.scalar.copy(
                 out=repeated[:, J_HALF * part : J_HALF * (part + 1)].rearrange("p (column x) -> p column x", x=ROW),
-                in_=turned[:, 0:J_HALF:ROW].unsqueeze(2).to_broadcast([P, J_HALF // ROW, ROW]),
+                in_=turned[:, 8 * part + 4 : J_HALF : ROW].unsqueeze(2).to_broadcast([P, J_HALF // ROW, ROW]),
             )
         for part in range(2):
             turned = bank(6 + part, [P, J_HALF])
@@ -138,8 +137,8 @@ def tile_list_quadrature_magnitude_mel_kernel(
             nc.scalar.copy(out=weights[:, J_HALF * part : J_HALF * (part + 1)], in_=turned[:])
 
         v_scales = held.tile([P, S], U8, name="v_scales", align_bytes=64)
-        ws_codes = held.tile([P, 2 * H], U8, name="ws_codes", align_bytes=64)
-        ws_scale = held.tile([P, H], U8, name="ws_scale", align_bytes=64)
+        ws_codes = held.tile([P, 2 * PASS], U8, name="ws_codes", align_bytes=64)
+        ws_scale = held.tile([P, PASS], U8, name="ws_scale", align_bytes=64)
         v_words = [held.tile([P, J_HALF], U32, name="v_words%d" % part, align_bytes=64) for part in range(2)]
 
         def entries(lists, j0, width):
@@ -151,21 +150,24 @@ def tile_list_quadrature_magnitude_mel_kernel(
             out=v_words[1][:], in_=table_words[:].bitcast(U32).indirect(entries(table_list, J_HALF, J_HALF))
         )
         nc.vector.tensor_copy(
-            out=ws_codes[:].bitcast(I32).rearrange("p (half t u) -> p half u t", half=2, t=PACK),
-            in_=ws_words_raw[:].rearrange("p (half u t) -> p half u t", half=2, t=PACK),
+            out=ws_codes[:].bitcast(I32).rearrange("p (t u) -> p u t", t=PACK),
+            in_=ws_words_raw[:, PASS // 2 :].rearrange("p (u t) -> p u t", t=PACK),
         )
         nc.vector.tensor_copy(
-            out=ws_scale[:].bitcast(U16).rearrange("p (half t u) -> p half u t", half=2, t=PACK),
-            in_=ws_scales_raw[:].bitcast(U16).rearrange("p (half u t) -> p half u t", half=2, t=PACK),
+            out=ws_scale[:].bitcast(U16).rearrange("p (t u) -> p u t", t=PACK),
+            in_=ws_scales_raw[:, PASS // 4 :].bitcast(U16).rearrange("p (u t) -> p u t", t=PACK),
         )
 
-        def product(unit, sums, passes, start, stop):
-            groups = [slice(0, PASS)] if unit in TURNED else [slice(P * t, P * (t + 1)) for t in range(PACK)]
+        def is_turned(unit):
+            return unit[0] == 0
+
+        def product(unit, sums, passes, start, stop, bins=slice(0, PASS)):
+            groups = [bins] if is_turned(unit) else [slice(P * t, P * (t + 1)) for t in range(PACK)]
             for cols in groups:
                 for order, (w_codes, w_scales, per_col, w_dtype, codes, scales) in enumerate(passes):
                     weight = (w_codes[:, per_col * cols.start : per_col * cols.stop].bitcast(w_dtype), w_scales[:, cols])
                     picked = (codes.bitcast(FP8X4), scales)
-                    still, moving = (picked, weight) if unit in TURNED else (weight, picked)
+                    still, moving = (picked, weight) if is_turned(unit) else (weight, picked)
                     nc.tensor.matmul_mx(
                         out=sums[:, cols],
                         lhsT=still[0],
@@ -176,15 +178,15 @@ def tile_list_quadrature_magnitude_mel_kernel(
                         stop=stop and order == len(passes) - 1,
                     )
 
-        def square(unit, dst, sums):
-            if unit in TURNED:
-                nc.scalar.activation(out=dst[:], in_=sums[:], func=ACT.Square)
-            else:
-                nc.scalar.activation(
-                    out=dst[:].rearrange("p (j t) -> p j t", t=PACK),
-                    in_=sums[:].rearrange("p (t j) -> p j t", t=PACK),
-                    func=ACT.Square,
-                )
+        def square(dst, dst_order, sums, sums_order, **sizes):
+            nc.scalar.activation(
+                out=dst[:].rearrange(dst_order, t=PACK, **sizes),
+                in_=sums[:].rearrange(sums_order, t=PACK, **sizes),
+                func=ACT.Square,
+            )
+
+        def square_direct(dst, sums):
+            square(dst, "p (j t) -> p j t", sums, "p (t j) -> p j t")
 
         def turn(unit, squares, start):
             for t in range(PACK):
@@ -199,7 +201,7 @@ def tile_list_quadrature_magnitude_mel_kernel(
                 )
 
         def turn_b(unit):
-            turned_sum[unit] = bank(TURNED[unit], [P, PASS])
+            turned_sum[unit] = bank(SUM_BANK[unit[1]], [P, PASS])
             turn(unit, b_square[unit], start=True)
 
         b_square, turned_sum = {}, {}
@@ -208,11 +210,9 @@ def tile_list_quadrature_magnitude_mel_kernel(
             half, jt = unit
             sums = bank(serial % BANKS, [P, PASS])
             j_in_half = P * jt % J_HALF
-            as_loaded = unit in TURNED
-            codes, scales = (ws_words_raw[:].bitcast(U8), ws_scales_raw[:].bitcast(U8)) if as_loaded else (ws_codes, ws_scale)
             ws_pass = (
-                codes[:, 2 * PASS * half : 2 * PASS * (half + 1)],
-                scales[:, PASS * half : PASS * (half + 1)],
+                ws_words_raw[:, 0 : PASS // 2].bitcast(U8) if is_turned(unit) else ws_codes[:],
+                ws_scales_raw[:, 0 : PASS // 4].bitcast(U8) if is_turned(unit) else ws_scale[:],
                 2,
                 FP4X4,
                 v_words[P * jt // J_HALF][:, j_in_half : j_in_half + P],
@@ -220,18 +220,14 @@ def tile_list_quadrature_magnitude_mel_kernel(
             )
             product(unit, sums, [ws_pass], start=True, stop=True)
             b_square[unit] = buffer("b_square%d%d" % unit, [P, PASS], F32)
-            if as_loaded:
-                nc.scalar.activation(
-                    out=b_square[unit][:].rearrange("p (t u e) -> p t u e", t=PACK, e=2),
-                    in_=sums[:].rearrange("p (u t e) -> p t u e", t=PACK, e=2),
-                    func=ACT.Square,
-                )
+            if is_turned(unit):
+                square(b_square[unit], "p (t u e) -> p t u e", sums, "p (u t e) -> p t u e", e=2)
             else:
-                square(unit, b_square[unit], sums)
+                square_direct(b_square[unit], sums)
         for unit in UNITS[:EARLY_TURNED]:
             turn_b(unit)
 
-        picked_planes, xg_rounded, w_rounded = {}, {}, {}
+        picked_planes, xg_rounded = {}, {}
         xg_codes, wc_codes = {}, {}
         xg_scales, wc_scales = {}, {}
         wm_codes = held.tile([P, 2, N], U32, name="wm_codes", align_bytes=64)
@@ -269,17 +265,20 @@ def tile_list_quadrature_magnitude_mel_kernel(
             codes = held.tile([P, width], U32, name="xg_codes1_%d" % j0, align_bytes=64)
             quantize_xg(1, j0, width, codes[:])
 
-        def round_wc(g, half, engine, t0, t1):
-            src = wc_raw[g, PASS * half][:].rearrange("p i (u t e) -> p t u i e", t=PACK, e=2)
-            dst = w_rounded[g, half].rearrange("p (t u e i) -> p t u i e", t=PACK, e=2, i=PACK)
+        def round_wc(engine, dst, src, t0=0, t1=PACK):
+            src = src.rearrange("p i (u t e) -> p t u i e", t=PACK, e=2)
+            dst = dst.rearrange("p (t u e i) -> p t u i e", t=PACK, e=2, i=PACK)
             round_copy(engine, dst[:, t0:t1], src[:, t0:t1])
 
-        def quantize_wc(g, half):
+        def wc_tiles(g, half, codes):
+            wc_codes[g, half] = codes[:]
             wc_scales[g, half] = held.tile([P, PASS], U8, name="wc_scales%d%d" % (g, half), align_bytes=64)[:]
+
+        def quantize_wc(g, half, src, col0=0, cols=PASS):
             nc.vector.quantize_mx(
-                out=wc_codes[g, half].bitcast(FP8X4),
-                scales=wc_scales[g, half],
-                in_=w_rounded[g, half],
+                out=wc_codes[g, half][:, col0 : col0 + cols].bitcast(FP8X4),
+                scales=wc_scales[g, half][:, col0 : col0 + cols],
+                in_=src,
             )
 
         def prepare_wm(half, tag):
@@ -292,17 +291,19 @@ def tile_list_quadrature_magnitude_mel_kernel(
 
         a_sums, a_square = {}, {}
 
-        def multiply_a(index, passes, start, stop):
+        def multiply_a(index, passes, start, stop, bins=slice(0, PASS)):
             unit = half, jt = UNITS[index]
             if start:
-                a_sums[unit] = bank(A_BANK[index], [P, PASS])
+                a_sums[unit] = bank(index % A_BANKS, [P, PASS])
             operands = [
                 (wc_codes[g, half], wc_scales[g, half], 1, FP8X4, xg_codes[g, jt], xg_scales[g, jt]) for g in passes
             ]
-            product(unit, a_sums[unit], operands, start, stop)
+            product(unit, a_sums[unit], operands, start, stop, bins)
 
-        for g in range(2):
-            picked_planes[g] = buffer("picked%d" % g, [P, PACK, S], F32)
+        last_plane = (PACK - 1) * S
+        picked_planes[0] = buffer("picked0", [P, PACK, S], F32)
+        picked_row = buffer("picked1", [P, last_plane + BACK + PASS * PACK // 2], F32)
+        picked_planes[1] = picked_row[:, 0 : PACK * S].rearrange("p (i j) -> p i j", i=PACK)
         gather(0, 0, J_HALF)
         gather(0, J_HALF, J_HALF)
         load_wc(0, PASS, PASS, "plane0")
@@ -324,59 +325,71 @@ def tile_list_quadrature_magnitude_mel_kernel(
         gather_plane(4)
         gather_plane(5)
         quantize_xg(0, 0, J_HALF, held.tile([P, J_HALF], U32, name="xg_codes0", align_bytes=64)[:])
-        w_rounded[1, 0] = buffer("round_w0", [P, PASS * PACK], BF16)[:]
-        round_wc(1, 0, "scalar", 0, PACK)
+        pass0_rounded = rounded("round_w0", PASS)
+        for bin0 in (0, QUARTER):
+            round_wc("scalar", pass0_rounded[:, PACK * bin0 : PACK * (bin0 + QUARTER)], wc_raw[0, 0][:, :, bin0 : bin0 + QUARTER])
         gather_plane(6)
-        wc_codes[1, 0] = buffer("plane6", [P, PASS], U32)[:]
-        quantize_wc(1, 0)
-        w_rounded[0, 0] = buffer("round_w1", [P, PASS * PACK], BF16)[:]
-        round_wc(0, 0, "scalar", 0, WC_SPLIT)
-        round_wc(0, 0, "vector", WC_SPLIT, PACK)
-        for g, half in ((0, 0), (0, 1), (1, 1)):
-            wc_codes[g, half] = held.tile([P, PASS], U32, name="wc_codes%d%d" % (g, half), align_bytes=64)[:]
-        quantize_wc(0, 0)
+        wc_tiles(0, 0, buffer("plane6", [P, PASS], U32))
+        quantize_wc(0, 0, pass0_rounded[:])
         for index in range(A_BANKS):
             multiply_a(index, [0], start=True, stop=False)
+        early_quarter = rounded("round_w1", QUARTER)
+        round_wc("scalar", early_quarter[:], wc_raw[1, 0][:])
+        for half in range(2):
+            wc_tiles(1, half, held.tile([P, PASS], U32, name="wc_codes1%d" % half, align_bytes=64))
+        quantize_wc(1, 0, early_quarter[:], 0, QUARTER)
+
+        tile_tags = ["round_piece0", "round_piece128", "round_piece256", "round_x0"]
+
+        def round_tile(jt):
+            round_xg(1, P * jt, NARROW, "scalar", rounded(tile_tags[jt], NARROW)[:])
 
         gather(7, 0, NARROW)
         gather(7, NARROW, WIDE)
-        for j0 in (0, NARROW):
-            round_xg(1, j0, NARROW, "vector", rounded("round_piece%d" % j0, NARROW)[:])
-        round_xg(1, WIDE, NARROW, "scalar", rounded("round_piece%d" % WIDE, NARROW)[:])
+        gather(7, NARROW + WIDE, NARROW)
+        round_tile(0)
+        round_tile(1)
+        late_quarter = picked_row[:, last_plane + J_HALF : PACK * S].bitcast(BF16)
+        round_wc("vector", late_quarter, wc_raw[1, QUARTER][:])
         quantize_last(0, NARROW)
-        gather(7, WIDE + NARROW, NARROW)
-        round_xg(1, WIDE + NARROW, NARROW, "vector", rounded("round_x0", NARROW)[:])
-        for j0 in (NARROW, WIDE, WIDE + NARROW):
-            quantize_last(j0, NARROW)
-        for j0 in (J_HALF, J_HALF + WIDE):
-            gather(7, j0, WIDE)
-        on_table = buffer("table", [P, 2, PASS * PACK], BF16)
-        w_rounded[0, 1], w_rounded[1, 1] = on_table[:, 0, :], on_table[:, 1, :]
+        multiply_a(0, [1], start=False, stop=False, bins=slice(0, QUARTER))
+        quantize_wc(1, 0, late_quarter, QUARTER, QUARTER)
+        quantize_last(P, NARROW)
+        round_tile(2)
+        round_tile(3)
+        quantize_last(2 * P, NARROW)
+        quantize_last(3 * P, NARROW)
+
+        gather(7, J_HALF, WIDE)
+        second_half = [buffer("table", [P, PASS * PACK], BF16)[:], picked_row[:, last_plane + BACK :].bitcast(BF16)]
         late = rounded("round_w0", J_HALF)
         round_xg(1, J_HALF, WIDE, "vector", late[:, 0 : PACK * WIDE])
-        quantize_xg(0, J_HALF, J_HALF, buffer("round_piece0", [P, J_HALF], U32)[:])
+        xg_rounded[0, BACK] = xg_rounded[0, J_HALF][:, PACK * WIDE :]
+        xg_rounded[0, J_HALF] = xg_rounded[0, J_HALF][:, 0 : PACK * WIDE]
+        quantize_xg(0, J_HALF, WIDE, buffer(tile_tags[2], [P, WIDE], U32)[:])
         quantize_last(J_HALF, WIDE)
-        round_xg(1, J_HALF + WIDE, WIDE, "vector", late[:, PACK * WIDE : PACK * J_HALF])
-        round_wc(0, 1, "vector", 0, PACK)
-        quantize_last(J_HALF + WIDE, WIDE)
-        round_wc(1, 1, "vector", 0, PACK)
-        for g in range(2):
-            quantize_wc(g, 1)
+        round_wc("vector", second_half[0], wc_raw[0, PASS][:])
+        wc_tiles(0, 1, held.tile([P, PASS], U32, name="wc_codes01", align_bytes=64))
+        quantize_wc(0, 1, second_half[0])
+        for t0 in (0, 2):
+            round_wc("vector", second_half[1], wc_raw[1, PASS][:], t0, t0 + 2)
+        for t0 in (0, 2):
+            quantize_wc(1, 1, second_half[1][:, PASS * t0 : PASS * (t0 + 2)], P * t0, 2 * P)
 
         h_rounded = [buffer(tag, [P, S * PACK], BF16) for tag in ("plane3", "plane4")]
         h_codes, h_scales = {}, {}
-        results = buffer("plane7", [P, N // P * S], F32)
+        results = buffer("plane5", [P, N // P * S], F32)
         mel_sums = {}
 
         def square_a(unit):
-            if unit == UNITS[-1]:
-                a_square[unit] = buffer("last_square", [P, PASS], F32)
+            a_square[unit] = shared.tile([P, PASS], F32, name="a_square", tag="a_square", bufs=SQUARE_BUFFERS)
+            if is_turned(unit):
+                square(a_square[unit], "p (t q w) -> p q t w", a_sums[unit], "p (q t w) -> p q t w", q=2)
             else:
-                a_square[unit] = shared.tile([P, PASS], F32, name="a_square", tag="a_square", bufs=SQUARE_BUFFERS)
-            square(unit, a_square[unit], a_sums[unit])
+                square_direct(a_square[unit], a_sums[unit])
 
         def add_squares(unit):
-            if unit in TURNED:
+            if is_turned(unit):
                 turn(unit, a_square[unit], start=False)
             else:
                 nc.vector.tensor_tensor(b_square[unit][:], a_square[unit][:], b_square[unit][:], ALU.add)
@@ -384,7 +397,7 @@ def tile_list_quadrature_magnitude_mel_kernel(
         def root(unit):
             half, jt = unit
             dst = h_rounded[half][:, PASS * jt : PASS * (jt + 1)]
-            if unit in TURNED:
+            if is_turned(unit):
                 nc.scalar.activation(
                     out=dst.rearrange("p (j t) -> p j t", t=PACK),
                     in_=turned_sum[unit][:].rearrange("p (t j) -> p j t", t=PACK),
@@ -395,7 +408,7 @@ def tile_list_quadrature_magnitude_mel_kernel(
 
         def quantize_h(half, j0, width):
             if (half, j0) == (0, 0):
-                codes = buffer("b_square%d%d" % UNITS[FIRST_DIRECT], [P, width], U32)
+                codes = buffer("b_square%d%d" % UNITS[FRONT_TILES], [P, width], U32)
             else:
                 codes = held.tile([P, width], U32, name="h_codes%d_%d" % (half, j0), align_bytes=64)
             scales = held.tile([P, width], U8, name="h_scales%d_%d" % (half, j0), align_bytes=64)
@@ -407,62 +420,89 @@ def tile_list_quadrature_magnitude_mel_kernel(
             for j in range(0, width, P):
                 h_codes[half, j0 + j], h_scales[half, j0 + j] = codes[:, j:width], scales[:, j:width]
 
-        def multiply_mel(j0, width, number, half):
-            if half == 0:
-                mel_sums[j0] = bank(number, [P, N // P, width])
+        def multiply_mel(j0, width, banks, half, opens):
+            per_bank = N // P // len(banks)
+            if opens:
+                mel_sums[j0] = [bank(number, [P, per_bank, width]) for number in banks]
             for c in range(N // P):
                 nc.tensor.matmul_mx(
-                    out=mel_sums[j0][:, c, :],
+                    out=mel_sums[j0][c // per_bank][:, c % per_bank, :],
                     lhsT=wm_codes[:, half, P * c : P * (c + 1)].bitcast(FP8X4),
                     lhsT_scale=wm_scales[:, half, P * c : P * (c + 1)],
                     rhs=h_codes[half, j0][:, 0:width].bitcast(FP8X4),
                     rhs_scale=h_scales[half, j0][:, 0:width],
-                    start=half == 0 and c == 0,
-                    stop=half == 1 and c == N // P - 1,
+                    start=opens and c % per_bank == 0,
+                    stop=not opens and c % per_bank == per_bank - 1,
                 )
 
-        def store(j0, width, engine):
-            if j0 == WIDE:
-                result = buffer("last_square", [P, N // P, width], F32)[:]
+        def add_bias(engine, result, sums, c0, count):
+            if engine == "scalar":
+                for c in range(count):
+                    column = bias[:, c0 + c : c0 + c + 1]
+                    nc.scalar.activation(out=result[:, c, :], in_=sums[:, c, :], func=ACT.Identity, bias=column)
+            elif count == 1:
+                nc.vector.tensor_scalar(result[:, 0, :], sums[:, 0, :], bias[:, c0 : c0 + 1], None, ALU.add)
             else:
-                result = results[:, N // P * j0 : N // P * (j0 + width)].rearrange("p (c j) -> p c j", j=width)
-            if engine == "vector":
-                spread = bias[:].unsqueeze(2).to_broadcast([P, N // P, width])
-                nc.vector.tensor_tensor(result, mel_sums[j0][:], spread, ALU.add)
-            else:
-                for c in range(N // P):
-                    nc.scalar.activation(
-                        out=result[:, c, :], in_=mel_sums[j0][:, c, :], func=ACT.Identity, bias=bias[:, c : c + 1]
-                    )
-            nc.sync.dma_start(out=out.rearrange("(c p) j -> p c j", p=P)[:, :, j0 : j0 + width], in_=result)
+                nc.vector.tensor_tensor(result, sums[:], bias[:].unsqueeze(2).to_broadcast(list(result.shape)), ALU.add)
 
-        mel_step = {j0: S // P + (j0 + width) // P + ROOT_LAG for j0, width, number, engine in OUT_PIECES}
-        last_step = max(mel_step.values())
-        open_step = {j0: min(step, len(UNITS) + SQUARE_LAG) for j0, step in mel_step.items()}
-        open_step[S - NARROW] = last_step
-        store_step = {j0: step + 1 if j0 == 0 else last_step + 1 for j0, step in mel_step.items()}
-        store_step[WIDE] = len(UNITS) + ADD_LAG
-        h_step = {J_HALF: S // P + ROOT_LAG, 0: S // P + ROOT_LAG + 1}
-        for step in range(last_step + 2):
-            for half, index in enumerate(WM_BEHIND):
-                if step == index + ROOT_LAG + 1:
-                    prepare_wm(half, "b_square%d%d" % UNITS[index])
-            for j0 in (0, J_HALF):
-                if step == h_step[j0]:
-                    quantize_h(0, j0, J_HALF)
-            for j0, width, number, engine in OUT_PIECES:
-                if step == open_step[j0]:
-                    multiply_mel(j0, width, number, 0)
-                if step == mel_step[j0]:
-                    quantize_h(1, j0, width)
-                    multiply_mel(j0, width, number, 1)
-                if step == store_step[j0]:
-                    store(j0, width, engine)
-            if step in LATE_TURNED:
+        def store(j0, width, engines):
+            result = results[:, N // P * j0 : N // P * (j0 + width)].rearrange("p (c j) -> p c j", j=width)
+            rows = out.rearrange("(c p) j -> p c j", p=P)[:, :, j0 : j0 + width]
+            count = N // P // len(engines)
+            for part, engine in enumerate(engines):
+                add_bias(engine, result[:, count * part : count * (part + 1), :], mel_sums[j0][part], count * part, count)
+            if count == 1:
+                for c in range(N // P):
+                    nc.sync.dma_start(out=rows[:, c, :], in_=result[:, c, :])
+            else:
+                nc.sync.dma_start(out=rows, in_=result)
+
+        def after_root(half, j_end):
+            return UNITS.index((half, j_end // P - 1)) + ROOT_LAG + 1
+
+        closing, code_step, mel_step = {}, {}, {}
+        for j0, width, banks, engines in OUT_PIECES:
+            closing[j0] = 1 if j0 < BACK else 0
+            code_step[j0] = after_root(closing[j0], j0 + width)
+            last_user = max([index for index in range(len(UNITS)) if index % A_BANKS == banks[0]] + [0])
+            mel_step[j0] = max(code_step[j0], last_user + SQUARE_LAG + 1) if banks[0] < A_BANKS else code_step[j0]
+        wm_step = [after_root(1, P * (half + 1)) for half in range(2)]
+        opening_codes = [(0, 0, J_HALF, wm_step[0]), (0, J_HALF, WIDE, wm_step[1])]
+        opening_codes = opening_codes + [(1, j0, NARROW, after_root(1, j0 + NARROW)) for j0 in range(BACK, S, P)]
+        for step in range(max(mel_step.values()) + 2):
+            if step == FRONT_TILES:
+                gather(7, BACK, WIDE)
+                quantize_xg(0, BACK, WIDE, held.tile([P, WIDE], U32, name="xg_codes0_back", align_bytes=64)[:])
+            if step == FRONT_TILES + ADD_LAG:
+                round_xg(1, BACK, WIDE, "vector", late[:, PACK * WIDE : PACK * J_HALF])
+            if step == FRONT_TILES + ROOT_LAG:
+                quantize_last(BACK, WIDE)
+            for half in range(2):
+                if step == wm_step[half]:
+                    prepare_wm(half, "b_square%d%d" % UNITS[FRONT_TILES + half])
+            adding = UNITS[step - ADD_LAG] if 0 <= step - ADD_LAG < len(UNITS) else None
+            if step == EARLY_TURNED:
                 turn_b(UNITS[step])
-            if 0 <= step - ADD_LAG < len(UNITS):
-                add_squares(UNITS[step - ADD_LAG])
-            if step < A_BANKS:
+            if adding:
+                add_squares(adding)
+            for half, j0, width, at in opening_codes:
+                if step == at:
+                    quantize_h(half, j0, width)
+            for j0, width, banks, engines in OUT_PIECES:
+                if step == mel_step[j0]:
+                    multiply_mel(j0, width, banks, 1 - closing[j0], opens=True)
+                if step == code_step[j0]:
+                    quantize_h(closing[j0], j0, width)
+                if step == mel_step[j0]:
+                    multiply_mel(j0, width, banks, closing[j0], opens=False)
+            for j0, width, banks, engines in OUT_PIECES:
+                if step == mel_step[j0] + 1:
+                    store(j0, width, engines)
+            if 2 * FRONT_TILES <= step < len(UNITS) - 1 and is_turned(UNITS[step + 1]):
+                turn_b(UNITS[step + 1])
+            if step == 0:
+                multiply_a(step, [1], start=False, stop=True, bins=slice(QUARTER, PASS))
+            elif step < A_BANKS:
                 multiply_a(step, [1], start=False, stop=True)
             elif step < len(UNITS):
                 multiply_a(step, [0, 1], start=True, stop=True)

@@ -327,7 +327,8 @@ def tile_list_quadrature_magnitude_mel_kernel(
         quantize_xg(0, 0, J_HALF, held.tile([P, J_HALF], U32, name="xg_codes0", align_bytes=64)[:])
         pass0_rounded = rounded("round_w0", PASS)
         for bin0 in (0, QUARTER):
-            round_wc("scalar", pass0_rounded[:, PACK * bin0 : PACK * (bin0 + QUARTER)], wc_raw[0, 0][:, :, bin0 : bin0 + QUARTER])
+            quarter_raw = wc_raw[0, 0][:, :, bin0 : bin0 + QUARTER]
+            round_wc("scalar", pass0_rounded[:, PACK * bin0 : PACK * (bin0 + QUARTER)], quarter_raw)
         gather_plane(6)
         wc_tiles(0, 0, buffer("plane6", [P, PASS], U32))
         quantize_wc(0, 0, pass0_rounded[:])
@@ -351,7 +352,7 @@ def tile_list_quadrature_magnitude_mel_kernel(
         round_tile(1)
         late_quarter = picked_row[:, last_plane + J_HALF : PACK * S].bitcast(BF16)
         round_wc("vector", late_quarter, wc_raw[1, QUARTER][:])
-        quantize_last(0, NARROW)
+        quantize_xg(1, 0, NARROW, buffer("wc_c", [P, NARROW], U32)[:])
         multiply_a(0, [1], start=False, stop=False, bins=slice(0, QUARTER))
         quantize_wc(1, 0, late_quarter, QUARTER, QUARTER)
         quantize_last(P, NARROW)
@@ -361,13 +362,13 @@ def tile_list_quadrature_magnitude_mel_kernel(
         quantize_last(3 * P, NARROW)
 
         gather(7, J_HALF, WIDE)
-        second_half = [buffer("table", [P, PASS * PACK], BF16)[:], picked_row[:, last_plane + BACK :].bitcast(BF16)]
         late = rounded("round_w0", J_HALF)
         round_xg(1, J_HALF, WIDE, "vector", late[:, 0 : PACK * WIDE])
         xg_rounded[0, BACK] = xg_rounded[0, J_HALF][:, PACK * WIDE :]
         xg_rounded[0, J_HALF] = xg_rounded[0, J_HALF][:, 0 : PACK * WIDE]
         quantize_xg(0, J_HALF, WIDE, buffer(tile_tags[2], [P, WIDE], U32)[:])
         quantize_last(J_HALF, WIDE)
+        second_half = [rounded("table", PASS)[:], picked_row[:, last_plane + BACK :].bitcast(BF16)]
         round_wc("vector", second_half[0], wc_raw[0, PASS][:])
         wc_tiles(0, 1, held.tile([P, PASS], U32, name="wc_codes01", align_bytes=64))
         quantize_wc(0, 1, second_half[0])
@@ -382,7 +383,10 @@ def tile_list_quadrature_magnitude_mel_kernel(
         mel_sums = {}
 
         def square_a(unit):
-            a_square[unit] = shared.tile([P, PASS], F32, name="a_square", tag="a_square", bufs=SQUARE_BUFFERS)
+            if unit == UNITS[FRONT_TILES]:
+                a_square[unit] = buffer("first_direct", [P, PASS], F32)
+            else:
+                a_square[unit] = shared.tile([P, PASS], F32, name="a_square", tag="a_square", bufs=SQUARE_BUFFERS)
             if is_turned(unit):
                 square(a_square[unit], "p (t q w) -> p q t w", a_sums[unit], "p (q t w) -> p q t w", q=2)
             else:
@@ -476,15 +480,16 @@ def tile_list_quadrature_magnitude_mel_kernel(
             if step == FRONT_TILES + ADD_LAG:
                 round_xg(1, BACK, WIDE, "vector", late[:, PACK * WIDE : PACK * J_HALF])
             if step == FRONT_TILES + ROOT_LAG:
-                quantize_last(BACK, WIDE)
+                quantize_xg(1, BACK, WIDE, buffer("first_direct", [P, WIDE], U32)[:])
             for half in range(2):
                 if step == wm_step[half]:
                     prepare_wm(half, "b_square%d%d" % UNITS[FRONT_TILES + half])
-            adding = UNITS[step - ADD_LAG] if 0 <= step - ADD_LAG < len(UNITS) else None
             if step == EARLY_TURNED:
-                turn_b(UNITS[step])
-            if adding:
-                add_squares(adding)
+                multiply_a(step, [0, 1], start=True, stop=True)
+            if step == EARLY_TURNED + 1:
+                turn_b(UNITS[EARLY_TURNED])
+            if 0 <= step - ADD_LAG < len(UNITS):
+                add_squares(UNITS[step - ADD_LAG])
             for half, j0, width, at in opening_codes:
                 if step == at:
                     quantize_h(half, j0, width)
@@ -504,7 +509,7 @@ def tile_list_quadrature_magnitude_mel_kernel(
                 multiply_a(step, [1], start=False, stop=True, bins=slice(QUARTER, PASS))
             elif step < A_BANKS:
                 multiply_a(step, [1], start=False, stop=True)
-            elif step < len(UNITS):
+            elif step < len(UNITS) and step != EARLY_TURNED:
                 multiply_a(step, [0, 1], start=True, stop=True)
             for lag, stage in ((SQUARE_LAG, square_a), (ROOT_LAG, root)):
                 if 0 <= step - lag < len(UNITS):

@@ -266,9 +266,9 @@ def tile_list_quadrature_magnitude_mel_kernel(
             quantize_xg(1, j0, width, codes[:])
 
         def round_wc(engine, dst, src, t0=0, t1=PACK):
-            src = src.rearrange("p i (u t e) -> p t u i e", t=PACK, e=2)
-            dst = dst.rearrange("p (t u e i) -> p t u i e", t=PACK, e=2, i=PACK)
-            round_copy(engine, dst[:, t0:t1], src[:, t0:t1])
+            src = src.rearrange("p i (u t e) -> p u t i e", t=PACK, e=2)
+            dst = dst.rearrange("p (t u e i) -> p u t i e", t=PACK, e=2, i=PACK)
+            round_copy(engine, dst[:, :, t0:t1], src[:, :, t0:t1])
 
         def wc_tiles(g, half, codes):
             wc_codes[g, half] = codes[:]

@@ -23,6 +23,7 @@ PASS = P * PACK
 ROW = 16
 RUN = 2
 J_HALF = S // 2
+DMA_ALIGN = 256
 BANKS = 8
 A_BANKS = 3
 EARLY_TURNED = BANKS - A_BANKS
@@ -56,7 +57,7 @@ def tile_list_quadrature_magnitude_mel_kernel(
         psum = ctx.enter_context(tc.psum_pool(name="psum", bufs=1))
 
         def buffer(tag, shape, dtype):
-            return shared.tile(shape, dtype, name=tag, tag=tag, bufs=1, align_bytes=64)
+            return shared.tile(shape, dtype, name=tag, tag=tag, bufs=1, align_bytes=DMA_ALIGN)
 
         def bank(number, shape):
             return psum.tile(shape, F32, name="bank%d" % number, tag="bank%d" % number, bufs=1)
@@ -87,9 +88,9 @@ def tile_list_quadrature_magnitude_mel_kernel(
         frame_lists = held.tile([P, S // ROW], U16, name="frame_lists")
         weights = held.tile([P, S], F32, name="weights")
         table_words = buffer("table", [P, T], I32)
-        table_scales = held.tile([P, T // 4], I32, name="table_scales")
-        ws_words_raw = held.tile([P, H // 2], I32, name="ws_words_raw", align_bytes=64)
-        ws_scales_raw = held.tile([P, H // 4], I32, name="ws_scales_raw", align_bytes=64)
+        table_scales = held.tile([P, T // 4], I32, name="table_scales", align_bytes=DMA_ALIGN)
+        ws_words_raw = held.tile([P, H // 2], I32, name="ws_words_raw", align_bytes=DMA_ALIGN)
+        ws_scales_raw = held.tile([P, H // 4], I32, name="ws_scales_raw", align_bytes=DMA_ALIGN)
         bias = held.tile([P, N // P], F32, name="bias")
         identity = held.tile([P, P], F32, name="identity")
 

@@ -27,7 +27,8 @@ DMA_ALIGN = 256
 BANKS = 8
 A_BANKS = 3
 EARLY_TURNED = BANKS - A_BANKS
-QUARTER = PASS // 2
+LATE = P
+EARLY = PASS - LATE
 NARROW = P
 WIDE = 2 * P
 
@@ -117,9 +118,9 @@ def tile_list_quadrature_magnitude_mel_kernel(
             load_plane(plane)
         load_wc(0, 0, PASS, "wc_a")
         load_plane(6)
-        load_wc(1, 0, QUARTER, "wc_b")
+        load_wc(1, 0, WIDE, "wc_b")
+        load_wc(1, WIDE, NARROW, "wc_c")
         load_plane(7)
-        load_wc(1, QUARTER, QUARTER, "wc_c")
 
         repeated = buffer("round_x0", [P, S], F32)
         turned = bank(4, [P, J_HALF])
@@ -150,13 +151,13 @@ def tile_list_quadrature_magnitude_mel_kernel(
         nc.vector.tensor_copy(
             out=v_words[1][:], in_=table_words[:].bitcast(U32).indirect(entries(table_list, J_HALF, J_HALF))
         )
-        nc.vector.tensor_copy(
-            out=ws_codes[:].bitcast(I32).rearrange("p (t u) -> p u t", t=PACK),
-            in_=ws_words_raw[:, PASS // 2 :].rearrange("p (u t) -> p u t", t=PACK),
+        nc.scalar.copy(
+            out=ws_codes[:].bitcast(U32).rearrange("p (t u) -> p t u", t=PACK),
+            in_=ws_words_raw[:, PASS // 2 :].bitcast(U32).rearrange("p (u t) -> p t u", t=PACK),
         )
-        nc.vector.tensor_copy(
-            out=ws_scale[:].bitcast(U16).rearrange("p (t u) -> p u t", t=PACK),
-            in_=ws_scales_raw[:, PASS // 4 :].bitcast(U16).rearrange("p (u t) -> p u t", t=PACK),
+        nc.scalar.copy(
+            out=ws_scale[:].bitcast(U16).rearrange("p (t u) -> p t u", t=PACK),
+            in_=ws_scales_raw[:, PASS // 4 :].bitcast(U16).rearrange("p (u t) -> p t u", t=PACK),
         )
 
         def is_turned(unit):
@@ -246,14 +247,16 @@ def tile_list_quadrature_magnitude_mel_kernel(
         def gather_plane(plane):
             gather(plane, 0, S)
 
-        def round_xg(g, j0, width, engine, dst):
-            xg_rounded[g, j0] = dst
-            src = picked_planes[g][:, :, j0 : j0 + width]
+        def interleave(engine, dst, src):
             round_copy(
                 engine,
                 dst.rearrange("p (run d i) -> p run i d", d=RUN, i=PACK),
                 src.rearrange("p i (run d) -> p run i d", d=RUN),
             )
+
+        def round_xg(g, j0, width, engine, dst):
+            xg_rounded[g, j0] = dst
+            interleave(engine, dst, picked_planes[g][:, :, j0 : j0 + width])
 
         def quantize_xg(g, j0, width, codes):
             scales = held.tile([P, width], U8, name="xg_scales%d_%d" % (g, j0), align_bytes=64)
@@ -305,6 +308,8 @@ def tile_list_quadrature_magnitude_mel_kernel(
         picked_planes[0] = buffer("picked0", [P, PACK, S], F32)
         picked_row = buffer("picked1", [P, last_plane + BACK + PASS * PACK // 2], F32)
         picked_planes[1] = picked_row[:, 0 : PACK * S].rearrange("p (i j) -> p i j", i=PACK)
+        late_raw = picked_row[:, last_plane + WIDE : last_plane + WIDE + PACK * LATE].rearrange("p (i r) -> p i r", i=PACK)
+        nc.sync.dma_start(out=late_raw, in_=wc[PASS:, EARLY:PASS].rearrange("(p i) r -> p i r", i=PACK))
         gather(0, 0, J_HALF)
         gather(0, J_HALF, J_HALF)
         load_wc(0, PASS, PASS, "plane0")
@@ -327,19 +332,20 @@ def tile_list_quadrature_magnitude_mel_kernel(
         gather_plane(5)
         quantize_xg(0, 0, J_HALF, held.tile([P, J_HALF], U32, name="xg_codes0", align_bytes=64)[:])
         pass0_rounded = rounded("round_w0", PASS)
-        for bin0 in (0, QUARTER):
-            quarter_raw = wc_raw[0, 0][:, :, bin0 : bin0 + QUARTER]
-            round_wc("scalar", pass0_rounded[:, PACK * bin0 : PACK * (bin0 + QUARTER)], quarter_raw)
+        interleave("scalar", pass0_rounded[:], wc_raw[0, 0][:])
+        quantize_xg(0, J_HALF, J_HALF, held.tile([P, J_HALF], U32, name="xg_codes0_late", align_bytes=64)[:])
         gather_plane(6)
         wc_tiles(0, 0, buffer("plane6", [P, PASS], U32))
         quantize_wc(0, 0, pass0_rounded[:])
         for index in range(A_BANKS):
             multiply_a(index, [0], start=True, stop=False)
-        early_quarter = rounded("round_w1", QUARTER)
-        round_wc("scalar", early_quarter[:], wc_raw[1, 0][:])
+        pass1_rounded = rounded("round_w1", PASS)
+        early_bins, late_bins = pass1_rounded[:, 0 : PACK * EARLY], pass1_rounded[:, PACK * EARLY :]
+        interleave("scalar", early_bins[:, 0 : PACK * WIDE], wc_raw[1, 0][:])
+        interleave("scalar", early_bins[:, PACK * WIDE :], wc_raw[1, WIDE][:])
         for half in range(2):
             wc_tiles(1, half, held.tile([P, PASS], U32, name="wc_codes1%d" % half, align_bytes=64))
-        quantize_wc(1, 0, early_quarter[:], 0, QUARTER)
+        quantize_wc(1, 0, early_bins, 0, EARLY)
 
         tile_tags = ["round_piece0", "round_piece128", "round_piece256", "round_x0"]
 
@@ -347,27 +353,25 @@ def tile_list_quadrature_magnitude_mel_kernel(
             round_xg(1, P * jt, NARROW, "scalar", rounded(tile_tags[jt], NARROW)[:])
 
         gather(7, 0, NARROW)
-        gather(7, NARROW, WIDE)
-        gather(7, NARROW + WIDE, NARROW)
+        gather(7, NARROW, NARROW)
         round_tile(0)
         round_tile(1)
-        late_quarter = picked_row[:, last_plane + J_HALF : PACK * S].bitcast(BF16)
-        round_wc("vector", late_quarter, wc_raw[1, QUARTER][:])
-        quantize_xg(1, 0, NARROW, buffer("wc_c", [P, NARROW], U32)[:])
-        multiply_a(0, [1], start=False, stop=False, bins=slice(0, QUARTER))
-        quantize_wc(1, 0, late_quarter, QUARTER, QUARTER)
+        interleave("vector", late_bins, late_raw)
+        quantize_last(0, NARROW)
+        gather(7, WIDE, NARROW)
+        multiply_a(0, [1], start=False, stop=False, bins=slice(0, WIDE))
+        multiply_a(0, [1], start=False, stop=False, bins=slice(WIDE, EARLY))
+        quantize_wc(1, 0, late_bins, EARLY, LATE)
+        gather(7, 3 * P, NARROW)
         quantize_last(P, NARROW)
         round_tile(2)
         round_tile(3)
         quantize_last(2 * P, NARROW)
-        quantize_last(3 * P, NARROW)
 
         gather(7, J_HALF, WIDE)
+        quantize_last(3 * P, NARROW)
         late = rounded("round_w0", J_HALF)
         round_xg(1, J_HALF, WIDE, "vector", late[:, 0 : PACK * WIDE])
-        xg_rounded[0, BACK] = xg_rounded[0, J_HALF][:, PACK * WIDE :]
-        xg_rounded[0, J_HALF] = xg_rounded[0, J_HALF][:, 0 : PACK * WIDE]
-        quantize_xg(0, J_HALF, WIDE, buffer(tile_tags[2], [P, WIDE], U32)[:])
         quantize_last(J_HALF, WIDE)
         second_half = [rounded("table", PASS)[:], picked_row[:, last_plane + BACK :].bitcast(BF16)]
         round_wc("vector", second_half[0], wc_raw[0, PASS][:])
@@ -389,7 +393,7 @@ def tile_list_quadrature_magnitude_mel_kernel(
             else:
                 a_square[unit] = shared.tile([P, PASS], F32, name="a_square", tag="a_square", bufs=SQUARE_BUFFERS)
             if is_turned(unit):
-                square(a_square[unit], "p (t q w) -> p q t w", a_sums[unit], "p (q t w) -> p q t w", q=2)
+                square(a_square[unit], "p (t u e) -> p t u e", a_sums[unit], "p (u t e) -> p t u e", e=2)
             else:
                 square_direct(a_square[unit], a_sums[unit])
 
@@ -477,7 +481,6 @@ def tile_list_quadrature_magnitude_mel_kernel(
         for step in range(max(mel_step.values()) + 2):
             if step == FRONT_TILES:
                 gather(7, BACK, WIDE)
-                quantize_xg(0, BACK, WIDE, held.tile([P, WIDE], U32, name="xg_codes0_back", align_bytes=64)[:])
             if step == FRONT_TILES + ADD_LAG:
                 round_xg(1, BACK, WIDE, "vector", late[:, PACK * WIDE : PACK * J_HALF])
             if step == FRONT_TILES + ROOT_LAG:
@@ -507,7 +510,7 @@ def tile_list_quadrature_magnitude_mel_kernel(
             if 2 * FRONT_TILES <= step < len(UNITS) - 1 and is_turned(UNITS[step + 1]):
                 turn_b(UNITS[step + 1])
             if step == 0:
-                multiply_a(step, [1], start=False, stop=True, bins=slice(QUARTER, PASS))
+                multiply_a(step, [1], start=False, stop=True, bins=slice(EARLY, PASS))
             elif step < A_BANKS:
                 multiply_a(step, [1], start=False, stop=True)
             elif step < len(UNITS) and step != EARLY_TURNED:

@@ -32,17 +32,17 @@ EARLY = PASS - LATE
 NARROW = P
 WIDE = 2 * P
 
-FRONT_TILES = 6
-BACK = FRONT_TILES * P
-UNITS = [(half, jt) for half in range(2) for jt in range(FRONT_TILES)]
-UNITS = UNITS + [(half, jt) for jt in range(FRONT_TILES, S // P) for half in (1, 0)]
-SUM_BANK = [A_BANKS + jt for jt in range(EARLY_TURNED)] + [A_BANKS, A_BANKS, 5]
+UNITS = [(0, jt) for jt in range(EARLY_TURNED)] + [(1, 0), (0, 5), (1, 1), (1, 2), (1, 3), (1, 4), (1, 5)]
+UNITS = UNITS + [(1, 6), (0, 6), (1, 7), (0, 7)]
+A_BANK = [0, 1, 2, 0, 1, 2, 0, 1, 2, 3, 0, 4, 1, 2, 0, 1]
+SUM_BANK = [3, 4, 5, 6, 7, 6, 3, 4]
+BACK = 6 * P
 OUT_PIECES = [
     (0, WIDE, (5,), ("vector",)),
-    (WIDE, WIDE, (6,), ("vector",)),
-    (2 * WIDE, WIDE, (2,), ("vector",)),
-    (BACK, NARROW, (4,), ("scalar",)),
-    (BACK + NARROW, NARROW, (7, 6), ("scalar", "vector")),
+    (WIDE, WIDE, (7,), ("vector",)),
+    (2 * WIDE, WIDE, (6,), ("vector",)),
+    (BACK, NARROW, (5,), ("scalar",)),
+    (BACK + NARROW, NARROW, (7, 2), ("scalar", "vector")),
 ]
 SQUARE_LAG, ADD_LAG, ROOT_LAG = 1, 2, 3
 SQUARE_BUFFERS = 4
@@ -147,10 +147,9 @@ def tile_list_quadrature_magnitude_mel_kernel(
             return lists[:, j0 // ROW : (j0 + width) // ROW]
 
         nc.vector.tensor_copy(out=v_scales[:], in_=table_scales[:].bitcast(U8).indirect(table_list[:]))
-        nc.vector.tensor_copy(out=v_words[0][:], in_=table_words[:].bitcast(U32).indirect(entries(table_list, 0, J_HALF)))
-        nc.vector.tensor_copy(
-            out=v_words[1][:], in_=table_words[:].bitcast(U32).indirect(entries(table_list, J_HALF, J_HALF))
-        )
+        for part in range(2):
+            picks = table_words[:].bitcast(U32).indirect(entries(table_list, J_HALF * part, J_HALF))
+            nc.vector.tensor_copy(out=v_words[part][:], in_=picks)
         nc.scalar.copy(
             out=ws_codes[:].bitcast(U32).rearrange("p (t u) -> p t u", t=PACK),
             in_=ws_words_raw[:, PASS // 2 :].bitcast(U32).rearrange("p (u t) -> p t u", t=PACK),
@@ -163,15 +162,22 @@ def tile_list_quadrature_magnitude_mel_kernel(
         def is_turned(unit):
             return unit[0] == 0
 
+        def places(unit):
+            return (P * unit[1], NARROW) if is_turned(unit) else (WIDE * (unit[1] // 2), WIDE)
+
         def product(unit, sums, passes, start, stop, bins=slice(0, PASS)):
-            groups = [bins] if is_turned(unit) else [slice(P * t, P * (t + 1)) for t in range(PACK)]
-            for cols in groups:
+            if is_turned(unit):
+                groups = [(bins, bins)]
+            else:
+                t0 = 2 * (unit[1] % 2)
+                groups = [(slice(P * (t0 + t), P * (t0 + t + 1)), slice(WIDE * t, WIDE * (t + 1))) for t in range(2)]
+            for cols, written in groups:
                 for order, (w_codes, w_scales, per_col, w_dtype, codes, scales) in enumerate(passes):
                     weight = (w_codes[:, per_col * cols.start : per_col * cols.stop].bitcast(w_dtype), w_scales[:, cols])
                     picked = (codes.bitcast(FP8X4), scales)
                     still, moving = (picked, weight) if is_turned(unit) else (weight, picked)
                     nc.tensor.matmul_mx(
-                        out=sums[:, cols],
+                        out=sums[:, written],
                         lhsT=still[0],
                         lhsT_scale=still[1],
                         rhs=moving[0],
@@ -180,15 +186,12 @@ def tile_list_quadrature_magnitude_mel_kernel(
                         stop=stop and order == len(passes) - 1,
                     )
 
-        def square(dst, dst_order, sums, sums_order, **sizes):
-            nc.scalar.activation(
-                out=dst[:].rearrange(dst_order, t=PACK, **sizes),
-                in_=sums[:].rearrange(sums_order, t=PACK, **sizes),
-                func=ACT.Square,
-            )
-
-        def square_direct(dst, sums):
-            square(dst, "p (j t) -> p j t", sums, "p (t j) -> p j t")
+        def square(unit, dst, sums):
+            if is_turned(unit):
+                dst, sums = dst.rearrange("p (t u e) -> p t u e", t=PACK, e=2), sums.rearrange("p (u t e) -> p t u e", t=PACK, e=2)
+            else:
+                dst, sums = dst.rearrange("p (j t) -> p j t", t=2), sums.rearrange("p (t j) -> p j t", t=2)
+            nc.scalar.activation(out=dst, in_=sums, func=ACT.Square)
 
         def turn(unit, squares, start):
             for t in range(PACK):
@@ -207,33 +210,40 @@ def tile_list_quadrature_magnitude_mel_kernel(
             turn(unit, b_square[unit], start=True)
 
         b_square, turned_sum = {}, {}
+        pair_sums = [buffer("pair_sums%d" % pair, [P, 2, PASS], F32) for pair in range(S // WIDE)]
         b_order = [(half, jt0 + jt) for jt0 in (0, J_HALF // P) for half in range(2) for jt in range(J_HALF // P)]
         for serial, unit in enumerate(b_order):
-            half, jt = unit
             sums = bank(serial % BANKS, [P, PASS])
-            j_in_half = P * jt % J_HALF
+            j0, width = places(unit)
             ws_pass = (
                 ws_words_raw[:, 0 : PASS // 2].bitcast(U8) if is_turned(unit) else ws_codes[:],
                 ws_scales_raw[:, 0 : PASS // 4].bitcast(U8) if is_turned(unit) else ws_scale[:],
                 2,
                 FP4X4,
-                v_words[P * jt // J_HALF][:, j_in_half : j_in_half + P],
-                v_scales[:, P * jt : P * (jt + 1)],
+                v_words[j0 // J_HALF][:, j0 % J_HALF : j0 % J_HALF + width],
+                v_scales[:, j0 : j0 + width],
             )
             product(unit, sums, [ws_pass], start=True, stop=True)
-            b_square[unit] = buffer("b_square%d%d" % unit, [P, PASS], F32)
             if is_turned(unit):
-                square(b_square[unit], "p (t u e) -> p t u e", sums, "p (u t e) -> p t u e", e=2)
+                b_square[unit] = buffer("b_square%d" % unit[1], [P, PASS], F32)[:]
             else:
-                square_direct(b_square[unit], sums)
+                b_square[unit] = pair_sums[unit[1] // 2][:, unit[1] % 2, :]
+            square(unit, b_square[unit], sums[:])
         for unit in UNITS[:EARLY_TURNED]:
             turn_b(unit)
 
         picked_planes, xg_rounded = {}, {}
-        xg_codes, wc_codes = {}, {}
-        xg_scales, wc_scales = {}, {}
+        xg_codes, xg_scales, wc_codes, wc_scales = {}, {}, {}, {}
         wm_codes = held.tile([P, 2, N], U32, name="wm_codes", align_bytes=64)
         wm_scales = held.tile([P, 2, N], U8, name="wm_scales", align_bytes=64)
+        for g in range(2):
+            for pair in range(S // WIDE):
+                if g == 1 or pair % 2 == 0:
+                    width = WIDE if g == 1 else J_HALF
+                    codes = held.tile([P, width], U32, name="xg_codes%d_%d" % (g, pair), align_bytes=64)
+                    scales = held.tile([P, width], U8, name="xg_scales%d_%d" % (g, pair), align_bytes=64)
+                    for j in range(0, width, P):
+                        xg_codes[g, WIDE * pair + j], xg_scales[g, WIDE * pair + j] = codes[:, j:width], scales[:, j:width]
 
         def rounded(tag, width):
             return buffer(tag, [P, width * PACK], BF16)
@@ -243,9 +253,6 @@ def tile_list_quadrature_magnitude_mel_kernel(
             dst = picked_planes[g][:, i, j0 : j0 + width]
             picks = x_plane[plane][:].indirect(entries(frame_lists, j0, width))
             nc.vector.tensor_tensor(dst, picks, weights[:, j0 : j0 + width], ALU.mult)
-
-        def gather_plane(plane):
-            gather(plane, 0, S)
 
         def interleave(engine, dst, src):
             round_copy(
@@ -258,21 +265,13 @@ def tile_list_quadrature_magnitude_mel_kernel(
             xg_rounded[g, j0] = dst
             interleave(engine, dst, picked_planes[g][:, :, j0 : j0 + width])
 
-        def quantize_xg(g, j0, width, codes):
-            scales = held.tile([P, width], U8, name="xg_scales%d_%d" % (g, j0), align_bytes=64)
-            nc.vector.quantize_mx(out=codes.bitcast(FP8X4), scales=scales[:], in_=xg_rounded[g, j0])
-            for j in range(0, width, P):
-                xg_codes[g, (j0 + j) // P] = codes[:, j : j + P]
-                xg_scales[g, (j0 + j) // P] = scales[:, j : j + P]
+        def quantize_xg(g, j0, width):
+            codes, scales = xg_codes[g, j0][:, 0:width], xg_scales[g, j0][:, 0:width]
+            nc.vector.quantize_mx(out=codes.bitcast(FP8X4), scales=scales, in_=xg_rounded[g, j0])
 
-        def quantize_last(j0, width):
-            codes = held.tile([P, width], U32, name="xg_codes1_%d" % j0, align_bytes=64)
-            quantize_xg(1, j0, width, codes[:])
-
-        def round_wc(engine, dst, src, t0=0, t1=PACK):
-            src = src.rearrange("p i (u t e) -> p u t i e", t=PACK, e=2)
-            dst = dst.rearrange("p (t u e i) -> p u t i e", t=PACK, e=2, i=PACK)
-            round_copy(engine, dst[:, :, t0:t1], src[:, :, t0:t1])
+        def round_wc(g, t0, dst):
+            src = wc_raw[g, PASS][:].rearrange("p i (u t e) -> p u t i e", t=PACK, e=2)
+            nc.vector.tensor_copy(out=dst.rearrange("p (t u e i) -> p u t i e", t=2, e=2, i=PACK), in_=src[:, :, t0 : t0 + 2])
 
         def wc_tiles(g, half, codes):
             wc_codes[g, half] = codes[:]
@@ -287,35 +286,34 @@ def tile_list_quadrature_magnitude_mel_kernel(
 
         def prepare_wm(half, tag):
             wm_rounded = buffer(tag, [P, N * PACK], BF16)
-            nc.vector.tensor_copy(
-                out=wm_rounded[:].rearrange("p (run d t) -> p run t d", d=RUN, t=PACK),
-                in_=wm_raw[:, half, :, :].rearrange("p t (run d) -> p run t d", d=RUN),
-            )
+            interleave("vector", wm_rounded[:], wm_raw[:, half, :, :])
             nc.vector.quantize_mx(out=wm_codes[:, half, :].bitcast(FP8X4), scales=wm_scales[:, half, :], in_=wm_rounded[:])
 
         a_sums, a_square = {}, {}
 
         def multiply_a(index, passes, start, stop, bins=slice(0, PASS)):
-            unit = half, jt = UNITS[index]
+            unit = UNITS[index]
+            j0, width = places(unit)
             if start:
-                a_sums[unit] = bank(index % A_BANKS, [P, PASS])
+                a_sums[unit] = bank(A_BANK[index], [P, PASS])
             operands = [
-                (wc_codes[g, half], wc_scales[g, half], 1, FP8X4, xg_codes[g, jt], xg_scales[g, jt]) for g in passes
+                (wc_codes[g, unit[0]], wc_scales[g, unit[0]], 1, FP8X4, xg_codes[g, j0][:, 0:width], xg_scales[g, j0][:, 0:width])
+                for g in passes
             ]
             product(unit, a_sums[unit], operands, start, stop, bins)
 
         last_plane = (PACK - 1) * S
         picked_planes[0] = buffer("picked0", [P, PACK, S], F32)
-        picked_row = buffer("picked1", [P, last_plane + BACK + PASS * PACK // 2], F32)
+        picked_row = buffer("picked1", [P, last_plane + BACK + PASS], F32)
         picked_planes[1] = picked_row[:, 0 : PACK * S].rearrange("p (i j) -> p i j", i=PACK)
         late_raw = picked_row[:, last_plane + WIDE : last_plane + WIDE + PACK * LATE].rearrange("p (i r) -> p i r", i=PACK)
         nc.sync.dma_start(out=late_raw, in_=wc[PASS:, EARLY:PASS].rearrange("(p i) r -> p i r", i=PACK))
         gather(0, 0, J_HALF)
         gather(0, J_HALF, J_HALF)
         load_wc(0, PASS, PASS, "plane0")
-        gather_plane(1)
+        gather(1, 0, S)
         load_wc(1, PASS, PASS, "plane1")
-        gather_plane(2)
+        gather(2, 0, S)
         wm_raw = buffer("plane2", [P, 2, PACK, N], F32)
         wm_rows = wm.rearrange("(half u t e) n -> half e u t n", half=2, t=PACK, e=2)
         for half in range(2):
@@ -323,18 +321,16 @@ def tile_list_quadrature_magnitude_mel_kernel(
                 nc.sync.dma_start(out=wm_raw[e:P:2, half, :, :], in_=wm_rows[half, e])
         with nc.allow_non_contiguous_dma(reason="band 128 c + p's bias goes to partition p, column c"):
             nc.sync.dma_start(out=bias[:], in_=bm.rearrange("(c p) -> p c", p=P))
-        gather(3, 0, J_HALF)
-        round_xg(0, 0, J_HALF, "scalar", rounded("round_x0", J_HALF)[:])
-        gather(3, J_HALF, J_HALF)
-        round_xg(0, J_HALF, J_HALF, "scalar", rounded("round_x1", J_HALF)[:])
-
-        gather_plane(4)
-        gather_plane(5)
-        quantize_xg(0, 0, J_HALF, held.tile([P, J_HALF], U32, name="xg_codes0", align_bytes=64)[:])
+        for part in range(2):
+            gather(3, J_HALF * part, J_HALF)
+            round_xg(0, J_HALF * part, J_HALF, "scalar", rounded("round_x%d" % part, J_HALF)[:])
+        gather(4, 0, S)
+        gather(5, 0, S)
+        quantize_xg(0, 0, J_HALF)
         pass0_rounded = rounded("round_w0", PASS)
         interleave("scalar", pass0_rounded[:], wc_raw[0, 0][:])
-        quantize_xg(0, J_HALF, J_HALF, held.tile([P, J_HALF], U32, name="xg_codes0_late", align_bytes=64)[:])
-        gather_plane(6)
+        quantize_xg(0, J_HALF, J_HALF)
+        gather(6, 0, S)
         wc_tiles(0, 0, buffer("plane6", [P, PASS], U32))
         quantize_wc(0, 0, pass0_rounded[:])
         for index in range(A_BANKS):
@@ -357,67 +353,73 @@ def tile_list_quadrature_magnitude_mel_kernel(
         round_tile(0)
         round_tile(1)
         interleave("vector", late_bins, late_raw)
-        quantize_last(0, NARROW)
+        quantize_xg(1, 0, NARROW)
         gather(7, WIDE, NARROW)
         multiply_a(0, [1], start=False, stop=False, bins=slice(0, WIDE))
         multiply_a(0, [1], start=False, stop=False, bins=slice(WIDE, EARLY))
         quantize_wc(1, 0, late_bins, EARLY, LATE)
         gather(7, 3 * P, NARROW)
-        quantize_last(P, NARROW)
+        quantize_xg(1, P, NARROW)
         round_tile(2)
         round_tile(3)
-        quantize_last(2 * P, NARROW)
-
+        quantize_xg(1, 2 * P, NARROW)
         gather(7, J_HALF, WIDE)
-        quantize_last(3 * P, NARROW)
+        quantize_xg(1, 3 * P, NARROW)
         late = rounded("round_w0", J_HALF)
         round_xg(1, J_HALF, WIDE, "vector", late[:, 0 : PACK * WIDE])
-        quantize_last(J_HALF, WIDE)
-        second_half = [rounded("table", PASS)[:], picked_row[:, last_plane + BACK :].bitcast(BF16)]
-        round_wc("vector", second_half[0], wc_raw[0, PASS][:])
+        quantize_xg(1, J_HALF, WIDE)
         wc_tiles(0, 1, held.tile([P, PASS], U32, name="wc_codes01", align_bytes=64))
-        quantize_wc(0, 1, second_half[0])
         for t0 in (0, 2):
-            round_wc("vector", second_half[1], wc_raw[1, PASS][:], t0, t0 + 2)
-        for t0 in (0, 2):
-            quantize_wc(1, 1, second_half[1][:, PASS * t0 : PASS * (t0 + 2)], P * t0, 2 * P)
+            if t0 == 0:
+                parts = [rounded("table", WIDE)[:], rounded("round_x1", WIDE)[:]]
+            else:
+                parts = [rounded("round_x1", WIDE)[:], picked_row[:, last_plane + BACK :].bitcast(BF16)]
+            for g in range(2):
+                round_wc(g, t0, parts[g])
+            for g in range(2):
+                quantize_wc(g, 1, parts[g], P * t0, 2 * P)
 
         h_rounded = [buffer(tag, [P, S * PACK], BF16) for tag in ("plane3", "plane4")]
         h_codes, h_scales = {}, {}
         results = buffer("plane5", [P, N // P * S], F32)
         mel_sums = {}
+        own_tag = {(1, 0): "b_square0", (1, 1): "b_square1", (1, 2): "b_square2", (1, 3): "b_square3", (1, 4): "wc_c"}
+        own_tag.update({(1, 6): "wc_b", (1, 7): "wc_a"})
+        code_tag = {(0, 0): "b_square1", (0, J_HALF): "b_square3", (1, 0): "wc_c"}
+        result_tag = {0: "wc_b", WIDE: "wc_a"}
 
         def square_a(unit):
-            if unit == UNITS[FRONT_TILES]:
-                a_square[unit] = buffer("first_direct", [P, PASS], F32)
+            if unit in own_tag:
+                a_square[unit] = buffer(own_tag[unit], [P, PASS], F32)
             else:
                 a_square[unit] = shared.tile([P, PASS], F32, name="a_square", tag="a_square", bufs=SQUARE_BUFFERS)
-            if is_turned(unit):
-                square(a_square[unit], "p (t u e) -> p t u e", a_sums[unit], "p (u t e) -> p t u e", e=2)
-            else:
-                square_direct(a_square[unit], a_sums[unit])
+            square(unit, a_square[unit][:], a_sums[unit][:])
 
         def add_squares(unit):
             if is_turned(unit):
                 turn(unit, a_square[unit], start=False)
             else:
-                nc.vector.tensor_tensor(b_square[unit][:], a_square[unit][:], b_square[unit][:], ALU.add)
+                nc.vector.tensor_tensor(b_square[unit], a_square[unit][:], b_square[unit], ALU.add)
 
-        def root(unit):
-            half, jt = unit
-            dst = h_rounded[half][:, PASS * jt : PASS * (jt + 1)]
-            if is_turned(unit):
+        def root(half, j0, width):
+            dst = h_rounded[half][:, PACK * j0 : PACK * (j0 + width)]
+            if half == 0:
                 nc.scalar.activation(
                     out=dst.rearrange("p (j t) -> p j t", t=PACK),
-                    in_=turned_sum[unit][:].rearrange("p (t j) -> p j t", t=PACK),
+                    in_=turned_sum[0, j0 // P][:].rearrange("p (t j) -> p j t", t=PACK),
                     func=ACT.Sqrt,
                 )
             else:
-                nc.scalar.activation(out=dst, in_=b_square[unit][:], func=ACT.Sqrt)
+                sums = pair_sums[j0 // WIDE][:].rearrange("p h (j t) -> p j h t", t=2)
+                nc.scalar.activation(
+                    out=dst.rearrange("p (j h t) -> p j h t", h=2, t=2),
+                    in_=sums[:, j0 % WIDE : j0 % WIDE + width],
+                    func=ACT.Sqrt,
+                )
 
         def quantize_h(half, j0, width):
-            if (half, j0) == (0, 0):
-                codes = buffer("b_square%d%d" % UNITS[FRONT_TILES], [P, width], U32)
+            if (half, j0) in code_tag:
+                codes = buffer(code_tag[half, j0], [P, width], U32)
             else:
                 codes = held.tile([P, width], U32, name="h_codes%d_%d" % (half, j0), align_bytes=64)
             scales = held.tile([P, width], U8, name="h_scales%d_%d" % (half, j0), align_bytes=64)
@@ -455,7 +457,10 @@ def tile_list_quadrature_magnitude_mel_kernel(
                 nc.vector.tensor_tensor(result, sums[:], bias[:].unsqueeze(2).to_broadcast(list(result.shape)), ALU.add)
 
         def store(j0, width, engines):
-            result = results[:, N // P * j0 : N // P * (j0 + width)].rearrange("p (c j) -> p c j", j=width)
+            if j0 in result_tag:
+                result = buffer(result_tag[j0], [P, N // P, width], F32)[:]
+            else:
+                result = results[:, N // P * j0 : N // P * (j0 + width)].rearrange("p (c j) -> p c j", j=width)
             rows = out.rearrange("(c p) j -> p c j", p=P)[:, :, j0 : j0 + width]
             count = N // P // len(engines)
             for part, engine in enumerate(engines):
@@ -466,55 +471,68 @@ def tile_list_quadrature_magnitude_mel_kernel(
             else:
                 nc.sync.dma_start(out=rows, in_=result)
 
-        def after_root(half, j_end):
-            return UNITS.index((half, j_end // P - 1)) + ROOT_LAG + 1
+        def finish(piece, closing):
+            j0, width, banks, engines = OUT_PIECES[piece]
+            multiply_mel(j0, width, banks, 1 - closing, opens=True)
+            quantize_h(closing, j0, width)
+            multiply_mel(j0, width, banks, closing, opens=False)
 
-        closing, code_step, mel_step = {}, {}, {}
-        for j0, width, banks, engines in OUT_PIECES:
-            closing[j0] = 1 if j0 < BACK else 0
-            code_step[j0] = after_root(closing[j0], j0 + width)
-            last_user = max([index for index in range(len(UNITS)) if index % A_BANKS == banks[0]] + [0])
-            mel_step[j0] = max(code_step[j0], last_user + SQUARE_LAG + 1) if banks[0] < A_BANKS else code_step[j0]
-        wm_step = [after_root(1, P * (half + 1)) for half in range(2)]
-        opening_codes = [(0, 0, J_HALF, wm_step[0]), (0, J_HALF, WIDE, wm_step[1])]
-        opening_codes = opening_codes + [(1, j0, NARROW, after_root(1, j0 + NARROW)) for j0 in range(BACK, S, P)]
-        for step in range(max(mel_step.values()) + 2):
-            if step == FRONT_TILES:
+        step_of = {unit: index for index, unit in enumerate(UNITS)}
+        last_pair = S // WIDE - 1
+        for step in range(len(UNITS) + ROOT_LAG + 1):
+            if step == step_of[1, 1]:
                 gather(7, BACK, WIDE)
-            if step == FRONT_TILES + ADD_LAG:
+            if step == step_of[1, 2]:
                 round_xg(1, BACK, WIDE, "vector", late[:, PACK * WIDE : PACK * J_HALF])
-            if step == FRONT_TILES + ROOT_LAG:
-                quantize_xg(1, BACK, WIDE, buffer("first_direct", [P, WIDE], U32)[:])
-            for half in range(2):
-                if step == wm_step[half]:
-                    prepare_wm(half, "b_square%d%d" % UNITS[FRONT_TILES + half])
+            if step == step_of[1, 2]:
+                quantize_xg(1, BACK, WIDE)
             if step == EARLY_TURNED:
-                multiply_a(step, [0, 1], start=True, stop=True)
-            if step == EARLY_TURNED + 1:
-                turn_b(UNITS[EARLY_TURNED])
-            if 0 <= step - ADD_LAG < len(UNITS):
                 add_squares(UNITS[step - ADD_LAG])
-            for half, j0, width, at in opening_codes:
-                if step == at:
-                    quantize_h(half, j0, width)
-            for j0, width, banks, engines in OUT_PIECES:
-                if step == mel_step[j0]:
-                    multiply_mel(j0, width, banks, 1 - closing[j0], opens=True)
-                if step == code_step[j0]:
-                    quantize_h(closing[j0], j0, width)
-                if step == mel_step[j0]:
-                    multiply_mel(j0, width, banks, closing[j0], opens=False)
-            for j0, width, banks, engines in OUT_PIECES:
-                if step == mel_step[j0] + 1:
-                    store(j0, width, engines)
-            if 2 * FRONT_TILES <= step < len(UNITS) - 1 and is_turned(UNITS[step + 1]):
-                turn_b(UNITS[step + 1])
-            if step == 0:
+            if A_BANKS <= step < len(UNITS):
+                multiply_a(step, [0, 1], start=True, stop=True)
+            elif step == 0:
                 multiply_a(step, [1], start=False, stop=True, bins=slice(EARLY, PASS))
             elif step < A_BANKS:
                 multiply_a(step, [1], start=False, stop=True)
-            elif step < len(UNITS) and step != EARLY_TURNED:
-                multiply_a(step, [0, 1], start=True, stop=True)
-            for lag, stage in ((SQUARE_LAG, square_a), (ROOT_LAG, root)):
-                if 0 <= step - lag < len(UNITS):
-                    stage(UNITS[step - lag])
+            if EARLY_TURNED <= step < len(UNITS) and is_turned(UNITS[step]):
+                turn_b(UNITS[step])
+            if 0 <= step - ADD_LAG < len(UNITS) and step != EARLY_TURNED:
+                add_squares(UNITS[step - ADD_LAG])
+            if 0 <= step - SQUARE_LAG < len(UNITS):
+                square_a(UNITS[step - SQUARE_LAG])
+            if 0 <= step - ROOT_LAG < len(UNITS):
+                half, serial = UNITS[step - ROOT_LAG]
+                if half == 0:
+                    root(0, P * serial, NARROW)
+                elif serial % 2 == 1 and serial // 2 < last_pair:
+                    root(1, WIDE * (serial // 2), WIDE)
+                elif serial % 2 == 1:
+                    root(1, BACK, NARROW)
+                    root(1, BACK + NARROW, NARROW)
+            done = UNITS[step - ROOT_LAG] if 0 <= step - ROOT_LAG < len(UNITS) else None
+            if step == step_of[1, 0] + ADD_LAG:
+                prepare_wm(0, "b_square0")
+            if step == step_of[1, 1] + ADD_LAG:
+                quantize_h(0, 0, J_HALF)
+            if step == step_of[1, 2] + ADD_LAG:
+                prepare_wm(1, "b_square2")
+            if step == step_of[1, 3] + ADD_LAG:
+                quantize_h(0, J_HALF, WIDE)
+            if step == step_of[1, 4] + ADD_LAG:
+                finish(0, 1)
+            if step == step_of[1, 5] + ADD_LAG:
+                finish(1, 1)
+            if done == (1, 5):
+                finish(2, 1)
+            for piece, unit in enumerate(((1, 6), (1, 7), (1, 7))):
+                if step == step_of[unit] + ADD_LAG:
+                    store(OUT_PIECES[piece][0], WIDE, OUT_PIECES[piece][3])
+            if done == (0, 6):
+                quantize_h(0, BACK, NARROW)
+            if done == (1, 7):
+                finish(3, 1)
+                store(BACK, NARROW, OUT_PIECES[3][3])
+                quantize_h(1, BACK + NARROW, NARROW)
+            if done == (0, 7):
+                finish(4, 0)
+                store(BACK + NARROW, NARROW, OUT_PIECES[4][3])

@@ -308,8 +308,7 @@ def tile_list_quadrature_magnitude_mel_kernel(
         picked_planes[1] = picked_row[:, 0 : PACK * S].rearrange("p (i j) -> p i j", i=PACK)
         late_raw = picked_row[:, last_plane + WIDE : last_plane + WIDE + PACK * LATE].rearrange("p (i r) -> p i r", i=PACK)
         nc.sync.dma_start(out=late_raw, in_=wc[PASS:, EARLY:PASS].rearrange("(p i) r -> p i r", i=PACK))
-        gather(0, 0, J_HALF)
-        gather(0, J_HALF, J_HALF)
+        gather(0, 0, S)
         load_wc(0, PASS, PASS, "plane0")
         gather(1, 0, S)
         load_wc(1, PASS, PASS, "plane1")
@@ -465,11 +464,7 @@ def tile_list_quadrature_magnitude_mel_kernel(
             count = N // P // len(engines)
             for part, engine in enumerate(engines):
                 add_bias(engine, result[:, count * part : count * (part + 1), :], mel_sums[j0][part], count * part, count)
-            if count == 1:
-                for c in range(N // P):
-                    nc.sync.dma_start(out=rows[:, c, :], in_=result[:, c, :])
-            else:
-                nc.sync.dma_start(out=rows, in_=result)
+            nc.sync.dma_start(out=rows, in_=result)
 
         def finish(piece, closing):
             j0, width, banks, engines = OUT_PIECES[piece]

from contextlib import ExitStack

import concourse.mybir as mybir
from concourse.masks import make_identity

KC, KS, H, N, T, S = 1024, 512, 1024, 256, 2048, 1024
FLOPS = 2 * S * H * (KC + KS + N)

F32 = mybir.dt.float32
BF16 = mybir.dt.bfloat16
I32 = mybir.dt.int32
U32 = mybir.dt.uint32
U16 = mybir.dt.uint16
U8 = mybir.dt.uint8
FP8X4 = mybir.dt.float8_e4m3fn_x4
FP4X4 = mybir.dt.float4_e2m1fn_x4
ACT = mybir.ActivationFunctionType
ALU = mybir.AluOpType

P = 128
PACK = 4
PASS = P * PACK
ROW = 16
RUN = 2
J_HALF = S // 2
DMA_ALIGN = 256
BANKS = 8
A_BANKS = 3
EARLY_TURNED = BANKS - A_BANKS
LATE = P
EARLY = PASS - LATE
NARROW = P
WIDE = 2 * P

UNITS = [(0, jt) for jt in range(EARLY_TURNED)] + [(1, 0), (0, 5), (1, 1), (1, 2), (1, 3), (1, 4), (1, 5)]
UNITS = UNITS + [(1, 6), (0, 6), (1, 7), (0, 7)]
A_BANK = [0, 1, 2, 0, 1, 2, 0, 1, 2, 3, 0, 4, 1, 2, 0, 1]
SUM_BANK = [3, 4, 5, 6, 7, 6, 3, 4]
BACK = 6 * P
OUT_PIECES = [
    (0, WIDE, (5,), ("vector",)),
    (WIDE, WIDE, (7,), ("vector",)),
    (2 * WIDE, WIDE, (6,), ("vector",)),
    (BACK, NARROW, (5,), ("scalar",)),
    (BACK + NARROW, NARROW, (7, 2), ("scalar", "vector")),
]
SQUARE_LAG, ADD_LAG, ROOT_LAG = 1, 2, 3
SQUARE_BUFFERS = 4


def tile_list_quadrature_magnitude_mel_kernel(
    tc, xT, wgt, offs2, tab_words, tab_scales, offs, wc, ws_words, ws_scales, wm, bm, out
):
    nc = tc.nc
    with ExitStack() as ctx:
        held = ctx.enter_context(tc.tile_pool(name="held", bufs=1))
        shared = ctx.enter_context(tc.tile_pool(name="shared", bufs=1))
        psum = ctx.enter_context(tc.psum_pool(name="psum", bufs=1))

        def buffer(tag, shape, dtype):
            return shared.tile(shape, dtype, name=tag, tag=tag, bufs=1, align_bytes=DMA_ALIGN)

        def bank(number, shape):
            return psum.tile(shape, F32, name="bank%d" % number, tag="bank%d" % number, bufs=1)

        def round_copy(engine, dst, src):
            if engine == "vector":
                nc.vector.tensor_copy(out=dst, in_=src)
            else:
                nc.scalar.copy(out=dst, in_=src)

        def load_scale_rows(dst, rows):
            for row in range(4):
                nc.sync.dma_start(out=dst[row:P:32, :], in_=rows[row:16:4, :].bitcast(I32))

        def load_plane(plane):
            g, i = divmod(plane, PACK)
            rows = xT[PASS * g : PASS * (g + 1), :].rearrange("(p i) t -> p i t", i=PACK)
            x_plane[plane] = buffer("plane%d" % plane, [P, T], F32)
            nc.sync.dma_start(out=x_plane[plane][:], in_=rows[:, i, :])

        def load_wc(g, bin0, bins, tag):
            block = wc[PASS * g : PASS * (g + 1), bin0 : bin0 + bins]
            wc_raw[g, bin0] = buffer(tag, [P, PACK, bins], F32)
            nc.sync.dma_start(out=wc_raw[g, bin0][:], in_=block.rearrange("(p i) r -> p i r", i=PACK))

        x_plane, wc_raw = {}, {}
        table_list = held.tile([P, S // ROW], U16, name="table_list")
        frame_lists = held.tile([P, S // ROW], U16, name="frame_lists")
        weights = held.tile([P, S], F32, name="weights")
        table_words = buffer("table", [P, T], I32)
        table_scales = held.tile([P, T // 4], I32, name="table_scales", align_bytes=DMA_ALIGN)
        ws_words_raw = held.tile([P, H // 2], I32, name="ws_words_raw", align_bytes=DMA_ALIGN)
        ws_scales_raw = held.tile([P, H // 4], I32, name="ws_scales_raw", align_bytes=DMA_ALIGN)
        bias = held.tile([P, N // P], F32, name="bias")
        identity = held.tile([P, P], F32, name="identity")

        warm_in = held.tile([P, 1], F32, name="warm_in")
        warm_out = held.tile([P, 1], F32, name="warm_out")
        nc.vector.memset(warm_in[:], 1.0)
        nc.scalar.activation(out=warm_out[:], in_=warm_in[:], func=ACT.Sqrt)

        group_rows = buffer("picked1", [P, J_HALF], F32)
        nc.gpsimd.memset(table_scales[:], 0)
        nc.vector.memset(group_rows[:], 0.0)
        nc.vector.memset(ws_scales_raw[:], 0)
        make_identity(nc, identity[:])

        nc.sync.dma_start(table_list[:], offs)
        nc.sync.dma_start(out=ws_words_raw[:], in_=ws_words[0].bitcast(I32))
        load_scale_rows(table_scales, tab_scales[0])
        half_rows = wgt.rearrange("p (part j) -> (p part) j", part=2)
        nc.sync.dma_start(out=group_rows[4:P:8, :], in_=half_rows[0 : 2 * P : ROW + 1, :])
        nc.sync.dma_start(out=table_words[:], in_=tab_words[0].rearrange("p t i -> p (t i)").bitcast(I32))
        nc.sync.dma_start(frame_lists[:], offs2)
        load_scale_rows(ws_scales_raw, ws_scales[0])
        for plane in range(6):
            load_plane(plane)
        load_wc(0, 0, PASS, "wc_a")
        load_plane(6)
        load_wc(1, 0, WIDE, "wc_b")
        load_wc(1, WIDE, NARROW, "wc_c")
        load_plane(7)

        repeated = buffer("round_x0", [P, S], F32)
        turned = bank(4, [P, J_HALF])
        for j0 in range(0, J_HALF, P):
            nc.tensor.transpose(turned[:, j0 : j0 + P], group_rows[:, j0 : j0 + P], identity[:])
        for part in range(2):
            nc.scalar.copy(
                out=repeated[:, J_HALF * part : J_HALF * (part + 1)].rearrange("p (column x) -> p column x", x=ROW),
                in_=turned[:, 8 * part + 4 : J_HALF : ROW].unsqueeze(2).to_broadcast([P, J_HALF // ROW, ROW]),
            )
        for part in range(2):
            turned = bank(6 + part, [P, J_HALF])
            for j0 in range(0, J_HALF, P):
                j = J_HALF * part + j0
                nc.tensor.transpose(turned[:, j0 : j0 + P], repeated[:, j : j + P], identity[:])
            nc.scalar.copy(out=weights[:, J_HALF * part : J_HALF * (part + 1)], in_=turned[:])

        v_scales = held.tile([P, S], U8, name="v_scales", align_bytes=64)
        ws_codes = held.tile([P, 2 * PASS], U8, name="ws_codes", align_bytes=64)
        ws_scale = held.tile([P, PASS], U8, name="ws_scale", align_bytes=64)
        v_words = [held.tile([P, J_HALF], U32, name="v_words%d" % part, align_bytes=64) for part in range(2)]

        def entries(lists, j0, width):
            return lists[:, j0 // ROW : (j0 + width) // ROW]

        nc.vector.tensor_copy(out=v_scales[:], in_=table_scales[:].bitcast(U8).indirect(table_list[:]))
        for part in range(2):
            picks = table_words[:].bitcast(U32).indirect(entries(table_list, J_HALF * part, J_HALF))
            nc.vector.tensor_copy(out=v_words[part][:], in_=picks)
        nc.scalar.copy(
            out=ws_codes[:].bitcast(U32).rearrange("p (t u) -> p t u", t=PACK),
            in_=ws_words_raw[:, PASS // 2 :].bitcast(U32).rearrange("p (u t) -> p t u", t=PACK),
        )
        nc.scalar.copy(
            out=ws_scale[:].bitcast(U16).rearrange("p (t u) -> p t u", t=PACK),
            in_=ws_scales_raw[:, PASS // 4 :].bitcast(U16).rearrange("p (u t) -> p t u", t=PACK),
        )

        def is_turned(unit):
            return unit[0] == 0

        def places(unit):
            return (P * unit[1], NARROW) if is_turned(unit) else (WIDE * (unit[1] // 2), WIDE)

        def product(unit, sums, passes, start, stop, bins=slice(0, PASS)):
            if is_turned(unit):
                groups = [(bins, bins)]
            else:
                t0 = 2 * (unit[1] % 2)
                groups = [(slice(P * (t0 + t), P * (t0 + t + 1)), slice(WIDE * t, WIDE * (t + 1))) for t in range(2)]
            for cols, written in groups:
                for order, (w_codes, w_scales, per_col, w_dtype, codes, scales) in enumerate(passes):
                    weight = (w_codes[:, per_col * cols.start : per_col * cols.stop].bitcast(w_dtype), w_scales[:, cols])
                    picked = (codes.bitcast(FP8X4), scales)
                    still, moving = (picked, weight) if is_turned(unit) else (weight, picked)
                    nc.tensor.matmul_mx(
                        out=sums[:, written],
                        lhsT=still[0],
                        lhsT_scale=still[1],
                        rhs=moving[0],
                        rhs_scale=moving[1],
                        start=start and order == 0,
                        stop=stop and order == len(passes) - 1,
                    )

        def square(unit, dst, sums):
            if is_turned(unit):
                dst, sums = dst.rearrange("p (t u e) -> p t u e", t=PACK, e=2), sums.rearrange("p (u t e) -> p t u e", t=PACK, e=2)
            else:
                dst, sums = dst.rearrange("p (j t) -> p j t", t=2), sums.rearrange("p (t j) -> p j t", t=2)
            nc.scalar.activation(out=dst, in_=sums, func=ACT.Square)

        def turn(unit, squares, start):
            for t in range(PACK):
                cols = slice(P * t, P * (t + 1))
                nc.tensor.matmul(
                    turned_sum[unit][:, cols],
                    lhsT=squares[:, cols],
                    rhs=identity[:],
                    start=start and t == 0,
                    stop=not start and t == PACK - 1,
                    is_transpose=True,
                )

        def turn_b(unit):
            turned_sum[unit] = bank(SUM_BANK[unit[1]], [P, PASS])
            turn(unit, b_square[unit], start=True)

        b_square, turned_sum = {}, {}
        pair_sums = [buffer("pair_sums%d" % pair, [P, 2, PASS], F32) for pair in range(S // WIDE)]
        b_order = [(half, jt0 + jt) for jt0 in (0, J_HALF // P) for half in range(2) for jt in range(J_HALF // P)]
        for serial, unit in enumerate(b_order):
            sums = bank(serial % BANKS, [P, PASS])
            j0, width = places(unit)
            ws_pass = (
                ws_words_raw[:, 0 : PASS // 2].bitcast(U8) if is_turned(unit) else ws_codes[:],
                ws_scales_raw[:, 0 : PASS // 4].bitcast(U8) if is_turned(unit) else ws_scale[:],
                2,
                FP4X4,
                v_words[j0 // J_HALF][:, j0 % J_HALF : j0 % J_HALF + width],
                v_scales[:, j0 : j0 + width],
            )
            product(unit, sums, [ws_pass], start=True, stop=True)
            if is_turned(unit):
                b_square[unit] = buffer("b_square%d" % unit[1], [P, PASS], F32)[:]
            else:
                b_square[unit] = pair_sums[unit[1] // 2][:, unit[1] % 2, :]
            square(unit, b_square[unit], sums[:])
        for unit in UNITS[:EARLY_TURNED]:
            turn_b(unit)

        picked_planes, xg_rounded = {}, {}
        xg_codes, xg_scales, wc_codes, wc_scales = {}, {}, {}, {}
        wm_codes = held.tile([P, 2, N], U32, name="wm_codes", align_bytes=64)
        wm_scales = held.tile([P, 2, N], U8, name="wm_scales", align_bytes=64)
        for g in range(2):
            for pair in range(S // WIDE):
                if g == 1 or pair % 2 == 0:
                    width = WIDE if g == 1 else J_HALF
                    codes = held.tile([P, width], U32, name="xg_codes%d_%d" % (g, pair), align_bytes=64)
                    scales = held.tile([P, width], U8, name="xg_scales%d_%d" % (g, pair), align_bytes=64)
                    for j in range(0, width, P):
                        xg_codes[g, WIDE * pair + j], xg_scales[g, WIDE * pair + j] = codes[:, j:width], scales[:, j:width]

        def rounded(tag, width):
            return buffer(tag, [P, width * PACK], BF16)

        def gather(plane, j0, width):
            g, i = divmod(plane, PACK)
            dst = picked_planes[g][:, i, j0 : j0 + width]
            picks = x_plane[plane][:].indirect(entries(frame_lists, j0, width))
            nc.vector.tensor_tensor(dst, picks, weights[:, j0 : j0 + width], ALU.mult)

        def interleave(engine, dst, src):
            round_copy(
                engine,
                dst.rearrange("p (run d i) -> p run i d", d=RUN, i=PACK),
                src.rearrange("p i (run d) -> p run i d", d=RUN),
            )

        def round_xg(g, j0, width, engine, dst):
            xg_rounded[g, j0] = dst
            interleave(engine, dst, picked_planes[g][:, :, j0 : j0 + width])

        def quantize_xg(g, j0, width):
            codes, scales = xg_codes[g, j0][:, 0:width], xg_scales[g, j0][:, 0:width]
            nc.vector.quantize_mx(out=codes.bitcast(FP8X4), scales=scales, in_=xg_rounded[g, j0])

        def round_wc(g, t0, dst):
            src = wc_raw[g, PASS][:].rearrange("p i (u t e) -> p u t i e", t=PACK, e=2)
            nc.vector.tensor_copy(out=dst.rearrange("p (t u e i) -> p u t i e", t=2, e=2, i=PACK), in_=src[:, :, t0 : t0 + 2])

        def wc_tiles(g, half, codes):
            wc_codes[g, half] = codes[:]
            wc_scales[g, half] = held.tile([P, PASS], U8, name="wc_scales%d%d" % (g, half), align_bytes=64)[:]

        def quantize_wc(g, half, src, col0=0, cols=PASS):
            nc.vector.quantize_mx(
                out=wc_codes[g, half][:, col0 : col0 + cols].bitcast(FP8X4),
                scales=wc_scales[g, half][:, col0 : col0 + cols],
                in_=src,
            )

        def prepare_wm(half, tag):
            wm_rounded = buffer(tag, [P, N * PACK], BF16)
            interleave("vector", wm_rounded[:], wm_raw[:, half, :, :])
            nc.vector.quantize_mx(out=wm_codes[:, half, :].bitcast(FP8X4), scales=wm_scales[:, half, :], in_=wm_rounded[:])

        a_sums, a_square = {}, {}

        def multiply_a(index, passes, start, stop, bins=slice(0, PASS)):
            unit = UNITS[index]
            j0, width = places(unit)
            if start:
                a_sums[unit] = bank(A_BANK[index], [P, PASS])
            operands = [
                (wc_codes[g, unit[0]], wc_scales[g, unit[0]], 1, FP8X4, xg_codes[g, j0][:, 0:width], xg_scales[g, j0][:, 0:width])
                for g in passes
            ]
            product(unit, a_sums[unit], operands, start, stop, bins)

        last_plane = (PACK - 1) * S
        picked_planes[0] = buffer("picked0", [P, PACK, S], F32)
        picked_row = buffer("picked1", [P, last_plane + BACK + PASS], F32)
        picked_planes[1] = picked_row[:, 0 : PACK * S].rearrange("p (i j) -> p i j", i=PACK)
        late_raw = picked_row[:, last_plane + WIDE : last_plane + WIDE + PACK * LATE].rearrange("p (i r) -> p i r", i=PACK)
        nc.sync.dma_start(out=late_raw, in_=wc[PASS:, EARLY:PASS].rearrange("(p i) r -> p i r", i=PACK))
        gather(0, 0, S)
        load_wc(0, PASS, PASS, "plane0")
        gather(1, 0, S)
        load_wc(1, PASS, PASS, "plane1")
        gather(2, 0, S)
        wm_raw = buffer("plane2", [P, 2, PACK, N], F32)
        wm_rows = wm.rearrange("(half u t e) n -> half e u t n", half=2, t=PACK, e=2)
        for half in range(2):
            for e in range(2):
                nc.sync.dma_start(out=wm_raw[e:P:2, half, :, :], in_=wm_rows[half, e])
        with nc.allow_non_contiguous_dma(reason="band 128 c + p's bias goes to partition p, column c"):
            nc.sync.dma_start(out=bias[:], in_=bm.rearrange("(c p) -> p c", p=P))
        for part in range(2):
            gather(3, J_HALF * part, J_HALF)
            round_xg(0, J_HALF * part, J_HALF, "scalar", rounded("round_x%d" % part, J_HALF)[:])
        gather(4, 0, S)
        gather(5, 0, S)
        quantize_xg(0, 0, J_HALF)
        pass0_rounded = rounded("round_w0", PASS)
        interleave("scalar", pass0_rounded[:], wc_raw[0, 0][:])
        quantize_xg(0, J_HALF, J_HALF)
        gather(6, 0, S)
        wc_tiles(0, 0, buffer("plane6", [P, PASS], U32))
        quantize_wc(0, 0, pass0_rounded[:])
        for index in range(A_BANKS):
            multiply_a(index, [0], start=True, stop=False)
        pass1_rounded = rounded("round_w1", PASS)
        early_bins, late_bins = pass1_rounded[:, 0 : PACK * EARLY], pass1_rounded[:, PACK * EARLY :]
        interleave("scalar", early_bins[:, 0 : PACK * WIDE], wc_raw[1, 0][:])
        interleave("scalar", early_bins[:, PACK * WIDE :], wc_raw[1, WIDE][:])
        for half in range(2):
            wc_tiles(1, half, held.tile([P, PASS], U32, name="wc_codes1%d" % half, align_bytes=64))
        quantize_wc(1, 0, early_bins, 0, EARLY)

        tile_tags = ["round_piece0", "round_piece128", "round_piece256", "round_x0"]

        def round_tile(jt):
            round_xg(1, P * jt, NARROW, "scalar", rounded(tile_tags[jt], NARROW)[:])

        gather(7, 0, NARROW)
        gather(7, NARROW, NARROW)
        round_tile(0)
        round_tile(1)
        interleave("vector", late_bins, late_raw)
        quantize_xg(1, 0, NARROW)
        gather(7, WIDE, NARROW)
        multiply_a(0, [1], start=False, stop=False, bins=slice(0, WIDE))
        multiply_a(0, [1], start=False, stop=False, bins=slice(WIDE, EARLY))
        quantize_wc(1, 0, late_bins, EARLY, LATE)
        gather(7, 3 * P, NARROW)
        quantize_xg(1, P, NARROW)
        round_tile(2)
        round_tile(3)
        quantize_xg(1, 2 * P, NARROW)
        gather(7, J_HALF, WIDE)
        quantize_xg(1, 3 * P, NARROW)
        late = rounded("round_w0", J_HALF)
        round_xg(1, J_HALF, WIDE, "vector", late[:, 0 : PACK * WIDE])
        quantize_xg(1, J_HALF, WIDE)
        wc_tiles(0, 1, held.tile([P, PASS], U32, name="wc_codes01", align_bytes=64))
        for t0 in (0, 2):
            if t0 == 0:
                parts = [rounded("table", WIDE)[:], rounded("round_x1", WIDE)[:]]
            else:
                parts = [rounded("round_x1", WIDE)[:], picked_row[:, last_plane + BACK :].bitcast(BF16)]
            for g in range(2):
                round_wc(g, t0, parts[g])
            for g in range(2):
                quantize_wc(g, 1, parts[g], P * t0, 2 * P)

        h_rounded = [buffer(tag, [P, S * PACK], BF16) for tag in ("plane3", "plane4")]
        h_codes, h_scales = {}, {}
        results = buffer("plane5", [P, N // P * S], F32)
        mel_sums = {}
        own_tag = {(1, 0): "b_square0", (1, 1): "b_square1", (1, 2): "b_square2", (1, 3): "b_square3", (1, 4): "wc_c"}
        own_tag.update({(1, 6): "wc_b", (1, 7): "wc_a"})
        code_tag = {(0, 0): "b_square1", (0, J_HALF): "b_square3", (1, 0): "wc_c"}
        result_tag = {0: "wc_b", WIDE: "wc_a"}

        def square_a(unit):
            if unit in own_tag:
                a_square[unit] = buffer(own_tag[unit], [P, PASS], F32)
            else:
                a_square[unit] = shared.tile([P, PASS], F32, name="a_square", tag="a_square", bufs=SQUARE_BUFFERS)
            square(unit, a_square[unit][:], a_sums[unit][:])

        def add_squares(unit):
            if is_turned(unit):
                turn(unit, a_square[unit], start=False)
            else:
                nc.vector.tensor_tensor(b_square[unit], a_square[unit][:], b_square[unit], ALU.add)

        def root(half, j0, width):
            dst = h_rounded[half][:, PACK * j0 : PACK * (j0 + width)]
            if half == 0:
                nc.scalar.activation(
                    out=dst.rearrange("p (j t) -> p j t", t=PACK),
                    in_=turned_sum[0, j0 // P][:].rearrange("p (t j) -> p j t", t=PACK),
                    func=ACT.Sqrt,
                )
            else:
                sums = pair_sums[j0 // WIDE][:].rearrange("p h (j t) -> p j h t", t=2)
                nc.scalar.activation(
                    out=dst.rearrange("p (j h t) -> p j h t", h=2, t=2),
                    in_=sums[:, j0 % WIDE : j0 % WIDE + width],
                    func=ACT.Sqrt,
                )

        def quantize_h(half, j0, width):
            if (half, j0) in code_tag:
                codes = buffer(code_tag[half, j0], [P, width], U32)
            else:
                codes = held.tile([P, width], U32, name="h_codes%d_%d" % (half, j0), align_bytes=64)
            scales = held.tile([P, width], U8, name="h_scales%d_%d" % (half, j0), align_bytes=64)
            nc.vector.quantize_mx(
                out=codes[:].bitcast(FP8X4),
                scales=scales[:],
                in_=h_rounded[half][:, PACK * j0 : PACK * (j0 + width)],
            )
            for j in range(0, width, P):
                h_codes[half, j0 + j], h_scales[half, j0 + j] = codes[:, j:width], scales[:, j:width]

        def multiply_mel(j0, width, banks, half, opens):
            per_bank = N // P // len(banks)
            if opens:
                mel_sums[j0] = [bank(number, [P, per_bank, width]) for number in banks]
            for c in range(N // P):
                nc.tensor.matmul_mx(
                    out=mel_sums[j0][c // per_bank][:, c % per_bank, :],
                    lhsT=wm_codes[:, half, P * c : P * (c + 1)].bitcast(FP8X4),
                    lhsT_scale=wm_scales[:, half, P * c : P * (c + 1)],
                    rhs=h_codes[half, j0][:, 0:width].bitcast(FP8X4),
                    rhs_scale=h_scales[half, j0][:, 0:width],
                    start=opens and c % per_bank == 0,
                    stop=not opens and c % per_bank == per_bank - 1,
                )

        def add_bias(engine, result, sums, c0, count):
            if engine == "scalar":
                for c in range(count):
                    column = bias[:, c0 + c : c0 + c + 1]
                    nc.scalar.activation(out=result[:, c, :], in_=sums[:, c, :], func=ACT.Identity, bias=column)
            elif count == 1:
                nc.vector.tensor_scalar(result[:, 0, :], sums[:, 0, :], bias[:, c0 : c0 + 1], None, ALU.add)
            else:
                nc.vector.tensor_tensor(result, sums[:], bias[:].unsqueeze(2).to_broadcast(list(result.shape)), ALU.add)

        def store(j0, width, engines):
            if j0 in result_tag:
                result = buffer(result_tag[j0], [P, N // P, width], F32)[:]
            else:
                result = results[:, N // P * j0 : N // P * (j0 + width)].rearrange("p (c j) -> p c j", j=width)
            rows = out.rearrange("(c p) j -> p c j", p=P)[:, :, j0 : j0 + width]
            count = N // P // len(engines)
            for part, engine in enumerate(engines):
                add_bias(engine, result[:, count * part : count * (part + 1), :], mel_sums[j0][part], count * part, count)
            nc.sync.dma_start(out=rows, in_=result)

        def finish(piece, closing):
            j0, width, banks, engines = OUT_PIECES[piece]
            multiply_mel(j0, width, banks, 1 - closing, opens=True)
            quantize_h(closing, j0, width)
            multiply_mel(j0, width, banks, closing, opens=False)

        step_of = {unit: index for index, unit in enumerate(UNITS)}
        last_pair = S // WIDE - 1
        for step in range(len(UNITS) + ROOT_LAG + 1):
            if step == step_of[1, 1]:
                gather(7, BACK, WIDE)
            if step == step_of[1, 2]:
                round_xg(1, BACK, WIDE, "vector", late[:, PACK * WIDE : PACK * J_HALF])
            if step == step_of[1, 2]:
                quantize_xg(1, BACK, WIDE)
            if step == EARLY_TURNED:
                add_squares(UNITS[step - ADD_LAG])
            if A_BANKS <= step < len(UNITS):
                multiply_a(step, [0, 1], start=True, stop=True)
            elif step == 0:
                multiply_a(step, [1], start=False, stop=True, bins=slice(EARLY, PASS))
            elif step < A_BANKS:
                multiply_a(step, [1], start=False, stop=True)
            if EARLY_TURNED <= step < len(UNITS) and is_turned(UNITS[step]):
                turn_b(UNITS[step])
            if 0 <= step - ADD_LAG < len(UNITS) and step != EARLY_TURNED:
                add_squares(UNITS[step - ADD_LAG])
            if 0 <= step - SQUARE_LAG < len(UNITS):
                square_a(UNITS[step - SQUARE_LAG])
            if 0 <= step - ROOT_LAG < len(UNITS):
                half, serial = UNITS[step - ROOT_LAG]
                if half == 0:
                    root(0, P * serial, NARROW)
                elif serial % 2 == 1 and serial // 2 < last_pair:
                    root(1, WIDE * (serial // 2), WIDE)
                elif serial % 2 == 1:
                    root(1, BACK, NARROW)
                    root(1, BACK + NARROW, NARROW)
            done = UNITS[step - ROOT_LAG] if 0 <= step - ROOT_LAG < len(UNITS) else None
            if step == step_of[1, 0] + ADD_LAG:
                prepare_wm(0, "b_square0")
            if step == step_of[1, 1] + ADD_LAG:
                quantize_h(0, 0, J_HALF)
            if step == step_of[1, 2] + ADD_LAG:
                prepare_wm(1, "b_square2")
            if step == step_of[1, 3] + ADD_LAG:
                quantize_h(0, J_HALF, WIDE)
            if step == step_of[1, 4] + ADD_LAG:
                finish(0, 1)
            if step == step_of[1, 5] + ADD_LAG:
                finish(1, 1)
            if done == (1, 5):
                finish(2, 1)
            for piece, unit in enumerate(((1, 6), (1, 7), (1, 7))):
                if step == step_of[unit] + ADD_LAG:
                    store(OUT_PIECES[piece][0], WIDE, OUT_PIECES[piece][3])
            if done == (0, 6):
                quantize_h(0, BACK, NARROW)
            if done == (1, 7):
                finish(3, 1)
                store(BACK, NARROW, OUT_PIECES[3][3])
                quantize_h(1, BACK + NARROW, NARROW)
            if done == (0, 7):
                finish(4, 0)
                store(BACK + NARROW, NARROW, OUT_PIECES[4][3])
